import numpy as np, ml_dtypes
CORES = [3,11,19,27,35,43,51,59]
N = 8
BF = ml_dtypes.bfloat16
C, L, S0, K, T, R, Q = 4096, 128, 768, 24, 3, 12, 8
M, S = C // L, S0 + L * T
def perms(rng):
    return np.ascontiguousarray(np.argsort(rng.random((N, 8, S0)), axis=-1))
def parts(rng):
    x = np.floor(rng.random((N, 8, 16, C)) * rng.integers(160, 257, (N, 8, 1, C))).astype(np.int64)
    v = np.floor(rng.random((N, 8, 16, S0)) * rng.integers(96, 257, (N, 8, 1, S0))).astype(np.int64)
    w = rng.integers(0, S0, (N, 8, C)); few = rng.integers(0, S0, (N, 8, 16))
    w = np.where(rng.random((N, 8, C)) < 0.25, np.take_along_axis(few, rng.integers(0, 16, (N, 8, C)), 2), w)
    th = rng.integers(48, 208, (N, 8, 1, T)) + rng.integers(-16, 17, (N, 8, 16, T))
    return x, v, perms(rng), perms(rng), w, th
def pack(x, v, e, h, w, th):
    big = lambda a: np.ascontiguousarray(a.reshape(N, 128, -1)).astype(np.float32).astype(BF)
    return {"x0": big(x), "v0": big(v), "e0": e.astype(np.int32), "h0": h.astype(np.int32), "w0": w.astype(np.int32), "th": big(th)}
def put(p, s, at):
    j = int(np.argmax(p == at)); p[j] = p[s]; p[s] = at
def setup_inputs(rng):
    return pack(*parts(rng))
def setup_inputs_spread(rng):
    x, v, e, h, w, th = parts(rng)
    x = np.floor(np.exp2(8 * rng.random((N, 8, 1, C))) * rng.random((N, 8, 16, C)) * (rng.random((N, 8, 1, C)) > 0.0625)).astype(np.int64)
    v = np.floor(np.exp2(8 * rng.random((N, 8, 1, S0)) * rng.random((N, 8, 1, S0))) * rng.random((N, 8, 16, S0)) * (rng.random((N, 8, 1, S0)) > 0.0625)).astype(np.int64)
    w = np.minimum(np.floor(S0 * rng.random((N, 8, C)) ** 3).astype(np.int64), S0 - 1)
    th = np.floor(np.exp2(8 * rng.random((N, 8, 1, T))) * rng.random((N, 8, 16, T))).astype(np.int64)
    return pack(x, v, e, h, w, th)
def setup_inputs_ends(rng):
    bx = rng.choice(np.array([0.0, 0.1, 0.5, 0.9, 1.0, 1.0]), (N, 8, 1, C)); bv = rng.choice(np.array([0.0, 0.1, 0.5, 0.9, 1.0]), (N, 8, 1, S0))
    bx[:, 7] = rng.choice(np.array([0.0, 0.0, 0.1, 0.1, 1.0]), (N, 1, C)); bx[:, 7, :, ::64] = 0.0
    x = 255 * (rng.random((N, 8, 16, C)) < bx).astype(np.int64); v = 255 * (rng.random((N, 8, 16, S0)) < bv).astype(np.int64)
    w = np.where(rng.random((N, 8, C)) < 0.75, (S0 - 1) * rng.integers(0, 2, (N, 8, C)), rng.integers(0, S0, (N, 8, C)))
    e, h = perms(rng), perms(rng)
    th = 255 * (rng.random((N, 8, 16, T)) < rng.choice(np.array([0.0, 0.25, 0.5, 0.75, 1.0]), (N, 8, 1, T))).astype(np.int64); th[:, 0, :, 0] = 0; th[:, 5, :, T - 1] = 255
    v[..., 0] = 255 * rng.integers(0, 2, (N, 8, 1)); v[..., S0 - 1] = 255 * rng.integers(0, 2, (N, 8, 1))
    v[:, 7, :, 0] = 255; v[:, 7, :, S0 - 1] = 255; w[:, 7] = np.where(((np.arange(C) >> 9) & 1) == 1, 0, S0 - 1)
    v[:, 0, :, 1] = 0; v[:, 0, 15, 1] = 132; v[:, 0, 1, 1] = 1
    v[:, 7, :, L - 2] = 255; v[:, 7, 15, L - 2] = 132; v[:, 7, 13, L - 2] = 254; v[:, 7, 0, L - 2] = 254
    for r in range(N):
        for g in range(8):
            opp = g == 7 or (g & 1) == 0
            put(e[r, g], 0, 0); put(e[r, g], S0 - 1, S0 - 1)
            put(h[r, g], 0, S0 - 1 if opp else 0); put(h[r, g], S0 - 1, 0 if opp else S0 - 1)
        if r & 1: x[r, 6] = 255; v[r, 6] = 0; th[r, 6] = 0
    return pack(x, v, e, h, w, th)
def setup_inputs_corners(rng):
    x, v, e, h, w, th = parts(rng); shift = int(rng.integers(0, 8))
    for r in range(N):
        for g in range(8):
            m = (r + g + shift) & 7; two = rng.permutation(L)[:2]; s1, s2 = int(two[0]), int(two[1])
            if m == 0:
                x[r, g] = 0; v[r, g][:, two] = 255; v[r, g][8, two] = 254; w[r, g] = np.where(((np.arange(C) >> 9) & 1) == 1, s1, s2)
                put(e[r, g], s1, 0); put(e[r, g], s2, 1); put(h[r, g], s1, S0 - 1); put(h[r, g], s2, S0 - 2)
            elif m == 1:
                x[r, g] = rng.integers(0, 100, (16, C)); v[r, g][:, s1] = rng.integers(100, 256, 16); w[r, g] = s1
                put(e[r, g], s1, 0); put(h[r, g], s1, S0 - 1)
            elif m == 2: x[r, g] = 255; v[r, g] = 0; th[r, g] = 0
            elif m == 3: x[r, g] = 255; v[r, g] = 0; v[r, g][:, s1] = 255; th[r, g] = 1
            elif m == 4: w[r, g] = rng.choice(np.array([0, S0 - 1, s1, s2]), C)
            elif m == 5: h[r, g] = e[r, g]
            elif m == 6: h[r, g] = S0 - 1 - e[r, g]
            else: th[r, g] = 255; x[r, g] = np.minimum(x[r, g], 254)
    return pack(x, v, e, h, w, th)
def setup_inputs_crowd(rng):
    x, v, e, h, w, th = parts(rng); o = int(rng.integers(0, N)); other = (o + 1 + int(rng.integers(0, N - 1))) & (N - 1); B = 16 * N
    c = rng.integers(96, 256, (N, 8, 16, 1)); c[:, :, 0] = 255
    d = np.zeros((N, 8, L), np.int64) + ((o - np.arange(N)) & (N - 1))[:, None, None]
    for g, i in ((1, int(rng.integers(0, L))), (5, L - 1)): d[other, g, i] = (d[other, g, i] + 1) & (N - 1)
    z = np.floor(rng.random((N, 8, 16, S0)) * (c + 1)).astype(np.int64)
    z0 = 16 * d + rng.integers(0, 16, (N, 8, L)) - np.sum(z[:, :, 1:, :L] * (2 * np.arange(1, 16) + 1)[:, None], axis=2)
    z[:, :, 0, :L] = (z0 & (B - 1)) + B * rng.integers(0, 256 // B, (N, 8, L))
    return pack(np.zeros_like(x) + c, c - z, e, h, w, th)
def setup_inputs_ties(rng):
    e, h, w = perms(rng), perms(rng), rng.integers(0, S0, (N, 8, C)); one = rng.random((N, 8, 1, 1)) < 0.5; one[:, 0] = True; one[:, 7] = False
    st = np.where(one, 1, 32); v = np.where(one, rng.integers(1, 255, (N, 8, 16, S0)), 32 * rng.integers(1, 7, (N, 8, 16, S0)))
    n = rng.choice(np.array([R - 1] * 12 + [R, 0, 16, R - 1]), (N, 8, 1, C)); less = np.argsort(rng.random((N, 8, 16, C)), axis=2) < n
    x = np.take_along_axis(v, w[:, :, None, :], 3) + st * np.where(less, -1, np.where(rng.random((N, 8, 16, C)) < 0.25, 1, 0))
    th = np.where(one, rng.integers(32, 200, (N, 8, 16, T)), 32 * rng.integers(1, 7, (N, 8, 16, T)))
    return pack(x, v, e, h, w, th)
def check_inputs(d):
    bad = []
    for k, lo, hi in (("x0", 0, 255), ("v0", 0, 255), ("e0", 0, S0 - 1), ("h0", 0, S0 - 1), ("w0", 0, S0 - 1), ("th", 0, 255)):
        a = np.asarray(d[k]).astype(np.float64)
        if not np.all((a >= lo) & (a <= hi) & (a == np.floor(a))): bad.append("range of " + k)
    for k in ("e0", "h0"):
        if not np.all(np.sort(np.asarray(d[k]), axis=-1) == np.arange(S0)): bad.append("permutation " + k)
    return bad
def mark(z):
    return np.sum(z.astype(np.int64) * (2 * np.arange(16) + 1)[:, None], axis=2) & 4095
def reference(x0, v0, e0, h0, w0, th):
    take = np.take_along_axis
    X = x0.astype(np.float32).astype(np.int32).reshape(N, 8, 16, C); W = w0.astype(np.int64)
    V = np.zeros((N, 8, 16, S), np.int32); V[..., :S0] = v0.astype(np.float32).astype(np.int32).reshape(N, 8, 16, S0)
    E = np.full((N, 8, S), -1, np.int64); E[..., :S0] = e0; H = np.full((N, 8, S), -1, np.int64); H[..., :S0] = h0
    thr = th.astype(np.float32).astype(np.int32).reshape(N, 8, 16, T)
    lane = np.arange(L); k = np.arange(K); kap = k * k + k + 1; lower = lane[None, :] < lane[:, None]
    y = V[..., :L] + 0; cur = np.zeros((N, 8, L), np.int64) + lane; A = np.zeros((N, 8), np.int64)
    for t in range(T):
        u = mark(y)
        a = (((u * u) >> 5)[..., None] + kap * u[..., None] + A[:, :, None, None]) & (C - 1)
        a = a.reshape(N, 8, L * K); s = take(W, a, 2)
        xa = take(X, a[:, :, None, :], 3).reshape(N, 8, 16, L, K); vs = take(V, s[:, :, None, :], 3).reshape(N, 8, 16, L, K)
        es = take(E, s, 2).reshape(N, 8, L, K); hs = take(H, s, 2).reshape(N, 8, L, K)
        par = (es < take(E, cur, 2)[..., None]) != (hs < take(H, cur, 2)[..., None])
        hit = par & (np.sum(vs > xa, axis=2) >= R)
        race = np.any(hit, axis=3); f = np.argmax(hit, axis=3)
        ff = f[:, :, None, :, None]; vf = take(vs, ff, 4)[..., 0]; xf = take(xa, ff, 4)[..., 0]
        yn = np.where(race[:, :, None, :], np.abs(vf - xf), np.abs(np.max(xa, axis=4) - y))
        new = np.where(race, take(s.reshape(N, 8, L, K), f[..., None], 3)[..., 0], cur)
        lead = ~race & ~np.any((cur[..., :, None] == cur[..., None, :]) & ~race[..., None, :] & lower, axis=3)
        will = np.sum(yn >= thr[..., t:t + 1], axis=2) >= Q
        for r in range(N):
            for g in range(8):
                i = np.flatnonzero(lead[r, g] & ~will[r, g]); V[r, g][:, cur[r, g, i]] = yn[r, g][:, i]
                i = np.flatnonzero(lead[r, g] & will[r, g]); c = cur[r, g, i]; n = S0 + L * t + i
                V[r, g][:, n] = yn[r, g][:, i]; new[r, g, i] = n
                fe = np.zeros(S, np.int64); fe[E[r, g, c]] = 1; fh = np.zeros(S, np.int64); fh[H[r, g, c]] = 1
                old = np.flatnonzero(E[r, g] >= 0); pe = E[r, g, old]; ph = H[r, g, old]
                E[r, g, old] = pe + (np.add.accumulate(fe) - fe)[pe]; H[r, g, old] = ph + np.add.accumulate(fh)[ph]
                E[r, g, n] = E[r, g, c] + 1; H[r, g, n] = H[r, g, c] - 1
        q = (np.arange(N)[:, None, None] + ((mark(yn) >> 4) & (N - 1))) & (N - 1)
        ya = np.ascontiguousarray(yn[q, np.arange(8)[None, :, None], :, lane[None, None, :]].transpose(0, 1, 3, 2))
        b = M * lane + (mark(ya) & (M - 1))
        np.put_along_axis(X, b[:, :, None, :], ya, 3); np.put_along_axis(W, b, new, 2)
        A = np.sum(race, axis=2); y, cur = yn, new
    return {"yx": X.reshape(N, 128, C).astype(np.float32).astype(BF), "yv": V.reshape(N, 128, S).astype(np.float32).astype(BF), "yw": W.astype(np.float32), "ye": E.astype(np.float32), "yh": H.astype(np.float32)}

@@ -1,0 +1,658 @@
+from concourse.bass import DstId, RemoteDMATransfer
+from concourse.mybir import AluOpType as OP, ActivationFunctionType as AF
+
+C, L, S0, NT = 4096, 128, 768, 3
+DUM, YC = 1168, 1296
+VW = YC + L
+PW = 1024
+BF, F32, I32, U16 = "bfloat16", "float32", "int32", "uint16"
+
+
+def _sb(n, d):
+    return ("sbuf", [128, n], d)
+
+
+SCRATCH = {
+    "XB": _sb(C, BF), "VB": _sb(VW, BF), "ST": _sb(VW, BF), "IA": _sb(C, BF), "GX": _sb(3200, BF), "GI": _sb(3072, BF),
+    "BT": _sb(3072, BF), "MS": _sb(3072, BF), "MT": _sb(128, BF), "TH": _sb(16, BF), "THF": _sb(4, F32),
+    "LD0": _sb(1024, BF), "LD1": _sb(1024, BF), "LD2": _sb(1024, BF), "AE": _sb(13 * PW, BF), "AH": _sb(13 * PW, BF),
+    "WL": _sb(256, I32), "W1": _sb(256, F32), "W2": _sb(256, F32), "WO": _sb(256, U16), "WN": _sb(256, F32),
+    "EL": _sb(96, I32), "E1": _sb(192, I32), "NP": _sb(288, BF),
+    "IO": _sb(144, F32), "IG": _sb(128, F32), "IM": _sb(128, F32), "I8": _sb(128, F32),
+    "PI": _sb(8, I32), "PJ": _sb(8, I32), "K": _sb(64, F32), "O": _sb(16, F32), "KI": _sb(48, I32), "KO": _sb(48, U16),
+    "BO": _sb(128, BF), "BOF": _sb(128, F32), "ID": _sb(128, BF), "LH0": _sb(128, BF), "LH1": _sb(128, BF),
+    "DM": _sb(128, F32), "CM": _sb(24, F32), "Z0": _sb(144, F32), "ZM": _sb(144, BF), "ZS": _sb(144, BF), "ZE": _sb(144, BF),
+    "ZH": _sb(144, BF), "ZP": _sb(144, BF), "ZQ": _sb(144, BF),
+    "FEH": _sb(16, BF), "FEN": _sb(384, BF), "I24": _sb(384, BF), "FV": _sb(8, BF), "FS": _sb(8, BF), "G8": _sb(8, BF), "RK": _sb(192, BF), "SEG": _sb(1024, BF),
+    "LD": _sb(128, BF), "DG": _sb(128, BF), "DD": _sb(128, BF), "NI": _sb(128, BF), "CT": _sb(384, BF), "SEL": _sb(1024, BF),
+    "TRI": _sb(128, BF), "NC": _sb(128, BF), "EA": _sb(1024, BF), "EQ": _sb(1024, BF), "ON": _sb(128, BF),
+    "FL": _sb(14 * 128, BF), "B0": _sb(256, BF), "B7": _sb(128, BF), "LO": _sb(256, BF), "HI": _sb(128, BF), "HN": _sb(128, BF), "SCM": _sb(784, BF),
+    "U": _sb(64, I32), "U1": _sb(64, I32), "UU": _sb(64, I32), "UB": _sb(64, I32), "UA": _sb(192, I32), "UC": _sb(192, I32),
+    "AO": _sb(192, U16), "SL": _sb(192, U16), "AC": _sb(4, F32), "SG": _sb(384, BF), "NPB": _sb(192, BF), "VL": _sb(192, F32),
+    "KY": _sb(192, F32), "DFL": _sb(192, F32), "SC": _sb(192, F32), "D1": _sb(128, F32), "D2": _sb(128, F32),
+    "SR": _sb(128, BF), "NR": _sb(8, BF), "PL": _sb(16, F32), "DL": _sb(16, F32), "SI": _sb(64, I32), "SO": _sb(64, U16), "LN": _sb(16, I32), "S2": _sb(32, I32),
+    "G1": _sb(128, BF), "G2": _sb(128, BF), "WB": _sb(128, BF), "SP": _sb(384, BF), "STP": _sb(128, BF), "BS": _sb(128, BF),
+    "M1": _sb(128, BF), "DF": _sb(128, BF), "ZZ": _sb(128, BF),
+    "PO": _sb(144, U16), "TT": _sb(784, F32), "MM": _sb(768, F32), "TM": _sb(768, "float16"), "BOH": _sb(128, "float16"), "OE": _sb(1152, F32), "OH": _sb(1152, F32),
+}
+PSUM = ["P0", "P1", "PE", "PV", "P4", "P5", "P6", "P7"]
+for _n in PSUM:
+    SCRATCH[_n] = ("psum", [128, 512], F32)
+NDMA = 32
+SEMAPHORES = ["sv", "sa", "sp", "sg", "sent", "arr0", "arr1", "arr2"] + ["d%d" % i for i in range(NDMA)]
+
+
+def rank_program(g, core, T, topo):
+    rank = T.rank_of(core)
+    if rank is None:
+        return
+    N = len(T.cores)
+    Q = {"v": g.vector, "a": g.scalar, "p": g.tensor, "g": g, "s": g.sync}
+    SEM = {"v": "sv", "a": "sa", "p": "sp", "g": "sg"}
+    cnt = {"sv": 0, "sa": 0, "sp": 0, "sg": 0, "sent": 0}
+    waited = {q: {} for q in Q}
+    hist = {}
+    nd = [0]
+
+    def A(name, lo=0, hi=None, step=1, p=None):
+        t = T[name]
+        if hi is None:
+            hi = t.shape[1]
+        ps = slice(0, 128) if p is None else slice(*p)
+        return (t[ps, lo:hi:step] if step != 1 else t[ps, lo:hi], [(name, lo, hi)])
+
+    def IND(win, off):
+        return (win[0].indirect(off[0]), win[1], off[1])
+
+    def wait(q, sem, val):
+        if waited[q].get(sem, 0) < val:
+            Q[q].wait_ge(T.sem[sem], val)
+            waited[q][sem] = val
+
+    def order(q, reads, writes, dma=False):
+        need = {}
+        for rs, wr in ((reads, False), (writes, True)):
+            for (nm, lo, hi) in rs:
+                bank = nm in PSUM
+                for (q2, sem, val, l2, h2, w2) in hist.get(nm, ()):
+                    same = q2 == q and not dma
+                    if bank and not same:
+                        hit = True
+                    elif same and q == "p":
+                        hit = False
+                    else:
+                        hit = (wr or w2) and l2 < hi and lo < h2
+                    if hit and need.get(sem, 0) < val:
+                        need[sem] = val
+        for sem in need:
+            wait(q, sem, need[sem])
+
+    def note(q, sem, val, reads, writes):
+        for rs, wr in ((reads, False), (writes, True)):
+            for (nm, lo, hi) in rs:
+                h = hist.setdefault(nm, [])
+                if wr:
+                    h[:] = [e for e in h if not (lo <= e[3] and e[4] <= hi and nm not in PSUM)]
+                h.append((q, sem, val, lo, hi, wr))
+
+    def run(q, fn, out, ins):
+        reads, writes = [], list(out[1])
+        if len(out) == 3:
+            reads += out[2]
+        for x in ins:
+            if isinstance(x, tuple):
+                reads += x[1]
+                if len(x) == 3:
+                    reads += x[2]
+        order(q, reads, writes)
+        sem = SEM[q]
+        fn().then_inc(T.sem[sem], 1)
+        cnt[sem] += 1
+        note(q, sem, cnt[sem], reads, writes)
+
+    def val(x):
+        return x[0] if isinstance(x, tuple) else x
+
+    def cp(o, i):
+        run("v", lambda: g.vector.tensor_copy(o[0], i[0]), o, [i])
+
+    def tt(o, a, b, op):
+        run("v", lambda: g.vector.tensor_tensor(o[0], a[0], b[0], op), o, [a, b])
+
+    def ts(o, a, s1, op0, s2=None, op1=None):
+        if op1 is None:
+            run("v", lambda: g.vector.tensor_scalar(o[0], a[0], val(s1), None, op0), o, [a, s1])
+        else:
+            run("v", lambda: g.vector.tensor_scalar(o[0], a[0], val(s1), val(s2), op0, op1), o, [a, s1, s2])
+
+    def ms(o, c):
+        run("v", lambda: g.vector.memset(o[0], c), o, [])
+
+    def scan(o, a, b, op0, op1, ini=0.0):
+        run("v", lambda: g.vector.tensor_tensor_scan(o[0], a[0], b[0], val(ini), op0, op1), o, [a, b, ini])
+
+    def act(o, i, f=AF.Identity, bias=None, scale=None):
+        kw = {}
+        if bias is not None:
+            kw["bias"] = val(bias)
+        if scale is not None:
+            kw["scale"] = val(scale)
+        run("a", lambda: g.scalar.activation(o[0], i[0], f, **kw), o, [i, bias, scale])
+
+    def mm(o, pairs, start=True, stop=True):
+        for n, (l, r) in enumerate(pairs):
+            run("p", lambda: g.tensor.matmul(o[0], l[0], r[0], start and n == 0, stop and n == len(pairs) - 1), o, [l, r])
+
+    def iota(o, pat, base=0, cm=0, fl=True):
+        if fl:
+            run("g", lambda: g.iota(o[0], pat, base, cm, allow_small_or_imprecise_dtypes=True), o, [])
+        else:
+            run("g", lambda: g.iota(o[0], pat, base, cm), o, [])
+
+    def asel(o, i, pat, op, base, cm, fill=0.0):
+        run("g", lambda: g.affine_select(o[0], i[0], pat, op, fill, base, cm), o, [i])
+
+    def dma(q, o, i, keep=False):
+        order(q, i[1], [] if keep else o[1], True)
+        sem = "d%d" % nd[0]
+        nd[0] += 1
+        Q[q].dma_start(o[0], i[0]).then_inc(T.sem[sem], 16)
+        cnt[sem] = 16
+        note("dma", sem, 16, i[1], [])
+        for (nm, lo, hi) in o[1]:
+            hist.setdefault(nm, []).append(("dma", sem, 16, lo, hi, True))
+
+    def H(ap):
+        return (ap, [])
+
+    def wrap(o, Z, name, lo, n):
+        mm(o, [(A(Z, 15 - p, 143 - p), A(name, lo + p, lo + 16 * n, 16)) for p in range(16)])
+
+    def K(j):
+        return A("K", j, j + 1)
+
+    def O(r):
+        return A("O", r, r + 1)
+
+    def zero(nm, d):
+        iota(A(nm, d * PW - 16, d * PW + 784), [[0, 800]])
+
+    dma("a", A("EL", 0, 48), H(T.e0[:, :]))
+    dma("s", A("EL", 48, 96), H(T.h0[:, :]))
+    for h in range(2):
+        dma("as"[h], A("WL", 128 * h, 128 * h + 128), H(T.w0[h::2, :]))
+    dma("a", A("VB", 0, S0), H(T.v0[:, :]))
+    for j in range(2):
+        dma("sa"[j], A("XB", 2048 * j, 2048 * j + 2048), H(T.x0[:, 2048 * j:2048 * j + 2048]))
+    dma("s", A("TH", 0, 3), H(T.th[:, :]))
+
+    iota(A("PI", 0, 1), [[0, 1]], 0, 1, False)
+    iota(A("IO"), [[1, 144]])
+    iota(A("KI", 0, 16), [[16, 8], [128, 2]], 0, 0, False)
+    iota(A("KI", 16, 32), [[2, 16]], 0, 0, False)
+    iota(A("KI", 32, 40), [[24, 8]], 23, 0, False)
+    iota(A("KI", 40, 48), [[1, 8]], 0, 0, False)
+    iota(A("I8"), [[1, 16], [0, 8]])
+    iota(A("IG"), [[1, 8], [0, 16]])
+    iota(A("IM"), [[0, 8], [1, 16]])
+    ms(A("ST", 0, S0), 0.0)
+    ms(A("ON"), 1.0)
+    ms(A("AC"), 0.0)
+    p_ = A("PI", 0, 1)
+    ts(A("PJ", 0, 1), p_, 15, OP.bitwise_and)
+    ts(A("PJ", 1, 2), p_, 4, OP.logical_shift_right)
+    ts(A("PJ", 2, 3), p_, 3, OP.bitwise_and)
+    ts(A("PJ", 3, 4), p_, 2, OP.logical_shift_right, 3, OP.bitwise_and)
+    ts(A("PJ", 4, 5), p_, 7, OP.bitwise_and)
+    ts(A("PJ", 5, 6), p_, 3, OP.logical_shift_right, 1, OP.bitwise_and)
+    ts(A("PJ", 6, 7), p_, 127, OP.bitwise_and)
+    cp(A("K", 0, 7), A("PJ", 0, 7))
+    kR, kG, kS, kQ, k7, kH, kP = [K(j) for j in range(7)]
+    ts(K(30), kR, 2.0, OP.is_equal, 8.0, OP.mult)
+    ts(K(7), k7, 32.0, OP.mult, kH, OP.add)
+    ts(A("O"), A("IO", 0, 16), kR, OP.is_equal)
+    ts(A("ST", 0, S0), A("ST", 0, S0), K(30), OP.add)
+    act(K(8), kR, scale=2.0, bias=1.0)
+    act(K(9), kG, scale=2.0)
+    act(K(10), kG, scale=2.0, bias=1.0)
+    act(K(17), kR, scale=1.5)
+    act(A("K", 11, 14), A("IO", 0, 24, 8), bias=k7)
+    act(A("NP", 240, 288), A("IO", 0, 48))
+    act(A("NP", 192, 240), A("IO", 0, 48), scale=0.0, bias=K(17))
+    act(A("K", 14, 17), A("K", 11, 14), AF.Square, bias=0.5)
+    act(A("K", 14, 17), A("K", 14, 17), bias=0.75)
+    act(K(35), kG, scale=16.0, bias=15.0)
+    ts(A("KI", 0, 16), A("KI", 0, 16), kR, OP.add)
+    ts(A("KI", 16, 32), A("KI", 16, 32), K(7), OP.add)
+    ts(A("LH0"), A("I8"), K(9), OP.is_equal, K(8), OP.mult)
+    cp(A("KO"), A("KI"))
+    ts(A("LH1"), A("I8"), K(10), OP.is_equal, K(8), OP.mult)
+    ts(A("E1", 0, 96), A("EL"), 5, OP.logical_shift_right)
+    ts(A("E1", 96, 192), A("EL"), 31, OP.bitwise_and)
+    cp(A("NP", 0, 192), A("E1"))
+    cp(A("W1"), IND(A("WL"), A("KO", 0, 16)))
+    for q in "as":
+        order(q, [], [("ST", 0, S0)], True)
+    for j, row, q in ((4, 8, "s"), (5, 9, "s"), (0, 0, "a"), (1, 4, "s"), (2, 1, "a"), (3, 5, "s")):
+        dma(q, A("ST", 0, S0, p=(row, 128, 16)), A("NP", 48 * j, 48 * j + 48), True)
+    run("v", lambda: g.vector.transpose(T.W2[:, :], T.W1[:, :]), A("W2"), [A("W1")])
+    ts(A("K", 18, 22), A("IO", 0, 4), kS, OP.is_equal)
+    ts(A("K", 22, 26), A("IO", 0, 4), kQ, OP.is_equal)
+    cp(A("WO"), IND(A("W2"), A("KO", 16, 32)))
+
+    def offsets(t):
+        yb = "LD%d" % (t - 1) if t else "VB"
+        mm(A("P4", 0, 64), [(A("LH0"), A(yb, 0, L, 2)), (A("LH1"), A(yb, 1, L, 2))])
+        steps = [lambda: cp(A("U1"), A("P4", 0, 64)),
+                 lambda: ts(A("U"), A("U1"), 4095, OP.bitwise_and),
+                 lambda: tt(A("UU"), A("U"), A("U"), OP.mult)]
+        for m in range(3):
+            steps.append(lambda m=m: ts(A("UA", 64 * m, 64 * m + 64), A("U"), K(14 + m), OP.mult, A("AC", 0, 1), OP.add))
+        steps.append(lambda: ts(A("UB"), A("UU"), 5, OP.logical_shift_right))
+        for m in range(3):
+            steps.append(lambda m=m: tt(A("UC", 64 * m, 64 * m + 64), A("UA", 64 * m, 64 * m + 64), A("UB"), OP.add))
+        steps.append(lambda: ts(A("UA"), A("UC"), 4095, OP.bitwise_and))
+        steps.append(lambda: cp(A("AO"), A("UA")))
+        return steps
+
+    steps = offsets(0)
+    ts(K(26), K(18), 32.0, OP.mult, K(19), OP.add)
+    steps[0]()
+    ts(A("Z0"), A("IO"), K(35), OP.is_equal)
+    steps[1]()
+    ts(A("CM", 0, 8), A("IO", 0, 8), kG, OP.is_equal)
+    for s in steps[2:]:
+        s()
+    act(K(27), K(21), bias=K(26))
+    act(K(28), K(20), scale=float(PW), bias=K(26))
+    act(K(29), K(20), scale=-0.125, bias=K(26))
+    act(A("K", 36, 40), A("K", 22, 26), scale=K(27))
+    act(A("K", 40, 44), A("K", 22, 26), scale=K(28))
+    act(A("K", 44, 48), A("K", 22, 26), scale=K(29))
+    act(K(48), K(38), scale=1.0 / 2048)
+    act(K(31), kP, scale=8.0)
+    act(A("ZS"), A("Z0"), scale=K(38))
+    act(A("FEH", 0, 8), A("CM", 0, 8), scale=K(44))
+    act(A("FEH", 8, 16), A("CM", 0, 8), scale=K(45))
+    act(K(52), kQ, scale=8.0, bias=kG)
+    act(K(54), K(29), scale=-1.0)
+    act(A("FV"), A("CM", 0, 8), scale=K(48))
+    act(A("G8"), A("CM", 0, 8), scale=-8192.0)
+    asel(A("ID"), A("ON"), [[-1, 128]], OP.is_equal, 0, 1)
+    iota(A("I24"), [[1, 16], [0, 24]])
+    iota(A("RK"), [[0, 192]])
+    iota(A("VB", S0, YC), [[0, YC - S0]])
+    iota(A("ST", S0, DUM), [[0, DUM - S0]])
+    iota(A("RK", p=(0, 1)), [[0, 8], [1024, 3], [0, 8]])
+    wait("g", "sg", cnt["sg"])
+    iota(A("RK", p=(32, 33)), [[0, 24], [1, 8]])
+    wait("g", "sg", cnt["sg"])
+    iota(A("SEG"), [[0, 1024]], 1)
+    asel(A("SEG"), A("SEG"), [[0, 128], [1, 8]], OP.is_gt, 0, 0)
+    iota(A("LN", 0, 8), [[16, 8]], 0, 0, False)
+    iota(A("DL", 0, 8), [[0, 8]], DUM, 1)
+    iota(A("DL", 8, 16), [[0, 8]], 2048 * 3072 + YC, 2049)
+    asel(A("TRI"), A("ON"), [[-1, 128]], OP.is_ge, 0, 1)
+    iota(A("SCM"), [[0, 784]], 1)
+    for d in (4, 1):
+        zero("AE", d)
+        zero("AH", d)
+
+    def consts_v():
+        ts(A("DM"), A("IM"), kR, OP.is_equal)
+        ts(A("BOF"), A("IG"), kG, OP.is_equal)
+        ts(A("BOH"), A("IG"), kG, OP.is_equal)
+        ms(A("DFL"), 0.0)
+        ms(A("PL", 8, 16), 0.0)
+        ts(A("LN", 0, 8), A("LN", 0, 8), kR, OP.add)
+        ts(K(50), kQ, 2.0, OP.is_lt, K(21), OP.is_gt)
+        ts(A("DFL", 0, 192, 24), A("DL", 8, 16), 1.0 / 2048, OP.mult)
+        ts(A("LN", 8, 16), A("LN", 0, 8), 32.0, OP.mult)
+
+    def consts_a():
+        act(A("VB", YC, VW), A("VB", 0, L))
+        act(A("THF", 0, 3), A("TH", 0, 3))
+        act(K(49), O(11), scale=-100.0)
+        act(K(51), K(24), scale=-1.0)
+        act(K(53), O(1), bias=O(5))
+        act(K(56), O(2), scale=12.0, bias=O(11))
+        act(K(58), O(2), scale=-1.0, bias=O(6))
+        act(K(59), O(8), scale=24.0, bias=O(3))
+        act(K(56), O(6), scale=8.0, bias=K(56))
+        for t in range(NT):
+            act(K(61 + t), K(58), scale=float(4 >> t), bias=K(59))
+        for t in range(1, NT):
+            act(K(61 + t), O(8), scale=4.0 * t, bias=K(61 + t))
+        act(A("FS"), A("CM", 0, 8), scale=K(38))
+        act(A("CM", 8, 16), A("CM", 0, 8), scale=2048.0)
+        act(A("NI"), A("ID"), scale=-2048.0)
+        act(A("ST", DUM, YC), A("IO", 0, 128), scale=K(53), bias=K(56))
+        act(A("ZM"), A("Z0"), scale=K(8))
+        act(A("CT", 0, 128), A("IO", 0, 128), scale=O(9), bias=K(61))
+        act(A("DD"), A("ID"), scale=K(51))
+
+    def consts_a2():
+        act(A("BO"), A("BOF"))
+        act(A("LD"), A("BOF"), scale=K(49))
+        act(A("DG"), A("ID"), scale=K(50))
+        act(A("ZE"), A("Z0"), scale=K(40))
+        act(A("ZH"), A("Z0"), scale=K(41))
+        act(A("CM", 16, 24), A("CM", 0, 8), scale=K(38))
+        act(A("HI"), A("ID"), scale=4096.0)
+        act(A("B0", 128, 256), A("BO"), scale=O(0))
+        act(K(12), O(7), bias=O(15))
+
+    def consts_a4():
+        for gg in range(8):
+            act(A("SEL", 128 * gg, 128 * gg + 128), A("ON"), scale=A("CM", 16 + gg, 17 + gg))
+
+    def build(j, q):
+        o, i = A("IA", 512 * j, 512 * j + 512), IND(A("ST", 0, S0), A("WO", 32 * j, 32 * j + 32))
+        (act if q == "a" else cp)(o, i)
+
+    for j in range(8):
+        build(j, "aavavava"[j])
+    act(A("ST", YC, VW), A("ST", 0, L))
+    ts(A("FEN"), A("I24"), K(52), OP.is_equal, K(54), OP.mult)
+
+    peers = [T.cores[(rank - d) % N] for d in range(1, N)]
+    SB = ("P6", "P4", "P6")
+
+    def gx(lo, hi, q):
+        (act if q == "a" else cp)(A("GX", 16 * lo, 16 * hi), IND(A("XB"), A("AO", lo, hi)))
+
+    def gi(m, q="a"):
+        (act if q == "a" else cp)(A("GI", 1024 * m, 1024 * m + 1024), IND(A("IA"), A("AO", 64 * m, 64 * m + 64)))
+        if m == 0:
+            mm(A("PE", 0, 384), [(A("ST", YC, VW), A("FEN"))], True, False)
+            mm(A("PV", 0, 192), [(A("ON", p=(0, 33)), A("RK", p=(0, 33)))], True, False)
+            opened = cnt["sp"]
+        wrap(A(SB[m], 0, 64), "ZS", "GI", 1024 * m, 64)
+        if m == 0:
+            wait("p", "sp", opened)
+        for kk in range(8):
+            k = 8 * m + kk
+            l = A("GI", 1024 * m + kk, 1024 * m + 1024, 8)
+            mm(A("PE", k, 384, 24), [(l, A("FEH"))], False, k == 23)
+            mm(A("PV", k, 192, 24), [(l, A("FV"))], False, k == 23)
+
+    def sl(m):
+        cp(A("SL", 64 * m, 64 * m + 64), A(SB[m], 0, 64))
+
+    def gv(m):
+        lo, hi = 1024 * m, 1024 * m + 1024
+        tt(A("BT", lo, hi), IND(A("VB", 0, 1152), A("SL", 64 * m, 64 * m + 64)), A("GX", lo, hi), OP.is_gt)
+
+    def mx(m):
+        scan(A("MS", 1024 * m, 1024 * m + 1024), A("SEG"), A("GX", 1024 * m, 1024 * m + 1024), OP.mult, OP.max)
+
+    def count(m):
+        for kk in range(8):
+            k = 8 * m + kk
+            if k == 0:
+                mm(A("P5", 0, 192), [(A("ID"), A("NPB"))], True, False)
+                wait("p", "sp", cnt["sp"])
+            mm(A("P5", k, 192, 24), [(A("BT", 1024 * m + kk, 1024 * m + 1024, 8), A("G8"))], False, k == 23)
+
+    def parallel():
+        act(A("SG"), A("PE", 0, 384), AF.Sign, bias=0.0625)
+        mm(A("P7", 0, 192), [(A("ID"), A("SG", 0, 192)), (A("ID"), A("SG", 192, 384))])
+        act(A("VL"), A("PV", 0, 192), bias=K(31))
+        act(A("NPB"), A("P7", 0, 192), AF.Abs, scale=28.0 * 4096, bias=23.0 * 4096)
+
+    def fold(ds, start, stop, first=()):
+        prs = list(first) + [(A("FL", 128 * (7 * o + d - 1), 128 * (7 * o + d)), ("AE", "AH")[o], d * PW - 1 + o) for (o, d) in ds]
+        mm(A("P0"), [(l, A(nm, c0, c0 + 512)) for (l, nm, c0) in prs], start, stop)
+        mm(A("P1", 0, 257), [(l, A(nm, c0 + 512, c0 + 769)) for (l, nm, c0) in prs], start, stop)
+
+    def slots(t, bank):
+        cp(A("SO", 48, 64), A(bank, 0, 16))
+        if t == 0:
+            return
+        cp(A("S2", 0, 16), A(bank, 0, 16))
+        ts(A("S2", 16, 32), A("S2", 0, 16), PW - 1, OP.bitwise_and)
+        ts(A("PO", 48 + 8 * t, 56 + 8 * t), A("S2", 16, 24), 1.0, OP.add)
+        cp(A("PO", 120 + 8 * t, 128 + 8 * t), A("S2", 24, 32))
+
+    def flags(t, o):
+        cp(IND(A(("AE", "AH")[o]), A("SO", 48 + 8 * o, 56 + 8 * o)), A("SP", 128 * t, 128 * t + 128))
+
+    def masks(lo, hi, b0, b1):
+        for o in range(2):
+            mm(A((b0, b1)[o], 0, hi - lo), [(A("LO", 128 * o, 128 * o + 128), A("ST", S0 + lo, S0 + hi)), (A("HN"), A("SP", lo, hi))])
+        for o in range(2):
+            ts(A("MM", 384 * o + lo, 384 * o + hi), A((b0, b1)[o], 0, hi - lo), K(17), OP.is_equal, K(10 - o), OP.mult)
+
+    def consts_a3():
+        act(K(9), K(12), scale=2.0, bias=-1.0)
+        act(K(10), kH, scale=-1.0, bias=1.0)
+        act(K(17), K(12), scale=-8.0, bias=k7)
+        act(K(10), K(10), scale=K(9))
+        act(K(9), kH, scale=K(9))
+        act(K(17), K(17), bias=-99.0)
+        act(A("LO", 0, 128), A("B7"), scale=O(2))
+        act(A("LO", 128, 256), A("B7"), scale=O(6))
+        act(A("HN"), A("ID"), scale=-100.0)
+        act(A("SCM"), A("SCM"), scale=K(12))
+
+    def flmat(o, d):
+        asel(A("FL", 128 * (7 * o + d - 1), 128 * (7 * o + d)), A("B0", 128 * o, 128 * o + 128), [[0, 8], [1, 16]], OP.is_ge, 1 - 8 * o - d, 0)
+
+    for t in range(NT):
+        last = t == NT - 1
+        land = "LD%d" % t
+        gi(0)
+        gx(0, 64 if t else 128, "v")
+        sl(0)
+        gi(1)
+        gv(0)
+        if t:
+            gx(64, 128, "a")
+            slots(t - 1, "P7")
+            flags(t - 1, 0)
+            if t == 2:
+                fold([(0, 2), (0, 6)], False, False)
+            flags(t - 1, 1)
+            if t == 2:
+                fold([(1, 2), (1, 6)], False, False)
+        sl(1)
+        if t == 1:
+            wrap(A("P0", 0, 56), "ZP", "ST", 0, 56)
+            wrap(A("P0", 56, 112), "ZQ", "ST", 0, 56)
+        gi(2)
+        gv(1)
+        sl(2)
+        if t == 1:
+            cp(A("PO", 0, 56), A("P0", 0, 56))
+            cp(A("PO", 72, 128), A("P0", 56, 112))
+        gx(128, 192, "a")
+        mx(0)
+        mx(1)
+        tt(A("MT"), A("MS", 7, 1024, 8), A("MS", 1031, 2048, 8), OP.max)
+        if t == 0:
+            consts_v()
+        parallel()
+        gv(2)
+        count(0)
+        count(1)
+        count(2)
+        mx(2)
+        if t == 0:
+            consts_a()
+            consts_a2()
+            consts_a4()
+        if t == 1:
+            consts_a3()
+        tt(A("KY"), A("P5", 0, 192), A("VL"), OP.max)
+        scan(A("SC"), A("DFL"), A("KY"), OP.max, OP.min)
+        tt(A("D1"), IND(A("SC"), A("KO", 32, 40)), A("DM"), OP.mult)
+        ts(A("NR"), A("SC", 23, 192, 24), 3072.0, OP.is_ge)
+        mm(A("P4", 0, 8), [(A("D1"), A("CM", 8, 16))])
+        mm(A("P7", 0, 8), [(A("ST", YC, VW), A("FS")), (A("NI"), A("NR"))], True, t == 0)
+        if t:
+            wait("p", "sp", cnt["sp"])
+            for gg in range(8):
+                mm(A("P7", gg, gg + 1), [(A("EQ", 128 * gg, 128 * gg + 128), A("NR", gg, gg + 1))], False, gg == 7)
+        if t == 1:
+            fold([(0, 4), (1, 4)], True, False, [(A("ID"), "SCM", 0)])
+        tt(A("GX", 3072, 3200), A("MT"), A("MS", 2055, 3072, 8), OP.max)
+        cp(A("SI", 0, 8), A("P4", 0, 8))
+        ts(A("SI", 8, 16), A("SI", 0, 8), 11, OP.logical_shift_right)
+        ts(A("SI", 16, 24), A("SI", 0, 8), 2047, OP.bitwise_and)
+        cp(A("SO", 8, 24), A("SI", 8, 24))
+        cp(A("G1"), IND(A("GX"), A("SO", 8, 16)))
+        tt(A("G2"), IND(A("VB"), A("SO", 16, 24)), A("G1"), OP.subtract)
+        ts(A("PL", 0, 8), A("P7", 0, 8), 2048.0, OP.add)
+        tt(A("PL", 0, 8), A("PL", 0, 8), A("DL", 0, 8), OP.min)
+        tt(A("D2"), IND(A("PL"), A("KO", 40, 48)), A("DM"), OP.mult)
+        if not last:
+            act(A("SR"), IND(A("SC"), A("KO", 32, 40)), AF.Sign, bias=-3071.9)
+        act(A("BS"), IND(A("ST"), A("SO", 16, 24)))
+        act(A(land, 0, L), A("G2"), AF.Abs)
+        y = A(land, 0, L)
+        order("g", y[1], [])
+        trs = []
+        for d in range(1, N):
+            dst = peers[d - 1]
+            rid, pid, _ = topo.addr(dst)
+            trs.append(RemoteDMATransfer(dst_ids=[DstId(rid=rid, pnc=pid)], dma_engine_mask=1 << topo.engines(core, dst)[d - 1],
+                                         remote_sem=T.sem["arr%d" % t], src=y[0], dst=T[land][:, L * d:L * d + L]))
+        g.remote_dma_fused(trs, local_sem=T.sem.sent)
+        cnt["sent"] += N - 1
+        mm(A("P6", 256, 264), [(A("D2"), A("CM", 0, 8))])
+        ts(A("WB"), y, A("THF", t, t + 1), OP.is_ge)
+        cp(A("SO", 24, 32), A("P6", 256, 264))
+        wrap(A("P4", 64, 72), "ZM", land, 0, 8)
+        act(A("STP"), IND(A("ST"), A("SO", 24, 32)))
+        tt(A("DF"), IND(A("VB", 0, YC), A("SO", 24, 32)), y, OP.subtract)
+        ct = A("CT", 128 * t, 128 * t + 128)
+        n0 = S0 + L * t
+        sp = A("SP", 128 * t, 128 * t + 128)
+        mm(A("P5", 0, 128), [(A("BO"), A("WB")), (A("LD"), A("STP"))])
+        mm(A("P6", 0, 128), [(A("DG"), A("STP")), (A("ID"), ct)])
+        mm(A("P7", 0, 128), [(A("DD"), A("STP")), (A("ID"), ct)])
+        act(A("ST", n0, n0 + L), A("P6", 0, 128))
+        cp(A("SI", 24, 32), A("P4", 64, 72))
+        ts(A("SI", 32, 40), A("SI", 24, 32), 112, OP.bitwise_and)
+        ts(sp, A("P5", 0, 128), 7.5, OP.is_ge)
+        ts(A("SI", 24, 32), A("SI", 32, 40), 8.0, OP.mult)
+        if not last:
+            steps = offsets(t + 1)
+            mm(A("P6", 0, 1), [(A("SR"), A("ON", 0, 1))])
+            act(A("AC", 0, 1), A("P6", 0, 1), bias=64.0, scale=-0.5)
+        tt(A("M1"), A("P7", 0, 128), sp, OP.mult)
+        tt(A("SI", 32, 40), A("SI", 24, 32), A("LN", 0, 8), OP.add)
+
+        def spawn_lists():
+            wrap(A("PE" if last else "P7", 0, 8), "ZE", "ST", n0, 8)
+            if last:
+                cp(A("SO", 48, 56), A("PE", 0, 8))
+                wrap(A("PV", 8, 16), "ZH", "ST", n0, 8)
+            else:
+                wrap(A("P7", 8, 16), "ZH", "ST", n0, 8)
+        if last:
+            spawn_lists()
+        mm(A("P5", 0, 128), [(A("ID"), A("BS")), (A("ID"), A("M1"))])
+        act(A("ST", YC, VW), A("P5", 0, 128))
+
+        def vwrite():
+            tt(A("DF"), A("DF"), sp, OP.mult)
+            cp(A("SO", 32, 40), A("SI", 32, 40))
+            tt(IND(A("VB", 0, YC), A("SO", 24, 32)), A("DF"), y, OP.add)
+            tt(A("VB", n0, n0 + L), y, sp, OP.mult)
+
+        def arrive():
+            wait("a", "arr%d" % t, N - 1)
+            act(A("ZZ"), IND(A(land), A("SO", 32, 40)))
+            wrap(A("P4", 72, 80), "ZM", "ZZ", 0, 8)
+
+        def blist():
+            cp(A("SI", 40, 48), A("P4", 72, 80))
+            ts(A("SI", 48, 56), A("SI", 40, 48), 31, OP.bitwise_and)
+            tt(A("SI", 40, 48), A("SI", 48, 56), A("LN", 8, 16), OP.add)
+            cp(A("SO", 40, 48), A("SI", 40, 48))
+
+        if not last:
+            act(A("NC"), A("ST", YC, VW), scale=-1.0)
+            act(A("VB", YC, VW), y)
+            steps[0]()
+            steps[1]()
+            vwrite()
+            for s in steps[2:]:
+                s()
+            for hb in range(2):
+                for gq in range(4):
+                    s = A("SEL", 512 * hb + 128 * gq, 512 * hb + 128 * gq + 128)
+                    mm(A(("PE", "PV")[hb], 128 * gq, 128 * gq + 128), [(s, A("NC")), (A("ST", YC, VW), s), (A("HI"), A("TRI"))])
+            if t == 0:
+                act(A("ZP"), A("Z0"), scale=K(36))
+                act(A("ZQ"), A("Z0"), scale=K(37))
+            else:
+                masks(0, 256, "P5", "P6")
+            act(A("EA", 0, 512), A("PE"), AF.Abs)
+            arrive()
+            spawn_lists()
+            act(A("EA", 512, 1024), A("PV"), AF.Abs)
+            act(A("EQ"), A("EA"), AF.Relu, bias=2048.0, scale=-2048.0)
+            act(A("CT", 128 * t + 128, 128 * t + 256), A("IO", 0, 128), scale=O(9), bias=K(62 + t))
+            blist()
+            cp(IND(A("IA"), A("SO", 40, 48)), A("ST", YC, VW))
+            cp(IND(A("XB"), A("SO", 40, 48)), A("ZZ"))
+            if t == 0:
+                zero("AE", 2)
+                zero("AH", 2)
+                zero("AE", 6)
+                zero("AH", 6)
+                asel(A("B0", 0, 128), A("B0", 128, 256), [[0, 8], [-1, 16]], OP.is_ge, 7, 0)
+                flmat(0, 4)
+                flmat(1, 4)
+                asel(A("B7"), A("BO"), [[0, 16], [1, 8]], OP.not_equal, -7, 0)
+                for d in (2, 6, 1, 3, 5, 7):
+                    flmat(0, d)
+                    flmat(1, d)
+            else:
+                for d in (3, 5, 7):
+                    zero("AE", d)
+                    zero("AH", d)
+                iota(A("TT", 768, 784), [[0, 16]])
+        else:
+            cp(A("SO", 32, 40), A("SI", 32, 40))
+            flags(t, 0)
+            cp(A("SO", 56, 64), A("PV", 8, 16))
+            flags(t, 1)
+            masks(256, 384, "P6", "P7")
+            fold([(0, d) for d in (1, 3, 5, 7)], False, False)
+            vwrite()
+            dma("s", H(T.yv[:, :]), A("VB", 0, 1152))
+            arrive()
+            fold([(1, d) for d in (1, 3, 5, 7)], False, True)
+            blist()
+            cp(IND(A("XB"), A("SO", 40, 48)), A("ZZ"))
+            dma("s", H(T.yx[:, :]), A("XB"))
+            cp(IND(A("IA"), A("SO", 40, 48)), A("ST", YC, VW))
+            cp(A("S2", 0, 8), A("PE", 0, 8))
+            cp(A("S2", 8, 16), A("PV", 8, 16))
+            ts(A("S2", 16, 32), A("S2", 0, 16), PW - 1, OP.bitwise_and)
+            ts(A("PO", 48 + 8 * t, 56 + 8 * t), A("S2", 16, 24), 1.0, OP.add)
+            cp(A("PO", 120 + 8 * t, 128 + 8 * t), A("S2", 24, 32))
+            scan(A("TT", 0, 512), A("SCM", 0, 512), A("P0"), OP.mult, OP.add)
+            scan(A("TT", 512, 769), A("SCM", 512, 769), A("P1", 0, 257), OP.mult, OP.add, A("TT", 511, 512))
+            tw = A("TT")
+            act(A("OE", 0, S0), IND(tw, A("PO", 0, 48)), bias=-1.0)
+            mm(A("P6", 0, 256), [(A("ZS", 15 - p, 143 - p), A("IA", 256 * p, 256 * p + 256)) for p in range(16)])
+            tt(A("TM", 0, 384), IND(tw, A("PO", 48, 72)), A("MM", 0, 384), OP.mult)
+            tt(A("TM", 384, 768), IND(tw, A("PO", 120, 144)), A("MM", 384, 768), OP.mult)
+            mm(A("P4", 0, 384), [(A("BOH"), A("TM", 0, 384))])
+            mm(A("P5", 0, 384), [(A("BOH"), A("TM", 384, 768))])
+            ts(A("OH", 0, 512), IND(tw, A("PO", 72, 104)), -1.0, OP.add)
+            act(A("WN"), A("P6", 0, 256))
+            dma("s", H(T.yw[:, :]), A("WN"))
+            act(A("OE", S0, 1152), A("P4", 0, 384), bias=-1.0)
+            dma("s", H(T.ye[:, :]), A("OE", p=(7, 128, 16)))
+            act(A("OH", 512, S0), IND(tw, A("PO", 104, 120)), bias=-1.0)
+            ts(A("OH", S0, 1152), A("P5", 0, 384), -1.0, OP.add)
+            dma("a", H(T.yh[:, :]), A("OH", p=(15, 128, 16)))
+
+    for sem in cnt:
+        if cnt[sem]:
+            wait("s" if sem[0] == "d" else "g", sem, cnt[sem])

@@ -5,6 +5,8 @@ C, L, S0, NT = 4096, 128, 768, 3
 DUM, YC = 1168, 1296
 VW = YC + L
 PW = 1024
+EARLY, XS, XS0, XA = 1, 192, 192, 80
+EB = 4
 BF, F32, I32, U16 = "bfloat16", "float32", "int32", "uint16"
 
 
@@ -15,7 +17,7 @@ def _sb(n, d):
 SCRATCH = {
     "XB": _sb(C, BF), "VB": _sb(VW, BF), "ST": _sb(VW, BF), "IA": _sb(C, BF), "GX": _sb(3200, BF), "GI": _sb(3072, BF),
     "BT": _sb(3072, BF), "MS": _sb(3072, BF), "MT": _sb(128, BF), "TH": _sb(16, BF), "THF": _sb(4, F32),
-    "LD0": _sb(1024, BF), "LD1": _sb(1024, BF), "LD2": _sb(1024, BF), "AE": _sb(13 * PW, BF), "AH": _sb(13 * PW, BF),
+    "LD0": _sb(1024, BF), "LD1": _sb(1024, BF), "LD2": _sb(1024, BF), "AE": _sb((13 + EB) * PW, BF), "AH": _sb(13 * PW, BF),
     "WL": _sb(256, I32), "W1": _sb(256, F32), "W2": _sb(256, F32), "WO": _sb(256, U16), "WN": _sb(256, F32),
     "EL": _sb(96, I32), "E1": _sb(192, I32), "NP": _sb(288, BF),
     "IO": _sb(144, F32), "IG": _sb(128, F32), "IM": _sb(128, F32), "I8": _sb(128, F32),
@@ -30,7 +32,7 @@ SCRATCH = {
     "U": _sb(64, I32), "U1": _sb(64, I32), "UU": _sb(64, I32), "UB": _sb(64, I32), "UA": _sb(192, I32), "UC": _sb(192, I32),
     "AO": _sb(192, U16), "SL": _sb(192, U16), "AC": _sb(4, F32), "SG": _sb(384, BF), "NPB": _sb(192, BF), "VL": _sb(192, F32),
     "KY": _sb(192, F32), "DFL": _sb(192, F32), "SC": _sb(192, F32), "D1": _sb(128, F32), "D2": _sb(128, F32),
-    "SR": _sb(128, BF), "NR": _sb(8, BF), "PL": _sb(16, F32), "DL": _sb(16, F32), "SI": _sb(64, I32), "SO": _sb(64, U16), "LN": _sb(16, I32), "S2": _sb(32, I32),
+    "SR": _sb(128, BF), "NR": _sb(8, BF), "PL": _sb(16, F32), "DL": _sb(16, F32), "SI": _sb(64, I32), "SO": _sb(64, U16), "LN": _sb(24, F32), "Z4": _sb(144, BF), "Z8": _sb(144, BF), "IN": _sb(128, BF), "ZR": _sb(800, BF), "S2": _sb(32, I32),
     "G1": _sb(128, BF), "G2": _sb(128, BF), "WB": _sb(128, BF), "SP": _sb(384, BF), "STP": _sb(128, BF), "BS": _sb(128, BF),
     "M1": _sb(128, BF), "DF": _sb(128, BF), "ZZ": _sb(128, BF),
     "PO": _sb(144, U16), "TT": _sb(784, F32), "MM": _sb(768, F32), "TM": _sb(768, "float16"), "BOH": _sb(128, "float16"), "OE": _sb(1152, F32), "OH": _sb(1152, F32),
@@ -38,7 +40,7 @@ SCRATCH = {
 PSUM = ["P0", "P1", "PE", "PV", "P4", "P5", "P6", "P7"]
 for _n in PSUM:
     SCRATCH[_n] = ("psum", [128, 512], F32)
-NDMA = 32
+NDMA = 40
 SEMAPHORES = ["sv", "sa", "sp", "sg", "sent", "arr0", "arr1", "arr2"] + ["d%d" % i for i in range(NDMA)]
 
 
@@ -175,7 +177,8 @@ def rank_program(g, core, T, topo):
         return A("O", r, r + 1)
 
     def zero(nm, d):
-        iota(A(nm, d * PW - 16, d * PW + 784), [[0, 800]])
+        lo = (d + (EB if nm == "AE" else 0)) * PW - 16
+        dma("s", A(nm, lo, lo + 800), A("ZR"))
 
     dma("a", A("EL", 0, 48), H(T.e0[:, :]))
     dma("s", A("EL", 48, 96), H(T.h0[:, :]))
@@ -193,7 +196,6 @@ def rank_program(g, core, T, topo):
     iota(A("KI", 32, 40), [[24, 8]], 23, 0, False)
     iota(A("KI", 40, 48), [[1, 8]], 0, 0, False)
     iota(A("I8"), [[1, 16], [0, 8]])
-    iota(A("IG"), [[1, 8], [0, 16]])
     iota(A("IM"), [[0, 8], [1, 16]])
     ms(A("ST", 0, S0), 0.0)
     ms(A("ON"), 1.0)
@@ -211,17 +213,23 @@ def rank_program(g, core, T, topo):
     ts(K(30), kR, 2.0, OP.is_equal, 8.0, OP.mult)
     ts(K(7), k7, 32.0, OP.mult, kH, OP.add)
     ts(A("O"), A("IO", 0, 16), kR, OP.is_equal)
-    ts(A("ST", 0, S0), A("ST", 0, S0), K(30), OP.add)
+    ts(A("K", 18, 22), A("IO", 0, 4), kS, OP.is_equal)
+    ts(A("K", 22, 26), A("IO", 0, 4), kQ, OP.is_equal)
+    ts(A("CM", 0, 8), A("IO", 0, 8), kG, OP.is_equal)
+    ts(K(35), kG, 16.0, OP.mult, 15.0, OP.add)
+    ts(K(26), K(18), 32.0, OP.mult, K(19), OP.add)
+    ts(K(50), kQ, 2.0, OP.is_lt, K(21), OP.is_gt)
+    ts(A("Z0"), A("IO"), K(35), OP.is_equal)
     act(K(8), kR, scale=2.0, bias=1.0)
     act(K(9), kG, scale=2.0)
     act(K(10), kG, scale=2.0, bias=1.0)
+    act(A("ST", 0, S0), A("ST", 0, S0), bias=K(30))
     act(K(17), kR, scale=1.5)
     act(A("K", 11, 14), A("IO", 0, 24, 8), bias=k7)
     act(A("NP", 240, 288), A("IO", 0, 48))
     act(A("NP", 192, 240), A("IO", 0, 48), scale=0.0, bias=K(17))
     act(A("K", 14, 17), A("K", 11, 14), AF.Square, bias=0.5)
     act(A("K", 14, 17), A("K", 14, 17), bias=0.75)
-    act(K(35), kG, scale=16.0, bias=15.0)
     ts(A("KI", 0, 16), A("KI", 0, 16), kR, OP.add)
     ts(A("KI", 16, 32), A("KI", 16, 32), K(7), OP.add)
     ts(A("LH0"), A("I8"), K(9), OP.is_equal, K(8), OP.mult)
@@ -236,14 +244,13 @@ def rank_program(g, core, T, topo):
     for j, row, q in ((4, 8, "s"), (5, 9, "s"), (0, 0, "a"), (1, 4, "s"), (2, 1, "a"), (3, 5, "s")):
         dma(q, A("ST", 0, S0, p=(row, 128, 16)), A("NP", 48 * j, 48 * j + 48), True)
     run("v", lambda: g.vector.transpose(T.W2[:, :], T.W1[:, :]), A("W2"), [A("W1")])
-    ts(A("K", 18, 22), A("IO", 0, 4), kS, OP.is_equal)
-    ts(A("K", 22, 26), A("IO", 0, 4), kQ, OP.is_equal)
+    ts(A("DM"), A("IM"), kR, OP.is_equal)
     cp(A("WO"), IND(A("W2"), A("KO", 16, 32)))
 
     def offsets(t):
-        yb = "LD%d" % (t - 1) if t else "VB"
-        mm(A("P4", 0, 64), [(A("LH0"), A(yb, 0, L, 2)), (A("LH1"), A(yb, 1, L, 2))])
-        steps = [lambda: cp(A("U1"), A("P4", 0, 64)),
+        yb = "G2" if t else "VB"
+        mm(A("PE", 0, 64), [(A("LH0"), A(yb, 0, L, 2)), (A("LH1"), A(yb, 1, L, 2))])
+        steps = [lambda: cp(A("U1"), A("PE", 0, 64)),
                  lambda: ts(A("U"), A("U1"), 4095, OP.bitwise_and),
                  lambda: tt(A("UU"), A("U"), A("U"), OP.mult)]
         for m in range(3):
@@ -256,12 +263,7 @@ def rank_program(g, core, T, topo):
         return steps
 
     steps = offsets(0)
-    ts(K(26), K(18), 32.0, OP.mult, K(19), OP.add)
-    steps[0]()
-    ts(A("Z0"), A("IO"), K(35), OP.is_equal)
-    steps[1]()
-    ts(A("CM", 0, 8), A("IO", 0, 8), kG, OP.is_equal)
-    for s in steps[2:]:
+    for s in steps:
         s()
     act(K(27), K(21), bias=K(26))
     act(K(28), K(20), scale=float(PW), bias=K(26))
@@ -279,6 +281,8 @@ def rank_program(g, core, T, topo):
     act(A("FV"), A("CM", 0, 8), scale=K(48))
     act(A("G8"), A("CM", 0, 8), scale=-8192.0)
     asel(A("ID"), A("ON"), [[-1, 128]], OP.is_equal, 0, 1)
+    iota(A("IN"), [[0, 128]], -1)
+    asel(A("IN"), A("IN"), [[-1, 128]], OP.is_equal, 0, 1)
     iota(A("I24"), [[1, 16], [0, 24]])
     iota(A("RK"), [[0, 192]])
     iota(A("VB", S0, YC), [[0, YC - S0]])
@@ -287,30 +291,26 @@ def rank_program(g, core, T, topo):
     wait("g", "sg", cnt["sg"])
     iota(A("RK", p=(32, 33)), [[0, 24], [1, 8]])
     wait("g", "sg", cnt["sg"])
-    iota(A("SEG"), [[0, 1024]], 1)
-    asel(A("SEG"), A("SEG"), [[0, 128], [1, 8]], OP.is_gt, 0, 0)
-    iota(A("LN", 0, 8), [[16, 8]], 0, 0, False)
+    iota(A("ZR"), [[0, 800]])
+    iota(A("SEG"), [[0, 128], [256, 8]])
+    iota(A("BOF"), [[0, 128]], 1)
+    asel(A("BOF"), A("BOF"), [[-16, 8], [0, 16]], OP.is_ge, 0, 1)
+    asel(A("BOF"), A("BOF"), [[16, 8], [0, 16]], OP.is_ge, 15, -1)
+    iota(A("DFL"), [[0, 192]])
+    iota(A("PL", 8, 16), [[0, 8]])
     iota(A("DL", 0, 8), [[0, 8]], DUM, 1)
     iota(A("DL", 8, 16), [[0, 8]], 2048 * 3072 + YC, 2049)
     asel(A("TRI"), A("ON"), [[-1, 128]], OP.is_ge, 0, 1)
     iota(A("SCM"), [[0, 784]], 1)
-    for d in (4, 1):
+    for d in (4, 2, 6):
         zero("AE", d)
         zero("AH", d)
 
-    def consts_v():
-        ts(A("DM"), A("IM"), kR, OP.is_equal)
-        ts(A("BOF"), A("IG"), kG, OP.is_equal)
-        ts(A("BOH"), A("IG"), kG, OP.is_equal)
-        ms(A("DFL"), 0.0)
-        ms(A("PL", 8, 16), 0.0)
-        ts(A("LN", 0, 8), A("LN", 0, 8), kR, OP.add)
-        ts(K(50), kQ, 2.0, OP.is_lt, K(21), OP.is_gt)
-        ts(A("DFL", 0, 192, 24), A("DL", 8, 16), 1.0 / 2048, OP.mult)
-        ts(A("LN", 8, 16), A("LN", 0, 8), 32.0, OP.mult)
-
     def consts_a():
-        act(A("VB", YC, VW), A("VB", 0, L))
+        act(A("LN", 0, 8), A("IO", 0, 128, 16), bias=kR)
+        act(A("LN", 8, 16), A("LN", 0, 8), scale=32.0)
+        act(A("LN", 16, 24), A("LN", 0, 8), bias=float(DUM))
+        act(K(55), O(0), scale=4096.0)
         act(A("THF", 0, 3), A("TH", 0, 3))
         act(K(49), O(11), scale=-100.0)
         act(K(51), K(24), scale=-1.0)
@@ -325,9 +325,14 @@ def rank_program(g, core, T, topo):
             act(K(61 + t), O(8), scale=4.0 * t, bias=K(61 + t))
         act(A("FS"), A("CM", 0, 8), scale=K(38))
         act(A("CM", 8, 16), A("CM", 0, 8), scale=2048.0)
+
+    def consts_a1():
+        act(A("DFL", 0, 192, 24), A("DL", 8, 16), scale=1.0 / 2048)
+        act(A("VB", YC, VW), A("VB", 0, L))
         act(A("NI"), A("ID"), scale=-2048.0)
         act(A("ST", DUM, YC), A("IO", 0, 128), scale=K(53), bias=K(56))
         act(A("ZM"), A("Z0"), scale=K(8))
+        act(A("Z8"), A("ZM"), scale=8.0)
         act(A("CT", 0, 128), A("IO", 0, 128), scale=O(9), bias=K(61))
         act(A("DD"), A("ID"), scale=K(51))
 
@@ -335,28 +340,36 @@ def rank_program(g, core, T, topo):
         act(A("BO"), A("BOF"))
         act(A("LD"), A("BOF"), scale=K(49))
         act(A("DG"), A("ID"), scale=K(50))
+
+    def consts_a6():
         act(A("ZE"), A("Z0"), scale=K(40))
         act(A("ZH"), A("Z0"), scale=K(41))
-        act(A("CM", 16, 24), A("CM", 0, 8), scale=K(38))
-        act(A("HI"), A("ID"), scale=4096.0)
-        act(A("B0", 128, 256), A("BO"), scale=O(0))
-        act(K(12), O(7), bias=O(15))
+        act(A("Z4"), A("Z0"), scale=K(55))
 
     def consts_a4():
+        act(A("CM", 16, 24), A("CM", 0, 8), scale=K(38))
+        act(A("HI"), A("ID"), scale=4096.0)
         for gg in range(8):
             act(A("SEL", 128 * gg, 128 * gg + 128), A("ON"), scale=A("CM", 16 + gg, 17 + gg))
+
+    def consts_a5():
+        act(A("B0", 128, 256), A("BO"), scale=O(0))
+        act(K(12), O(7), bias=O(15))
+        act(A("ZP"), A("Z0"), scale=K(36))
+        act(A("ZQ"), A("Z0"), scale=K(37))
 
     def build(j, q):
         o, i = A("IA", 512 * j, 512 * j + 512), IND(A("ST", 0, S0), A("WO", 32 * j, 32 * j + 32))
         (act if q == "a" else cp)(o, i)
 
+    consts_a()
     for j in range(8):
         build(j, "aavavava"[j])
     act(A("ST", YC, VW), A("ST", 0, L))
     ts(A("FEN"), A("I24"), K(52), OP.is_equal, K(54), OP.mult)
 
     peers = [T.cores[(rank - d) % N] for d in range(1, N)]
-    SB = ("P6", "P4", "P6")
+    SB = ("P4", "P5", "P4")
 
     def gx(lo, hi, q):
         (act if q == "a" else cp)(A("GX", 16 * lo, 16 * hi), IND(A("XB"), A("AO", lo, hi)))
@@ -384,7 +397,7 @@ def rank_program(g, core, T, topo):
         tt(A("BT", lo, hi), IND(A("VB", 0, 1152), A("SL", 64 * m, 64 * m + 64)), A("GX", lo, hi), OP.is_gt)
 
     def mx(m):
-        scan(A("MS", 1024 * m, 1024 * m + 1024), A("SEG"), A("GX", 1024 * m, 1024 * m + 1024), OP.mult, OP.max)
+        scan(A("MS", 1024 * m, 1024 * m + 1024), A("SEG"), A("GX", 1024 * m, 1024 * m + 1024), OP.min, OP.max)
 
     def count(m):
         for kk in range(8):
@@ -396,32 +409,33 @@ def rank_program(g, core, T, topo):
 
     def parallel():
         act(A("SG"), A("PE", 0, 384), AF.Sign, bias=0.0625)
-        mm(A("P7", 0, 192), [(A("ID"), A("SG", 0, 192)), (A("ID"), A("SG", 192, 384))])
+        mm(A("P4", 256, 448), [(A("ID"), A("SG", 0, 192)), (A("ID"), A("SG", 192, 384))])
         act(A("VL"), A("PV", 0, 192), bias=K(31))
-        act(A("NPB"), A("P7", 0, 192), AF.Abs, scale=28.0 * 4096, bias=23.0 * 4096)
+        act(A("NPB"), A("P4", 256, 448), AF.Abs, scale=28.0 * 4096, bias=23.0 * 4096)
 
     def fold(ds, start, stop, first=()):
-        prs = list(first) + [(A("FL", 128 * (7 * o + d - 1), 128 * (7 * o + d)), ("AE", "AH")[o], d * PW - 1 + o) for (o, d) in ds]
+        prs = list(first) + [(A("FL", 128 * (7 * o + d - 1), 128 * (7 * o + d)), ("AE", "AH")[o], (d + EB * (1 - o)) * PW - 1 + o) for (o, d) in ds]
         mm(A("P0"), [(l, A(nm, c0, c0 + 512)) for (l, nm, c0) in prs], start, stop)
         mm(A("P1", 0, 257), [(l, A(nm, c0 + 512, c0 + 769)) for (l, nm, c0) in prs], start, stop)
 
     def slots(t, bank):
-        cp(A("SO", 48, 64), A(bank, 0, 16))
+        cp(A("SO", 48, 64), A(bank, 256, 272))
         if t == 0:
             return
-        cp(A("S2", 0, 16), A(bank, 0, 16))
+        cp(A("S2", 0, 16), A(bank, 256, 272))
         ts(A("S2", 16, 32), A("S2", 0, 16), PW - 1, OP.bitwise_and)
         ts(A("PO", 48 + 8 * t, 56 + 8 * t), A("S2", 16, 24), 1.0, OP.add)
         cp(A("PO", 120 + 8 * t, 128 + 8 * t), A("S2", 24, 32))
 
     def flags(t, o):
-        cp(IND(A(("AE", "AH")[o]), A("SO", 48 + 8 * o, 56 + 8 * o)), A("SP", 128 * t, 128 * t + 128))
+        lo = (EB - (4 >> t)) * PW if o == 0 else (4 >> t) * PW
+        cp(IND(A(("AE", "AH")[o], lo), A("SO", 48 + 8 * o, 56 + 8 * o)), A("SP", 128 * t, 128 * t + 128))
 
-    def masks(lo, hi, b0, b1):
+    def masks(lo, hi):
         for o in range(2):
-            mm(A((b0, b1)[o], 0, hi - lo), [(A("LO", 128 * o, 128 * o + 128), A("ST", S0 + lo, S0 + hi)), (A("HN"), A("SP", lo, hi))])
+            mm(A("P5", 256 * o, 256 * o + hi - lo), [(A("LO", 128 * o, 128 * o + 128), A("ST", S0 + lo, S0 + hi)), (A("HN"), A("SP", lo, hi))])
         for o in range(2):
-            ts(A("MM", 384 * o + lo, 384 * o + hi), A((b0, b1)[o], 0, hi - lo), K(17), OP.is_equal, K(10 - o), OP.mult)
+            ts(A("MM", 384 * o + lo, 384 * o + hi), A("P5", 256 * o, 256 * o + hi - lo), K(17), OP.is_equal, K(10 - o), OP.mult)
 
     def consts_a3():
         act(K(9), K(12), scale=2.0, bias=-1.0)
@@ -433,7 +447,6 @@ def rank_program(g, core, T, topo):
         act(A("LO", 0, 128), A("B7"), scale=O(2))
         act(A("LO", 128, 256), A("B7"), scale=O(6))
         act(A("HN"), A("ID"), scale=-100.0)
-        act(A("SCM"), A("SCM"), scale=K(12))
 
     def flmat(o, d):
         asel(A("FL", 128 * (7 * o + d - 1), 128 * (7 * o + d)), A("B0", 128 * o, 128 * o + 128), [[0, 8], [1, 16]], OP.is_ge, 1 - 8 * o - d, 0)
@@ -447,14 +460,21 @@ def rank_program(g, core, T, topo):
         gi(1)
         gv(0)
         if t:
-            gx(64, 128, "a")
-            slots(t - 1, "P7")
-            flags(t - 1, 0)
+            gx(XA, 128, "a")
+            if XA > 64:
+                gx(64, XA, "v")
+            if not EARLY:
+                slots(t - 1, "P5")
+                flags(t - 1, 0)
             if t == 2:
                 fold([(0, 2), (0, 6)], False, False)
-            flags(t - 1, 1)
+            if EARLY < 2:
+                flags(t - 1, 1)
             if t == 2:
                 fold([(1, 2), (1, 6)], False, False)
+            else:
+                for d in (1, 3, 5, 7):
+                    zero("AH", d)
         sl(1)
         if t == 1:
             wrap(A("P0", 0, 56), "ZP", "ST", 0, 56)
@@ -465,66 +485,86 @@ def rank_program(g, core, T, topo):
         if t == 1:
             cp(A("PO", 0, 56), A("P0", 0, 56))
             cp(A("PO", 72, 128), A("P0", 56, 112))
-        gx(128, 192, "a")
+        xs = XS if t else XS0
+        gx(128, xs, "a")
         mx(0)
         mx(1)
-        tt(A("MT"), A("MS", 7, 1024, 8), A("MS", 1031, 2048, 8), OP.max)
-        if t == 0:
-            consts_v()
+        if xs < 192:
+            gx(xs, 192, "v")
         parallel()
+        ma, mb = A("MS", 7, 1024, 8), A("MS", 1031, 2048, 8)
+        mm(A("PE", 0, 128), [(A("ID"), ma), (A("IN"), mb)])
+        act(A("MT"), A("PE", 0, 128), AF.Relu)
         gv(2)
         count(0)
+        mm(A("PE", 128, 256), [(A("ID"), A("MT")), (A("ID"), mb)])
         count(1)
+        act(A("MT"), A("PE", 128, 256))
         count(2)
         mx(2)
         if t == 0:
-            consts_a()
+            consts_a1()
             consts_a2()
-            consts_a4()
-        if t == 1:
-            consts_a3()
+        else:
+            act(A("EA", 0, 512), A("P6"), AF.Abs)
+            act(A("EA", 512, 1024), A("P7"), AF.Abs)
+            act(A("EQ"), A("EA"), AF.Relu, bias=2048.0, scale=-2048.0)
         tt(A("KY"), A("P5", 0, 192), A("VL"), OP.max)
         scan(A("SC"), A("DFL"), A("KY"), OP.max, OP.min)
         tt(A("D1"), IND(A("SC"), A("KO", 32, 40)), A("DM"), OP.mult)
         ts(A("NR"), A("SC", 23, 192, 24), 3072.0, OP.is_ge)
         mm(A("P4", 0, 8), [(A("D1"), A("CM", 8, 16))])
-        mm(A("P7", 0, 8), [(A("ST", YC, VW), A("FS")), (A("NI"), A("NR"))], True, t == 0)
+        mm(A("P7", 0, 8), [(A("ST", YC, VW), A("FS")), (A("ON", p=(0, 1)), A("RK", 16, 24, p=(0, 1))), (A("NI"), A("NR"))], True, t == 0)
         if t:
             wait("p", "sp", cnt["sp"])
             for gg in range(8):
                 mm(A("P7", gg, gg + 1), [(A("EQ", 128 * gg, 128 * gg + 128), A("NR", gg, gg + 1))], False, gg == 7)
+        if not last:
+            act(A("SR"), IND(A("SC"), A("KO", 32, 40)), AF.Sign, bias=-3071.9)
+            mm(A("PV", 0, 1), [(A("SR"), A("ON", 0, 1))])
+            act(A("AC", 0, 1), A("PV", 0, 1), bias=64.0, scale=-0.5)
         if t == 1:
-            fold([(0, 4), (1, 4)], True, False, [(A("ID"), "SCM", 0)])
+            fold([(0, 4), (1, 4)], True, False)
+        if t == 2:
+            fold([], False, False, [(A("ID"), "SCM", 0)])
         tt(A("GX", 3072, 3200), A("MT"), A("MS", 2055, 3072, 8), OP.max)
         cp(A("SI", 0, 8), A("P4", 0, 8))
         ts(A("SI", 8, 16), A("SI", 0, 8), 11, OP.logical_shift_right)
         ts(A("SI", 16, 24), A("SI", 0, 8), 2047, OP.bitwise_and)
         cp(A("SO", 8, 24), A("SI", 8, 24))
         cp(A("G1"), IND(A("GX"), A("SO", 8, 16)))
-        tt(A("G2"), IND(A("VB"), A("SO", 16, 24)), A("G1"), OP.subtract)
-        ts(A("PL", 0, 8), A("P7", 0, 8), 2048.0, OP.add)
-        tt(A("PL", 0, 8), A("PL", 0, 8), A("DL", 0, 8), OP.min)
-        tt(A("D2"), IND(A("PL"), A("KO", 40, 48)), A("DM"), OP.mult)
-        if not last:
-            act(A("SR"), IND(A("SC"), A("KO", 32, 40)), AF.Sign, bias=-3071.9)
-        act(A("BS"), IND(A("ST"), A("SO", 16, 24)))
-        act(A(land, 0, L), A("G2"), AF.Abs)
-        y = A(land, 0, L)
-        order("g", y[1], [])
+        tt(A(land, 0, L), IND(A("VB"), A("SO", 16, 24)), A("G1"), OP.subtract)
+        order("g", [(land, 0, L)], [])
         trs = []
         for d in range(1, N):
             dst = peers[d - 1]
             rid, pid, _ = topo.addr(dst)
             trs.append(RemoteDMATransfer(dst_ids=[DstId(rid=rid, pnc=pid)], dma_engine_mask=1 << topo.engines(core, dst)[d - 1],
-                                         remote_sem=T.sem["arr%d" % t], src=y[0], dst=T[land][:, L * d:L * d + L]))
+                                         remote_sem=T.sem["arr%d" % t], src=T[land][:, 0:L], dst=T[land][:, L * d:L * d + L]))
         g.remote_dma_fused(trs, local_sem=T.sem.sent)
         cnt["sent"] += N - 1
+        tt(A("PL", 0, 8), A("P7", 0, 8), A("DL", 0, 8), OP.min)
+        tt(A("D2"), IND(A("PL"), A("KO", 40, 48)), A("DM"), OP.mult)
+        act(A("BS"), IND(A("ST"), A("SO", 16, 24)))
+        act(A("G2"), A(land, 0, L), AF.Abs)
+        y = A("G2")
         mm(A("P6", 256, 264), [(A("D2"), A("CM", 0, 8))])
+        steps = [] if last else offsets(t + 1)
+
+        def step(n=1):
+            for _ in range(n):
+                if steps:
+                    steps.pop(0)()
         ts(A("WB"), y, A("THF", t, t + 1), OP.is_ge)
         cp(A("SO", 24, 32), A("P6", 256, 264))
-        wrap(A("P4", 64, 72), "ZM", land, 0, 8)
+        wrap(A("P4", 64, 72), "Z8", "G2", 0, 8)
         act(A("STP"), IND(A("ST"), A("SO", 24, 32)))
-        tt(A("DF"), IND(A("VB", 0, YC), A("SO", 24, 32)), y, OP.subtract)
+        if t == 0:
+            consts_a6()
+        step(7)
+        if last:
+            tt(A("DF"), IND(A("VB", 0, YC), A("SO", 24, 32)), y, OP.subtract)
+            cp(A("BOH"), A("BO"))
         ct = A("CT", 128 * t, 128 * t + 128)
         n0 = S0 + L * t
         sp = A("SP", 128 * t, 128 * t + 128)
@@ -532,38 +572,34 @@ def rank_program(g, core, T, topo):
         mm(A("P6", 0, 128), [(A("DG"), A("STP")), (A("ID"), ct)])
         mm(A("P7", 0, 128), [(A("DD"), A("STP")), (A("ID"), ct)])
         act(A("ST", n0, n0 + L), A("P6", 0, 128))
-        cp(A("SI", 24, 32), A("P4", 64, 72))
-        ts(A("SI", 32, 40), A("SI", 24, 32), 112, OP.bitwise_and)
+        cp(A("SI", 32, 40), A("P4", 64, 72))
         ts(sp, A("P5", 0, 128), 7.5, OP.is_ge)
-        ts(A("SI", 24, 32), A("SI", 32, 40), 8.0, OP.mult)
-        if not last:
-            steps = offsets(t + 1)
-            mm(A("P6", 0, 1), [(A("SR"), A("ON", 0, 1))])
-            act(A("AC", 0, 1), A("P6", 0, 1), bias=64.0, scale=-0.5)
+        ts(A("SI", 24, 32), A("SI", 32, 40), 896, OP.bitwise_and)
         tt(A("M1"), A("P7", 0, 128), sp, OP.mult)
         tt(A("SI", 32, 40), A("SI", 24, 32), A("LN", 0, 8), OP.add)
+        step()
 
         def spawn_lists():
-            wrap(A("PE" if last else "P7", 0, 8), "ZE", "ST", n0, 8)
             if last:
+                wrap(A("PE", 0, 8), "ZE", "STP", 0, 8)
                 cp(A("SO", 48, 56), A("PE", 0, 8))
-                wrap(A("PV", 8, 16), "ZH", "ST", n0, 8)
+                wrap(A("PV", 8, 16), "ZH", "STP", 0, 8)
             else:
-                wrap(A("P7", 8, 16), "ZH", "ST", n0, 8)
+                bank = "PV" if EARLY else "P5"
+                wrap(A(bank, 256, 264), "ZE", "STP", 0, 8)
+                wrap(A(bank, 264, 272), "ZH", "STP", 0, 8)
         if last:
             spawn_lists()
         mm(A("P5", 0, 128), [(A("ID"), A("BS")), (A("ID"), A("M1"))])
         act(A("ST", YC, VW), A("P5", 0, 128))
 
-        def vwrite():
-            tt(A("DF"), A("DF"), sp, OP.mult)
-            cp(A("SO", 32, 40), A("SI", 32, 40))
-            tt(IND(A("VB", 0, YC), A("SO", 24, 32)), A("DF"), y, OP.add)
-            tt(A("VB", n0, n0 + L), y, sp, OP.mult)
+        def vlist():
+            mm(A("P6", 256, 264), [(A("Z4", 15 - p, 143 - p), A("SP", 128 * t + p, 128 * t + 128, 16)) for p in range(16)]
+               + [(A("D2"), A("CM", 0, 8))])
 
         def arrive():
             wait("a", "arr%d" % t, N - 1)
-            act(A("ZZ"), IND(A(land), A("SO", 32, 40)))
+            act(A("ZZ"), IND(A(land), A("SO", 32, 40)), AF.Abs)
             wrap(A("P4", 72, 80), "ZM", "ZZ", 0, 8)
 
         def blist():
@@ -575,34 +611,44 @@ def rank_program(g, core, T, topo):
         if not last:
             act(A("NC"), A("ST", YC, VW), scale=-1.0)
             act(A("VB", YC, VW), y)
-            steps[0]()
-            steps[1]()
-            vwrite()
-            for s in steps[2:]:
-                s()
+            act(A("VB", n0, n0 + L), y)
+            vlist()
+            if EARLY:
+                spawn_lists()
+            cp(A("SO", 32, 40), A("SI", 32, 40))
+            step(3)
+            tt(A("SI", 56, 64), A("P6", 256, 264), A("LN", 16, 24), OP.min)
+            step()
+            cp(A("SO", 0, 8), A("SI", 56, 64))
+            act(A("CT", 128 * t + 128, 128 * t + 256), A("IO", 0, 128), scale=O(9), bias=K(62 + t))
+            cp(IND(A("VB", 0, YC), A("SO", 0, 8)), y)
+            if EARLY:
+                slots(t, "PV")
+                for o in range(EARLY):
+                    flags(t, o)
+            if t == 1:
+                consts_a3()
+                masks(0, 256)
+            else:
+                consts_a5()
+            arrive()
+            if t == 0:
+                consts_a4()
+            else:
+                act(A("SCM"), A("SCM"), scale=K(12))
+            blist()
+            if not EARLY:
+                spawn_lists()
             for hb in range(2):
                 for gq in range(4):
                     s = A("SEL", 512 * hb + 128 * gq, 512 * hb + 128 * gq + 128)
-                    mm(A(("PE", "PV")[hb], 128 * gq, 128 * gq + 128), [(s, A("NC")), (A("ST", YC, VW), s), (A("HI"), A("TRI"))])
-            if t == 0:
-                act(A("ZP"), A("Z0"), scale=K(36))
-                act(A("ZQ"), A("Z0"), scale=K(37))
-            else:
-                masks(0, 256, "P5", "P6")
-            act(A("EA", 0, 512), A("PE"), AF.Abs)
-            arrive()
-            spawn_lists()
-            act(A("EA", 512, 1024), A("PV"), AF.Abs)
-            act(A("EQ"), A("EA"), AF.Relu, bias=2048.0, scale=-2048.0)
-            act(A("CT", 128 * t + 128, 128 * t + 256), A("IO", 0, 128), scale=O(9), bias=K(62 + t))
-            blist()
+                    mm(A(("P6", "P7")[hb], 128 * gq, 128 * gq + 128), [(s, A("NC")), (A("ST", YC, VW), s), (A("HI"), A("TRI"))])
             cp(IND(A("IA"), A("SO", 40, 48)), A("ST", YC, VW))
             cp(IND(A("XB"), A("SO", 40, 48)), A("ZZ"))
             if t == 0:
-                zero("AE", 2)
-                zero("AH", 2)
-                zero("AE", 6)
-                zero("AH", 6)
+                wait("s", "arr0", N - 1)
+                for d in (1, 3, 5, 7):
+                    zero("AE", d)
                 asel(A("B0", 0, 128), A("B0", 128, 256), [[0, 8], [-1, 16]], OP.is_ge, 7, 0)
                 flmat(0, 4)
                 flmat(1, 4)
@@ -611,18 +657,21 @@ def rank_program(g, core, T, topo):
                     flmat(0, d)
                     flmat(1, d)
             else:
-                for d in (3, 5, 7):
-                    zero("AE", d)
-                    zero("AH", d)
                 iota(A("TT", 768, 784), [[0, 16]])
         else:
             cp(A("SO", 32, 40), A("SI", 32, 40))
             flags(t, 0)
             cp(A("SO", 56, 64), A("PV", 8, 16))
             flags(t, 1)
-            masks(256, 384, "P6", "P7")
+            act(A("VB", n0, n0 + L), y)
+            masks(256, 384)
             fold([(0, d) for d in (1, 3, 5, 7)], False, False)
-            vwrite()
+            cp(A("S2", 0, 8), A("PE", 0, 8))
+            cp(A("S2", 8, 16), A("PV", 8, 16))
+            tt(A("DF"), A("DF"), sp, OP.mult)
+            ts(A("S2", 16, 32), A("S2", 0, 16), PW - 1, OP.bitwise_and)
+            tt(IND(A("VB", 0, YC), A("SO", 24, 32)), A("DF"), y, OP.add)
+            tt(A("VB", S0, 1152), A("VB", S0, 1152), A("SP"), OP.mult)
             dma("s", H(T.yv[:, :]), A("VB", 0, 1152))
             arrive()
             fold([(1, d) for d in (1, 3, 5, 7)], False, True)
@@ -630,9 +679,6 @@ def rank_program(g, core, T, topo):
             cp(IND(A("XB"), A("SO", 40, 48)), A("ZZ"))
             dma("s", H(T.yx[:, :]), A("XB"))
             cp(IND(A("IA"), A("SO", 40, 48)), A("ST", YC, VW))
-            cp(A("S2", 0, 8), A("PE", 0, 8))
-            cp(A("S2", 8, 16), A("PV", 8, 16))
-            ts(A("S2", 16, 32), A("S2", 0, 16), PW - 1, OP.bitwise_and)
             ts(A("PO", 48 + 8 * t, 56 + 8 * t), A("S2", 16, 24), 1.0, OP.add)
             cp(A("PO", 120 + 8 * t, 128 + 8 * t), A("S2", 24, 32))
             scan(A("TT", 0, 512), A("SCM", 0, 512), A("P0"), OP.mult, OP.add)
@@ -650,7 +696,7 @@ def rank_program(g, core, T, topo):
             act(A("OE", S0, 1152), A("P4", 0, 384), bias=-1.0)
             dma("s", H(T.ye[:, :]), A("OE", p=(7, 128, 16)))
             act(A("OH", 512, S0), IND(tw, A("PO", 104, 120)), bias=-1.0)
-            ts(A("OH", S0, 1152), A("P5", 0, 384), -1.0, OP.add)
+            act(A("OH", S0, 1152), A("P5", 0, 384), bias=-1.0)
             dma("a", H(T.yh[:, :]), A("OH", p=(15, 128, 16)))
 
     for sem in cnt:

@@ -2,11 +2,21 @@ from concourse.bass import DstId, RemoteDMATransfer
 from concourse.mybir import AluOpType as OP, ActivationFunctionType as AF
 
 C, L, S0, NT = 4096, 128, 768, 3
-DUM, YC = 1168, 1296
+DUM, YC = 1152, 1280
 VW = YC + L
 PW = 1024
-EARLY, XS, XS0, XA = 1, 192, 192, 80
-EB = 4
+XA = (104, 88, 88)
+KW = 25
+GM = 3079
+BUILD = "avavavav"
+FL1 = 2
+OHV = 32
+BT, MS = 3072, 6144
+TABLE = ((("AE", 2048, 5248, 256), ("AH", 2176, 4352, 256)), (("AE", 0, 3200, 256), ("AH", 0, 2176, 256)),
+         (("AE", 0, 6272, 512), ("GB", 0, 4224, 512)))
+CYC, PECYC, FIX, GFIX, GATHER, SCATTER, HOP = 0.00091, 0.00046, 0.01, 0.055, 1.25, 3.0, 0.25
+XLAG, FLOOR, NEXT, POOL, FIXA = 5.0, 64, 0.2, 2.4, 0.11
+HEAVY, GUARD, HOLD, TRAVEL, SWEEPS, EARLY = 0.3, 2.5, (8.0, 2.5, 2.5), (6.5, 4.2, 4.0), 3, 66.0
 BF, F32, I32, U16 = "bfloat16", "float32", "int32", "uint16"
 
 
@@ -15,31 +25,35 @@ def _sb(n, d):
 
 
 SCRATCH = {
-    "XB": _sb(C, BF), "VB": _sb(VW, BF), "ST": _sb(VW, BF), "IA": _sb(C, BF), "GX": _sb(3200, BF), "GI": _sb(3072, BF),
-    "BT": _sb(3072, BF), "MS": _sb(3072, BF), "MT": _sb(128, BF), "TH": _sb(16, BF), "THF": _sb(4, F32),
-    "LD0": _sb(1024, BF), "LD1": _sb(1024, BF), "LD2": _sb(1024, BF), "AE": _sb((13 + EB) * PW, BF), "AH": _sb(13 * PW, BF),
+    "XB": _sb(C, BF), "VB": _sb(VW, BF), "ST": _sb(VW, BF), "IA": _sb(C, BF), "GX": _sb(4096, BF), "GB": _sb(8192, BF),
+    "MT": _sb(256, BF), "TH": _sb(16, BF),
+    "LD0": _sb(1024, BF), "LD1": _sb(1024, BF), "LD2": _sb(1024, BF), "AE": _sb(6272, BF), "AH": _sb(4352, BF),
     "WL": _sb(256, I32), "W1": _sb(256, F32), "W2": _sb(256, F32), "WO": _sb(256, U16), "WN": _sb(256, F32),
     "EL": _sb(96, I32), "E1": _sb(192, I32), "NP": _sb(288, BF),
-    "IO": _sb(144, F32), "IG": _sb(128, F32), "IM": _sb(128, F32), "I8": _sb(128, F32),
+    "IO": _sb(144, F32), "IM": _sb(128, F32), "I8": _sb(128, F32),
     "PI": _sb(8, I32), "PJ": _sb(8, I32), "K": _sb(64, F32), "O": _sb(16, F32), "KI": _sb(48, I32), "KO": _sb(48, U16),
-    "BO": _sb(128, BF), "BOF": _sb(128, F32), "ID": _sb(128, BF), "LH0": _sb(128, BF), "LH1": _sb(128, BF),
-    "DM": _sb(128, F32), "CM": _sb(24, F32), "Z0": _sb(144, F32), "ZM": _sb(144, BF), "ZS": _sb(144, BF), "ZE": _sb(144, BF),
-    "ZH": _sb(144, BF), "ZP": _sb(144, BF), "ZQ": _sb(144, BF),
-    "FEH": _sb(16, BF), "FEN": _sb(384, BF), "I24": _sb(384, BF), "FV": _sb(8, BF), "FS": _sb(8, BF), "G8": _sb(8, BF), "RK": _sb(192, BF), "SEG": _sb(1024, BF),
-    "LD": _sb(128, BF), "DG": _sb(128, BF), "DD": _sb(128, BF), "NI": _sb(128, BF), "CT": _sb(384, BF), "SEL": _sb(1024, BF),
-    "TRI": _sb(128, BF), "NC": _sb(128, BF), "EA": _sb(1024, BF), "EQ": _sb(1024, BF), "ON": _sb(128, BF),
-    "FL": _sb(14 * 128, BF), "B0": _sb(256, BF), "B7": _sb(128, BF), "LO": _sb(256, BF), "HI": _sb(128, BF), "HN": _sb(128, BF), "SCM": _sb(784, BF),
-    "U": _sb(64, I32), "U1": _sb(64, I32), "UU": _sb(64, I32), "UB": _sb(64, I32), "UA": _sb(192, I32), "UC": _sb(192, I32),
-    "AO": _sb(192, U16), "SL": _sb(192, U16), "AC": _sb(4, F32), "SG": _sb(384, BF), "NPB": _sb(192, BF), "VL": _sb(192, F32),
-    "KY": _sb(192, F32), "DFL": _sb(192, F32), "SC": _sb(192, F32), "D1": _sb(128, F32), "D2": _sb(128, F32),
-    "SR": _sb(128, BF), "NR": _sb(8, BF), "PL": _sb(16, F32), "DL": _sb(16, F32), "SI": _sb(64, I32), "SO": _sb(64, U16), "LN": _sb(24, F32), "Z4": _sb(144, BF), "Z8": _sb(144, BF), "IN": _sb(128, BF), "ZR": _sb(800, BF), "S2": _sb(32, I32),
-    "G1": _sb(128, BF), "G2": _sb(128, BF), "WB": _sb(128, BF), "SP": _sb(384, BF), "STP": _sb(128, BF), "BS": _sb(128, BF),
+    "BO": _sb(128, BF), "ID": _sb(144, BF), "LH0": _sb(128, BF), "LH1": _sb(128, BF),
+    "DM": _sb(128, F32), "CM": _sb(8, F32), "Z0": _sb(144, F32), "ZM": _sb(144, BF), "ZS": _sb(144, BF), "ZE": _sb(144, BF),
+    "ZF": _sb(144, BF), "ZP": _sb(144, BF), "ZQ": _sb(144, BF), "Z8": _sb(144, BF),
+    "FEH": _sb(16, BF), "FEN": _sb(400, BF), "I24": _sb(400, BF), "FV": _sb(8, BF), "FS": _sb(8, BF), "G8": _sb(8, BF),
+    "RK": _sb(800, BF), "OI": _sb(128, BF), "SEG": _sb(1024, BF),
+    "LD": _sb(128, BF), "DG": _sb(128, BF), "DD": _sb(128, BF), "NI": _sb(128, BF), "CT": _sb(384, BF), "SEL": _sb(512, BF),
+    "TRI": _sb(128, BF), "EA": _sb(1024, BF), "EQ": _sb(1024, BF), "ON": _sb(128, BF),
+    "FL": _sb(14 * 128, BF), "B0": _sb(256, BF), "B7": _sb(128, BF), "LO": _sb(256, BF), "HI": _sb(128, BF), "HN": _sb(128, BF),
+    "SCM": _sb(784, BF), "U": _sb(64, I32), "U1": _sb(64, I32), "UU": _sb(64, I32), "UB": _sb(64, I32), "UA": _sb(192, I32),
+    "UC": _sb(192, I32), "AO": _sb(192, U16), "SL": _sb(192, U16), "AC": _sb(4, F32), "SG": _sb(400, BF), "NPB": _sb(200, BF),
+    "VL": _sb(200, F32), "SC": _sb(200, F32), "SF": _sb(8, F32), "D1": _sb(128, F32), "D2": _sb(128, F32),
+    "SR": _sb(128, BF), "NR": _sb(8, BF), "PL": _sb(16, F32), "SI": _sb(64, I32), "SO": _sb(64, U16), "LN": _sb(24, F32),
+    "IN": _sb(128, BF), "ZR": _sb(800, BF), "S2": _sb(64, I32),
+    "G1": _sb(128, BF), "WB": _sb(128, BF), "SP": _sb(384, BF), "STP": _sb(384, BF), "BS": _sb(128, BF),
     "M1": _sb(128, BF), "DF": _sb(128, BF), "ZZ": _sb(128, BF),
-    "PO": _sb(144, U16), "TT": _sb(784, F32), "MM": _sb(768, F32), "TM": _sb(768, "float16"), "BOH": _sb(128, "float16"), "OE": _sb(1152, F32), "OH": _sb(1152, F32),
+    "PO": _sb(144, U16), "TT": _sb(784, F32), "MM": _sb(768, F32), "MA": _sb(768, F32), "TM": _sb(768, "float16"),
+    "BOH": _sb(256, "float16"), "OE": _sb(1152, F32), "OH": _sb(1152, F32),
 }
 PSUM = ["P0", "P1", "PE", "PV", "P4", "P5", "P6", "P7"]
 for _n in PSUM:
     SCRATCH[_n] = ("psum", [128, 512], F32)
+START = {}
 NDMA = 40
 SEMAPHORES = ["sv", "sa", "sp", "sg", "sent", "arr0", "arr1", "arr2"] + ["d%d" % i for i in range(NDMA)]
 
@@ -71,12 +85,14 @@ def rank_program(g, core, T, topo):
             Q[q].wait_ge(T.sem[sem], val)
             waited[q][sem] = val
 
-    def order(q, reads, writes, dma=False):
+    def order(q, reads, writes, dma=False, keep=False):
         need = {}
         for rs, wr in ((reads, False), (writes, True)):
             for (nm, lo, hi) in rs:
                 bank = nm in PSUM
                 for (q2, sem, val, l2, h2, w2) in hist.get(nm, ()):
+                    if keep and wr and q2 == "dma":
+                        continue
                     same = q2 == q and not dma
                     if bank and not same:
                         hit = True
@@ -97,20 +113,29 @@ def rank_program(g, core, T, topo):
                     h[:] = [e for e in h if not (lo <= e[3] and e[4] <= hi and nm not in PSUM)]
                 h.append((q, sem, val, lo, hi, wr))
 
-    def run(q, fn, out, ins):
+    calls, due = [], [0.0]
+
+    def record(q, fn, reads, writes, cost, lag=HOP, kind="c", **kw):
+        calls.append(dict(q=q, fn=fn, r=reads, w=writes, cost=cost, lag=lag, kind=kind, due=due[0], **kw))
+
+    def run(q, fn, out, ins, per=1.0, cost=None, **kw):
         reads, writes = [], list(out[1])
         if len(out) == 3:
             reads += out[2]
-        for x in ins:
-            if isinstance(x, tuple):
-                reads += x[1]
-                if len(x) == 3:
-                    reads += x[2]
-        order(q, reads, writes)
-        sem = SEM[q]
-        fn().then_inc(T.sem[sem], 1)
-        cnt[sem] += 1
-        note(q, sem, cnt[sem], reads, writes)
+        aps = [x for x in ins if isinstance(x, tuple)]
+        for x in aps:
+            reads += x[1]
+            if len(x) == 3:
+                reads += x[2]
+        if cost is None:
+            ind = [x for x in [out] + aps if len(x) == 3]
+            if ind:
+                cost = GFIX + 16 * (ind[0][2][0][2] - ind[0][2][0][1]) * (SCATTER if len(out) == 3 else GATHER) * CYC
+            else:
+                if q == "v" and per == 1.0 and all(SCRATCH[x[1][0][0]][2] in (BF, U16, "float16") for x in [out] + aps if x[0].shape[1] > 1):
+                    per = 0.5
+                cost = FIX + max(FLOOR, out[0].shape[1] * per) * CYC if q == "v" else FIXA + out[0].shape[1] * CYC
+        record(q, fn, reads, writes, cost, heavy=cost > HEAVY and q in "va", **kw)
 
     def val(x):
         return x[0] if isinstance(x, tuple) else x
@@ -119,13 +144,19 @@ def rank_program(g, core, T, topo):
         run("v", lambda: g.vector.tensor_copy(o[0], i[0]), o, [i])
 
     def tt(o, a, b, op):
-        run("v", lambda: g.vector.tensor_tensor(o[0], a[0], b[0], op), o, [a, b])
+        run("v", lambda: g.vector.tensor_tensor(o[0], a[0], b[0], op), o, [a, b], 1.001 if a[1][0][0] in PSUM else 2.0)
 
     def ts(o, a, s1, op0, s2=None, op1=None):
         if op1 is None:
             run("v", lambda: g.vector.tensor_scalar(o[0], a[0], val(s1), None, op0), o, [a, s1])
         else:
             run("v", lambda: g.vector.tensor_scalar(o[0], a[0], val(s1), val(s2), op0, op1), o, [a, s1, s2])
+
+    def lin(o, i, a, b=None):
+        if b is None:
+            ts(o, i, a, OP.mult)
+        else:
+            ts(o, i, a, OP.mult, b, OP.add)
 
     def ms(o, c):
         run("v", lambda: g.vector.memset(o[0], c), o, [])
@@ -141,34 +172,125 @@ def rank_program(g, core, T, topo):
             kw["scale"] = val(scale)
         run("a", lambda: g.scalar.activation(o[0], i[0], f, **kw), o, [i, bias, scale])
 
-    def mm(o, pairs, start=True, stop=True):
-        for n, (l, r) in enumerate(pairs):
-            run("p", lambda: g.tensor.matmul(o[0], l[0], r[0], start and n == 0, stop and n == len(pairs) - 1), o, [l, r])
+    def lia(o, i, a, b=None):
+        act(o, i, scale=a, bias=b)
 
-    def iota(o, pat, base=0, cm=0, fl=True):
+    def mm(o, pairs, start=True, stop=True, fence=False):
+        fns = [lambda l=l, r=r, n=n: g.tensor.matmul(o[0], l[0], r[0], start and n == 0, stop and n == len(pairs) - 1)
+               for n, (l, r) in enumerate(pairs)]
+        cost = sum(max(64, o[0].shape[1]) * PECYC * (4 if SCRATCH[l[1][0][0]][2] == F32 else 1) for l, r in pairs)
+        run("p", fns, o, [x for pr in pairs for x in pr], cost=cost, fence=fence)
+
+    def iota(o, pat, base=0, cm=0, fl=True, solo=False):
+        cost = 0.13 + POOL * o[0].shape[1] * CYC
         if fl:
-            run("g", lambda: g.iota(o[0], pat, base, cm, allow_small_or_imprecise_dtypes=True), o, [])
+            run("g", lambda: g.iota(o[0], pat, base, cm, allow_small_or_imprecise_dtypes=True), o, [], cost=cost, solo=solo)
         else:
-            run("g", lambda: g.iota(o[0], pat, base, cm), o, [])
+            run("g", lambda: g.iota(o[0], pat, base, cm), o, [], cost=cost)
 
-    def asel(o, i, pat, op, base, cm, fill=0.0):
-        run("g", lambda: g.affine_select(o[0], i[0], pat, op, fill, base, cm), o, [i])
+    def asel(o, i, pat, op, base, cm, fill=0.0, solo=False):
+        run("g", lambda: g.affine_select(o[0], i[0], pat, op, fill, base, cm), o, [i], cost=0.17 + POOL * o[0].shape[1] * CYC, solo=solo)
 
-    def dma(q, o, i, keep=False):
-        order(q, i[1], [] if keep else o[1], True)
-        sem = "d%d" % nd[0]
-        nd[0] += 1
-        Q[q].dma_start(o[0], i[0]).then_inc(T.sem[sem], 16)
-        cnt[sem] = 16
-        note("dma", sem, 16, i[1], [])
-        for (nm, lo, hi) in o[1]:
-            hist.setdefault(nm, []).append(("dma", sem, 16, lo, hi, True))
+    def dma(q, o, i, keep=False, lag=2.5, after=()):
+        record(q, lambda: Q[q].dma_start(o[0], i[0]), list(i[1]) + list(after), list(o[1]), 0.1, lag, "dma", keep=keep, heavy=True)
+
+    def plan():
+        seen, preds, lastq = {}, [], {}
+        for n, c in enumerate(calls):
+            ps = {}
+            for rs, wr in ((c["r"], False), (c["w"], True)):
+                for (nm, lo, hi) in rs:
+                    h = seen.setdefault(nm, [])
+                    for (m, l2, h2, w2) in h:
+                        if m != n and (nm in PSUM or ((wr or w2) and l2 < hi and lo < h2 and not (c.get("keep") and calls[m].get("keep")))):
+                            same = calls[m]["q"] == c["q"] and calls[m]["kind"] == "c"
+                            ps[m] = calls[m]["lag"] if not same else NEXT if c["q"] != "p" or c.get("fence") else 0.0
+                    if nm in PSUM or wr and not c.get("keep"):
+                        h[:] = [e for e in h if not (nm in PSUM or lo <= e[1] and e[2] <= hi)]
+                    h.append((n, lo, hi, wr))
+            if c.get("heavy"):
+                if c["q"] in lastq:
+                    ps.setdefault(lastq[c["q"]], 0.0)
+                lastq[c["q"]] = n
+            preds.append(ps)
+        succs = [{} for c in calls]
+        for n in range(len(calls)):
+            for m in preds[n]:
+                succs[m][n] = preds[n][m]
+        tail = [c["lag"] if c["kind"] == "dma" else 0.0 for c in calls]
+
+        def place(turn, before, head, forward):
+            busy, first, end = {q: [] for q in Q}, {}, {}
+            for n in turn:
+                c = calls[n]
+                at = max([end[m] + before[n][m] for m in before[n]] + [head[n]])
+                for (a, b) in busy[c["q"]]:
+                    if at + c["cost"] <= a:
+                        break
+                    at = max(at, b)
+                first[n], end[n] = at, at + c["cost"]
+                ahead, behind = (GUARD, c["hold"]) if c["kind"] == "send" else (0.0, 0.0)
+                busy[c["q"]].append((at - ahead, end[n] + behind) if forward else (at - behind, end[n] + ahead))
+                busy[c["q"]].sort()
+            return first, end
+
+        late = [max(tail[n], c["due"]) for n, c in enumerate(calls)]
+        way = list(late)
+        for n in reversed(range(len(calls))):
+            way[n] += calls[n]["cost"]
+            for m in preds[n]:
+                way[m] = max(way[m], way[n] + preds[n][m])
+        best = None
+        for sweep in range(SWEEPS):
+            first, end = place(sorted(range(len(calls)), key=lambda n: (-way[n], n)), preds, [0.0] * len(calls), True)
+            span = max(end[n] + tail[n] for n in end)
+            if best is None or span < best:
+                best, start = span, first
+            way = place(sorted(range(len(calls)), key=lambda n: (-end[n], -n)), succs, late, False)[1]
+        return start
+
+    def issue(start):
+        solo, lastp = False, {}
+        for n in sorted(range(len(calls)), key=lambda n: (start[n], n)):
+            c = calls[n]
+            q = c["q"]
+            reads, writes = ([x for x in rs if x[0] in SCRATCH] for rs in (c["r"], c["w"]))
+            for (nm, lo, hi) in c["r"]:
+                if nm not in SCRATCH:
+                    wait(q, nm, N - 1)
+            if c["kind"] == "dma":
+                order(q, reads, writes, True, c["keep"])
+                sem = "d%d" % nd[0]
+                nd[0] += 1
+                c["fn"]().then_inc(T.sem[sem], 16)
+                cnt[sem] = 16
+                note("dma", sem, 16, reads, [])
+                for (nm, lo, hi) in writes:
+                    hist.setdefault(nm, []).append(("dma", sem, 16, lo, hi, True))
+                continue
+            if q == "g":
+                if solo or c.get("solo"):
+                    wait("g", "sg", cnt["sg"])
+                solo = c.get("solo")
+            order(q, reads, writes)
+            if c["kind"] == "send":
+                c["fn"]()
+                cnt["sent"] += N - 1
+                continue
+            if c.get("fence"):
+                wait("p", "sp", lastp[writes[0][0]])
+            for fn in (c["fn"] if q == "p" else [c["fn"]]):
+                fn().then_inc(T.sem[SEM[q]], 1)
+                cnt[SEM[q]] += 1
+            if q == "p":
+                lastp[writes[0][0]] = cnt["sp"]
+            note(q, SEM[q], cnt[SEM[q]], reads, writes)
 
     def H(ap):
         return (ap, [])
 
-    def wrap(o, Z, name, lo, n):
-        mm(o, [(A(Z, 15 - p, 143 - p), A(name, lo + p, lo + 16 * n, 16)) for p in range(16)])
+    def wrap(o, Z, name, lo, n, stop=True):
+        mm(o, [(A(Z, 15 - p, 143 - p), A(name, lo + p, lo + 16 * n, 16)) for p in range(16)], True, stop)
 
     def K(j):
         return A("K", j, j + 1)
@@ -176,28 +298,33 @@ def rank_program(g, core, T, topo):
     def O(r):
         return A("O", r, r + 1)
 
-    def zero(nm, d):
-        lo = (d + (EB if nm == "AE" else 0)) * PW - 16
-        dma("s", A(nm, lo, lo + 800), A("ZR"))
+    def plane(o, d):
+        t = 0 if d == 4 else 1 + d % 2
+        nm, lo, hi, unit = TABLE[t][o]
+        return nm, lo + unit * (d + (4 >> t) * (1 - 2 * o))
+
+    def zero(o, d, after=()):
+        nm, c = plane(o, d)
+        dma("s", A(nm, c - 16 + 16 * o, c + 784), A("ZR", 0, 800 - 16 * o), lag=6.0, after=after)
 
     dma("a", A("EL", 0, 48), H(T.e0[:, :]))
     dma("s", A("EL", 48, 96), H(T.h0[:, :]))
     for h in range(2):
         dma("as"[h], A("WL", 128 * h, 128 * h + 128), H(T.w0[h::2, :]))
-    dma("a", A("VB", 0, S0), H(T.v0[:, :]))
+    dma("a", A("VB", 0, L), H(T.v0[:, 0:L]))
     for j in range(2):
-        dma("sa"[j], A("XB", 2048 * j, 2048 * j + 2048), H(T.x0[:, 2048 * j:2048 * j + 2048]))
-    dma("s", A("TH", 0, 3), H(T.th[:, :]))
+        dma("sa"[j], A("XB", 2048 * j, 2048 * j + 2048), H(T.x0[:, 2048 * j:2048 * j + 2048]), lag=XLAG + j)
+    dma("a", A("VB", L, S0), H(T.v0[:, L:S0]), lag=XLAG + 2)
 
     iota(A("PI", 0, 1), [[0, 1]], 0, 1, False)
     iota(A("IO"), [[1, 144]])
     iota(A("KI", 0, 16), [[16, 8], [128, 2]], 0, 0, False)
     iota(A("KI", 16, 32), [[2, 16]], 0, 0, False)
-    iota(A("KI", 32, 40), [[24, 8]], 23, 0, False)
+    iota(A("KI", 32, 40), [[KW, 8]], KW - 1, 0, False)
     iota(A("KI", 40, 48), [[1, 8]], 0, 0, False)
     iota(A("I8"), [[1, 16], [0, 8]])
     iota(A("IM"), [[0, 8], [1, 16]])
-    ms(A("ST", 0, S0), 0.0)
+    ms(A("ST", 0, YC), 0.0)
     ms(A("ON"), 1.0)
     ms(A("AC"), 0.0)
     p_ = A("PI", 0, 1)
@@ -208,497 +335,456 @@ def rank_program(g, core, T, topo):
     ts(A("PJ", 4, 5), p_, 7, OP.bitwise_and)
     ts(A("PJ", 5, 6), p_, 3, OP.logical_shift_right, 1, OP.bitwise_and)
     ts(A("PJ", 6, 7), p_, 127, OP.bitwise_and)
+    ts(A("PJ", 7, 8), p_, 4, OP.logical_shift_right, 1, OP.bitwise_and)
     cp(A("K", 0, 7), A("PJ", 0, 7))
     kR, kG, kS, kQ, k7, kH, kP = [K(j) for j in range(7)]
     ts(K(30), kR, 2.0, OP.is_equal, 8.0, OP.mult)
-    ts(K(7), k7, 32.0, OP.mult, kH, OP.add)
+    ts(A("NP", 192, 240), A("ON", 0, 48), kR, OP.mult, 1.5, OP.mult)
+    act(A("ST", 0, S0), A("ST", 0, S0), bias=K(30))
+    cp(A("NP", 240, 288), A("IO", 0, 48))
+    lin(K(7), k7, 32.0, kH)
     ts(A("O"), A("IO", 0, 16), kR, OP.is_equal)
     ts(A("K", 18, 22), A("IO", 0, 4), kS, OP.is_equal)
     ts(A("K", 22, 26), A("IO", 0, 4), kQ, OP.is_equal)
-    ts(A("CM", 0, 8), A("IO", 0, 8), kG, OP.is_equal)
-    ts(K(35), kG, 16.0, OP.mult, 15.0, OP.add)
-    ts(K(26), K(18), 32.0, OP.mult, K(19), OP.add)
-    ts(K(50), kQ, 2.0, OP.is_lt, K(21), OP.is_gt)
+    ts(A("CM"), A("IO", 0, 8), kG, OP.is_equal)
+    lin(K(35), kG, 16.0, 15.0)
+    lin(K(26), K(18), 32.0, K(19))
     ts(A("Z0"), A("IO"), K(35), OP.is_equal)
-    act(K(8), kR, scale=2.0, bias=1.0)
-    act(K(9), kG, scale=2.0)
-    act(K(10), kG, scale=2.0, bias=1.0)
-    act(A("ST", 0, S0), A("ST", 0, S0), bias=K(30))
-    act(K(17), kR, scale=1.5)
+    due[0] = EARLY + 1.0
+    lia(K(8), kR, 2.0, 1.0)
+    lia(K(9), kG, 2.0)
+    lia(K(10), kG, 2.0, 1.0)
     act(A("K", 11, 14), A("IO", 0, 24, 8), bias=k7)
-    act(A("NP", 240, 288), A("IO", 0, 48))
-    act(A("NP", 192, 240), A("IO", 0, 48), scale=0.0, bias=K(17))
+    lia(K(31), kP, 8.0)
     act(A("K", 14, 17), A("K", 11, 14), AF.Square, bias=0.5)
+    lia(K(52), kQ, 8.0, kG)
     act(A("K", 14, 17), A("K", 14, 17), bias=0.75)
-    ts(A("KI", 0, 16), A("KI", 0, 16), kR, OP.add)
-    ts(A("KI", 16, 32), A("KI", 16, 32), K(7), OP.add)
-    ts(A("LH0"), A("I8"), K(9), OP.is_equal, K(8), OP.mult)
-    cp(A("KO"), A("KI"))
-    ts(A("LH1"), A("I8"), K(10), OP.is_equal, K(8), OP.mult)
+    due[0] = 0.0
     ts(A("E1", 0, 96), A("EL"), 5, OP.logical_shift_right)
     ts(A("E1", 96, 192), A("EL"), 31, OP.bitwise_and)
     cp(A("NP", 0, 192), A("E1"))
+    ts(A("KI", 0, 16), A("KI", 0, 16), kR, OP.add)
+    ts(A("KI", 16, 32), A("KI", 16, 32), K(7), OP.add)
+    cp(A("KO"), A("KI"))
     cp(A("W1"), IND(A("WL"), A("KO", 0, 16)))
-    for q in "as":
-        order(q, [], [("ST", 0, S0)], True)
     for j, row, q in ((4, 8, "s"), (5, 9, "s"), (0, 0, "a"), (1, 4, "s"), (2, 1, "a"), (3, 5, "s")):
         dma(q, A("ST", 0, S0, p=(row, 128, 16)), A("NP", 48 * j, 48 * j + 48), True)
+    dma("s", A("TH", 0, 3), H(T.th[:, :]))
     run("v", lambda: g.vector.transpose(T.W2[:, :], T.W1[:, :]), A("W2"), [A("W1")])
-    ts(A("DM"), A("IM"), kR, OP.is_equal)
+    ts(A("LH0"), A("I8"), K(9), OP.is_equal, K(8), OP.mult)
+    ts(A("LH1"), A("I8"), K(10), OP.is_equal, K(8), OP.mult)
     cp(A("WO"), IND(A("W2"), A("KO", 16, 32)))
 
     def offsets(t):
-        yb = "G2" if t else "VB"
-        mm(A("PE", 0, 64), [(A("LH0"), A(yb, 0, L, 2)), (A("LH1"), A(yb, 1, L, 2))])
-        steps = [lambda: cp(A("U1"), A("PE", 0, 64)),
-                 lambda: ts(A("U"), A("U1"), 4095, OP.bitwise_and),
-                 lambda: tt(A("UU"), A("U"), A("U"), OP.mult)]
+        y0 = YC if t else 0
+        mm(A("PE", 0, 64), [(A("LH0"), A("VB", y0, y0 + L, 2)), (A("LH1"), A("VB", y0 + 1, y0 + L, 2))])
+        cp(A("U1"), A("PE", 0, 64))
+        ts(A("U"), A("U1"), 4095, OP.bitwise_and)
+        tt(A("UU"), A("U"), A("U"), OP.mult)
         for m in range(3):
-            steps.append(lambda m=m: ts(A("UA", 64 * m, 64 * m + 64), A("U"), K(14 + m), OP.mult, A("AC", 0, 1), OP.add))
-        steps.append(lambda: ts(A("UB"), A("UU"), 5, OP.logical_shift_right))
+            lin(A("UA", 64 * m, 64 * m + 64), A("U"), K(14 + m), A("AC", 0, 1))
+        ts(A("UB"), A("UU"), 5, OP.logical_shift_right)
         for m in range(3):
-            steps.append(lambda m=m: tt(A("UC", 64 * m, 64 * m + 64), A("UA", 64 * m, 64 * m + 64), A("UB"), OP.add))
-        steps.append(lambda: ts(A("UA"), A("UC"), 4095, OP.bitwise_and))
-        steps.append(lambda: cp(A("AO"), A("UA")))
-        return steps
+            tt(A("UC", 64 * m, 64 * m + 64), A("UA", 64 * m, 64 * m + 64), A("UB"), OP.add)
+        ts(A("UA"), A("UC"), 4095, OP.bitwise_and)
+        cp(A("AO"), A("UA"))
+        calls[-1]["heavy"] = True
 
-    steps = offsets(0)
-    for s in steps:
-        s()
-    act(K(27), K(21), bias=K(26))
-    act(K(28), K(20), scale=float(PW), bias=K(26))
-    act(K(29), K(20), scale=-0.125, bias=K(26))
-    act(A("K", 36, 40), A("K", 22, 26), scale=K(27))
-    act(A("K", 40, 44), A("K", 22, 26), scale=K(28))
-    act(A("K", 44, 48), A("K", 22, 26), scale=K(29))
-    act(K(48), K(38), scale=1.0 / 2048)
-    act(K(31), kP, scale=8.0)
-    act(A("ZS"), A("Z0"), scale=K(38))
-    act(A("FEH", 0, 8), A("CM", 0, 8), scale=K(44))
-    act(A("FEH", 8, 16), A("CM", 0, 8), scale=K(45))
-    act(K(52), kQ, scale=8.0, bias=kG)
-    act(K(54), K(29), scale=-1.0)
-    act(A("FV"), A("CM", 0, 8), scale=K(48))
-    act(A("G8"), A("CM", 0, 8), scale=-8192.0)
-    asel(A("ID"), A("ON"), [[-1, 128]], OP.is_equal, 0, 1)
-    iota(A("IN"), [[0, 128]], -1)
-    asel(A("IN"), A("IN"), [[-1, 128]], OP.is_equal, 0, 1)
-    iota(A("I24"), [[1, 16], [0, 24]])
-    iota(A("RK"), [[0, 192]])
-    iota(A("VB", S0, YC), [[0, YC - S0]])
-    iota(A("ST", S0, DUM), [[0, DUM - S0]])
-    iota(A("RK", p=(0, 1)), [[0, 8], [1024, 3], [0, 8]])
-    wait("g", "sg", cnt["sg"])
-    iota(A("RK", p=(32, 33)), [[0, 24], [1, 8]])
-    wait("g", "sg", cnt["sg"])
-    iota(A("ZR"), [[0, 800]])
+    due[0] = EARLY
+    lia(K(29), K(20), -0.125, K(26))
+    lia(A("K", 36, 40), A("K", 22, 26), K(26))
+    lia(A("K", 44, 48), A("K", 22, 26), K(29))
+    lia(K(54), K(29), -1.0)
+    lia(K(48), K(38), 1.0 / 4096)
+    lia(A("ZS"), A("Z0"), K(38))
+    lia(A("FEH", 0, 8), A("CM"), K(44))
+    lia(A("FEH", 8, 16), A("CM"), K(45))
+    lia(A("FV"), A("CM"), K(48))
+    due[0] = 0.0
+    rk = [A("RK", 200 * j, 200 * j + 200, p=(0, 1)) for j in range(4)]
+    iota(A("RK", 0, 600, p=(0, 1)), [[0, 600]])
+    iota(rk[3], [[0, 8], [-1, KW]], KW - 1)
+    asel(rk[0], rk[0], [[0, 8], [1, KW]], OP.is_ge, -17, 0, 1016.0)
+    iota(A("OI", p=(0, 1)), [[1, 128]])
+    asel(rk[0], rk[0], [[0, 8], [1, KW]], OP.is_ge, -9, 0, 2032.0)
+    for j, c in ((1, 1 / 4096), (2, -2.0 ** 19), (3, GM - 3072 + YC / 4096), (0, 3072.0)):
+        o = A("RK", 200 * j, 200 * j + 200, KW, p=(0, 1))
+        asel(o, o, [[0, 8]], OP.is_gt, 0, 0, c)
+    iota(A("I24"), [[1, 16], [0, KW]])
+    lia(A("VB", S0, YC), A("ST", S0, YC), 0.0)
+
+    def diag(name, c):
+        n = T[name].shape[1]
+        asel(A(name), A("ST", S0, S0 + n), [[-1, n]], OP.not_equal, 0, 1, c)
+
+    ID = A("ID", 0, 128)
+    diag("ID", 1.0)
     iota(A("SEG"), [[0, 128], [256, 8]])
-    iota(A("BOF"), [[0, 128]], 1)
-    asel(A("BOF"), A("BOF"), [[-16, 8], [0, 16]], OP.is_ge, 0, 1)
-    asel(A("BOF"), A("BOF"), [[16, 8], [0, 16]], OP.is_ge, 15, -1)
-    iota(A("DFL"), [[0, 192]])
+    diag("IN", -1.0)
+    iota(A("ZR"), [[0, 800]])
+    diag("NI", -2032.0)
     iota(A("PL", 8, 16), [[0, 8]])
-    iota(A("DL", 0, 8), [[0, 8]], DUM, 1)
-    iota(A("DL", 8, 16), [[0, 8]], 2048 * 3072 + YC, 2049)
+    asel(A("BO"), A("ON"), [[-16, 8], [0, 16]], OP.is_ge, 0, 1)
+    asel(A("LD"), A("ST", S0, S0 + 128), [[-16, 8], [0, 16]], OP.not_equal, -11, 1, -100.0)
+    asel(A("BO"), A("BO"), [[16, 8], [0, 16]], OP.is_ge, 15, -1)
+    asel(A("DD"), A("IN"), [[0, 8], [1, 16]], OP.is_ge, -8, 0)
+    asel(A("DG"), ID, [[0, 8], [-1, 16]], OP.is_ge, 6, 0)
+    asel(A("DG"), A("DG"), [[0, 8], [1, 16]], OP.not_equal, -3, 0)
+    diag("HI", 4096.0)
     asel(A("TRI"), A("ON"), [[-1, 128]], OP.is_ge, 0, 1)
-    iota(A("SCM"), [[0, 784]], 1)
-    for d in (4, 2, 6):
-        zero("AE", d)
-        zero("AH", d)
+    for o in range(2):
+        zero(o, 4)
 
-    def consts_a():
-        act(A("LN", 0, 8), A("IO", 0, 128, 16), bias=kR)
-        act(A("LN", 8, 16), A("LN", 0, 8), scale=32.0)
-        act(A("LN", 16, 24), A("LN", 0, 8), bias=float(DUM))
-        act(K(55), O(0), scale=4096.0)
-        act(A("THF", 0, 3), A("TH", 0, 3))
-        act(K(49), O(11), scale=-100.0)
-        act(K(51), K(24), scale=-1.0)
-        act(K(53), O(1), bias=O(5))
-        act(K(56), O(2), scale=12.0, bias=O(11))
-        act(K(58), O(2), scale=-1.0, bias=O(6))
-        act(K(59), O(8), scale=24.0, bias=O(3))
-        act(K(56), O(6), scale=8.0, bias=K(56))
-        for t in range(NT):
-            act(K(61 + t), K(58), scale=float(4 >> t), bias=K(59))
+    def consts_first():
+        lin(A("G8"), A("CM"), -8192.0)
+        lin(A("FS"), A("CM"), K(38))
+        ts(K(32), kP, float(DUM), OP.add)
+        cp(A("VB", YC, VW), A("VB", 0, L))
+
+    def consts_leaders():
+        ts(K(53), O(1), O(5), OP.add)
+        lin(K(56), O(2), 12.0, O(11))
+        lin(K(58), O(2), -1.0, O(6))
+        lin(K(59), O(8), 24.0, O(3))
+        lin(K(56), O(6), 8.0, K(56))
+        lin(K(28), K(20), 256.0, K(26))
+        lin(K(61), K(58), 4.0, K(59))
+        lin(K(40), K(22), K(28))
+        lin(K(33), O(0), 128.0)
+        ts(A("LN", 0, 8), A("IO", 0, 128, 16), kR, OP.add)
+        lia(A("ST", DUM, YC), A("IO", 0, 128), K(53), K(56))
+        lin(A("LN", 8, 16), A("LN", 0, 8), 32.0)
+        ts(A("LN", 16, 24), A("LN", 0, 8), float(DUM), OP.add)
+        lia(A("ZM"), A("Z0"), K(8))
+        lin(A("CT", 0, 128), A("IO", 0, 128), O(9), K(61))
+        lia(A("Z8"), A("ZM"), 8.0)
+        lin(A("ZE"), A("Z0"), K(40))
+
+    def consts_rounds():
+        lin(K(34), K(38), K(60))
         for t in range(1, NT):
-            act(K(61 + t), O(8), scale=4.0 * t, bias=K(61 + t))
-        act(A("FS"), A("CM", 0, 8), scale=K(38))
-        act(A("CM", 8, 16), A("CM", 0, 8), scale=2048.0)
+            lin(K(61 + t), K(58), float(4 >> t), K(59))
+        lin(K(55), K(34), -1.0, K(38))
+        for t in range(1, NT):
+            lin(K(61 + t), O(8), 4.0 * t, K(61 + t))
+        for j, (k, w) in enumerate(((55, 1.0), (34, 1.0), (55, -1.0), (34, -1.0))):
+            ts(A("SEL", 128 * j, 128 * j + 128), A("ON"), K(k), OP.mult, w, OP.mult)
 
-    def consts_a1():
-        act(A("DFL", 0, 192, 24), A("DL", 8, 16), scale=1.0 / 2048)
-        act(A("VB", YC, VW), A("VB", 0, L))
-        act(A("NI"), A("ID"), scale=-2048.0)
-        act(A("ST", DUM, YC), A("IO", 0, 128), scale=K(53), bias=K(56))
-        act(A("ZM"), A("Z0"), scale=K(8))
-        act(A("Z8"), A("ZM"), scale=8.0)
-        act(A("CT", 0, 128), A("IO", 0, 128), scale=O(9), bias=K(61))
-        act(A("DD"), A("ID"), scale=K(51))
+    def consts_masks():
+        ts(K(12), O(7), O(15), OP.add)
+        lin(K(10), kH, -1.0, 1.0)
+        lin(K(9), K(12), 2.0, -1.0)
+        lin(K(17), K(12), 8.0, 99.0)
+        lin(K(10), K(10), K(9))
+        lin(K(17), k7, -1.0, K(17))
+        lin(K(9), kH, K(9))
 
-    def consts_a2():
-        act(A("BO"), A("BOF"))
-        act(A("LD"), A("BOF"), scale=K(49))
-        act(A("DG"), A("ID"), scale=K(50))
-
-    def consts_a6():
-        act(A("ZE"), A("Z0"), scale=K(40))
-        act(A("ZH"), A("Z0"), scale=K(41))
-        act(A("Z4"), A("Z0"), scale=K(55))
-
-    def consts_a4():
-        act(A("CM", 16, 24), A("CM", 0, 8), scale=K(38))
-        act(A("HI"), A("ID"), scale=4096.0)
-        for gg in range(8):
-            act(A("SEL", 128 * gg, 128 * gg + 128), A("ON"), scale=A("CM", 16 + gg, 17 + gg))
-
-    def consts_a5():
-        act(A("B0", 128, 256), A("BO"), scale=O(0))
-        act(K(12), O(7), bias=O(15))
-        act(A("ZP"), A("Z0"), scale=K(36))
-        act(A("ZQ"), A("Z0"), scale=K(37))
+    def consts_places():
+        for nm, ws in (("ZP", ((0, 32.0), (1, 1.0), (3, 1.0))), ("ZQ", ((4, 32.0), (5, 1.0)))):
+            iota(A(nm), [[0, 144]])
+            for r, w in ws:
+                asel(A(nm, 15, 144, 16), A(nm, 15, 144, 16), [[-16, 9]], OP.not_equal, -r, 1, w)
+        asel(A("ZF"), A("ZE"), [[0, 144]], OP.is_equal, 0, 0)
+        asel(A("ZF", 15, 144, 16), A("ZF", 15, 144, 16), [[-16, 9]], OP.not_equal, -2, 1, 512.0)
+        asel(A("HN"), A("ZR", 0, 128), [[-1, 128]], OP.not_equal, 0, 1, -100.0)
+        asel(A("B7"), A("ON"), [[0, 16], [1, 8]], OP.not_equal, -7, 0)
+        for o in range(2):
+            asel(A("LO", 128 * o, 128 * o + 128), A("B7"), [[-16, 8], [0, 16]], OP.is_equal, -2 - 4 * o, 1)
+        asel(A("B0", 128, 256), A("ON"), [[-16, 8], [0, 16]], OP.is_equal, 0, 1)
+        asel(A("B0", 0, 128), A("B0", 128, 256), [[0, 8], [-1, 16]], OP.is_ge, 7, 0)
 
     def build(j, q):
         o, i = A("IA", 512 * j, 512 * j + 512), IND(A("ST", 0, S0), A("WO", 32 * j, 32 * j + 32))
         (act if q == "a" else cp)(o, i)
 
-    consts_a()
-    for j in range(8):
-        build(j, "aavavava"[j])
-    act(A("ST", YC, VW), A("ST", 0, L))
+    consts_first()
+    offsets(0)
+    ts(A("DM"), A("IM"), kR, OP.is_equal)
+    cp(K(60), A("PJ", 7, 8))
     ts(A("FEN"), A("I24"), K(52), OP.is_equal, K(54), OP.mult)
+    for j in range(8):
+        build(j, BUILD[j])
+    cp(A("ST", YC, VW), A("ST", 0, L))
 
     peers = [T.cores[(rank - d) % N] for d in range(1, N)]
     SB = ("P4", "P5", "P4")
+    one = A("ON", p=(0, 1))
 
     def gx(lo, hi, q):
         (act if q == "a" else cp)(A("GX", 16 * lo, 16 * hi), IND(A("XB"), A("AO", lo, hi)))
 
-    def gi(m, q="a"):
-        (act if q == "a" else cp)(A("GI", 1024 * m, 1024 * m + 1024), IND(A("IA"), A("AO", 64 * m, 64 * m + 64)))
+    def gi(m):
+        act(A("GB", 1024 * m, 1024 * m + 1024), IND(A("IA"), A("AO", 64 * m, 64 * m + 64)))
         if m == 0:
-            mm(A("PE", 0, 384), [(A("ST", YC, VW), A("FEN"))], True, False)
-            mm(A("PV", 0, 192), [(A("ON", p=(0, 33)), A("RK", p=(0, 33)))], True, False)
-            opened = cnt["sp"]
-        wrap(A(SB[m], 0, 64), "ZS", "GI", 1024 * m, 64)
-        if m == 0:
-            wait("p", "sp", opened)
+            mm(A("PE", 0, 16 * KW), [(A("ST", YC, VW), A("FEN"))], True, False)
+            mm(A("PV", 0, 8 * KW), [(one, rk[0]), (one, rk[3]), (A("OI", p=(0, 1)), rk[1])], True, False)
+        wrap(A(SB[m], 0, 64), "ZS", "GB", 1024 * m, 64)
         for kk in range(8):
             k = 8 * m + kk
-            l = A("GI", 1024 * m + kk, 1024 * m + 1024, 8)
-            mm(A("PE", k, 384, 24), [(l, A("FEH"))], False, k == 23)
-            mm(A("PV", k, 192, 24), [(l, A("FV"))], False, k == 23)
+            l = A("GB", 1024 * m + kk, 1024 * m + 1024, 8)
+            mm(A("PE", KW - 1 - k, 16 * KW, KW), [(l, A("FEH"))], False, k == 23, k == 0)
+            mm(A("PV", KW - 1 - k, 8 * KW, KW), [(l, A("FV"))], False, k == 23, k == 0)
 
     def sl(m):
         cp(A("SL", 64 * m, 64 * m + 64), A(SB[m], 0, 64))
+        calls[-1]["heavy"] = True
 
-    def gv(m):
-        lo, hi = 1024 * m, 1024 * m + 1024
-        tt(A("BT", lo, hi), IND(A("VB", 0, 1152), A("SL", 64 * m, 64 * m + 64)), A("GX", lo, hi), OP.is_gt)
+    def gv(m, c0=0, c1=64):
+        lo, hi = 64 * m + c0, 64 * m + c1
+        tt(A("GB", BT + 16 * lo, BT + 16 * hi), IND(A("VB", 0, 1152), A("SL", lo, hi)), A("GX", 16 * lo, 16 * hi), OP.is_gt)
 
     def mx(m):
-        scan(A("MS", 1024 * m, 1024 * m + 1024), A("SEG"), A("GX", 1024 * m, 1024 * m + 1024), OP.min, OP.max)
+        o = A("GB", MS + 1024 * m, MS + 1024 * m + 1024) if m < 2 else A("GX", GM - 7, GM + 1017)
+        scan(o, A("SEG"), A("GX", 1024 * m, 1024 * m + 1024), OP.min, OP.max)
 
     def count(m):
+        if m == 0:
+            mm(A("P5", 0, 8 * KW), [(one, rk[2])], True, False)
         for kk in range(8):
             k = 8 * m + kk
-            if k == 0:
-                mm(A("P5", 0, 192), [(A("ID"), A("NPB"))], True, False)
-                wait("p", "sp", cnt["sp"])
-            mm(A("P5", k, 192, 24), [(A("BT", 1024 * m + kk, 1024 * m + 1024, 8), A("G8"))], False, k == 23)
+            mm(A("P5", KW - 1 - k, 8 * KW, KW), [(A("GB", BT + 1024 * m + kk, BT + 1024 * m + 1024, 8), A("G8"))], False, k == 23, k in (0, 16))
 
     def parallel():
-        act(A("SG"), A("PE", 0, 384), AF.Sign, bias=0.0625)
-        mm(A("P4", 256, 448), [(A("ID"), A("SG", 0, 192)), (A("ID"), A("SG", 192, 384))])
-        act(A("VL"), A("PV", 0, 192), bias=K(31))
-        act(A("NPB"), A("P4", 256, 448), AF.Abs, scale=28.0 * 4096, bias=23.0 * 4096)
+        act(A("SG"), A("PE", 0, 16 * KW), AF.Sign, bias=0.0625)
+        mm(A("P4", 256, 256 + 8 * KW), [(ID, A("SG", 0, 8 * KW)), (ID, A("SG", 8 * KW, 16 * KW))])
+        act(A("VL"), A("PV", 0, 8 * KW), bias=K(31))
+        act(A("NPB"), A("P4", 256, 256 + 8 * KW), AF.Abs, scale=29.0 * 4096, bias=93.0 * 1024)
+        calls[-1]["heavy"] = True
 
     def fold(ds, start, stop, first=()):
-        prs = list(first) + [(A("FL", 128 * (7 * o + d - 1), 128 * (7 * o + d)), ("AE", "AH")[o], (d + EB * (1 - o)) * PW - 1 + o) for (o, d) in ds]
-        mm(A("P0"), [(l, A(nm, c0, c0 + 512)) for (l, nm, c0) in prs], start, stop)
-        mm(A("P1", 0, 257), [(l, A(nm, c0 + 512, c0 + 769)) for (l, nm, c0) in prs], start, stop)
+        prs = list(first) + [(A("FL", 128 * (7 * o + d - 1), 128 * (7 * o + d)), plane(o, d)[0], plane(o, d)[1] - 1 + o) for (o, d) in ds]
+        for n, (l, nm, c0) in enumerate(prs):
+            mm(A("P0"), [(l, A(nm, c0, c0 + 512))], start and n == 0, stop and n == len(prs) - 1)
+            mm(A("P1", 0, 257), [(l, A(nm, c0 + 512, c0 + 769))], start and n == 0, stop and n == len(prs) - 1)
 
-    def slots(t, bank):
-        cp(A("SO", 48, 64), A(bank, 256, 272))
-        if t == 0:
-            return
-        cp(A("S2", 0, 16), A(bank, 256, 272))
-        ts(A("S2", 16, 32), A("S2", 0, 16), PW - 1, OP.bitwise_and)
-        ts(A("PO", 48 + 8 * t, 56 + 8 * t), A("S2", 16, 24), 1.0, OP.add)
-        cp(A("PO", 120 + 8 * t, 128 + 8 * t), A("S2", 24, 32))
+    def places():
+        ts(A("S2", 32, 64), A("S2", 0, 32), PW - 1, OP.bitwise_and)
+        for t in range(1, NT):
+            ts(A("PO", 48 + 8 * t, 56 + 8 * t), A("S2", 16 + 16 * t, 24 + 16 * t), 1.0, OP.add)
+            cp(A("PO", 120 + 8 * t, 128 + 8 * t), A("S2", 24 + 16 * t, 32 + 16 * t))
 
     def flags(t, o):
-        lo = (EB - (4 >> t)) * PW if o == 0 else (4 >> t) * PW
-        cp(IND(A(("AE", "AH")[o], lo), A("SO", 48 + 8 * o, 56 + 8 * o)), A("SP", 128 * t, 128 * t + 128))
+        nm, lo, hi, unit = TABLE[t][o]
+        cp(IND(A(nm, lo, hi), A("SO", 48 + 8 * o, 56 + 8 * o)), A("SP", 128 * t, 128 * t + 128))
 
-    def masks(lo, hi):
+    def masks(lo, hi, bank):
+        ps = [A(bank, 256 * o, 256 * o + hi - lo) for o in range(2)]
         for o in range(2):
-            mm(A("P5", 256 * o, 256 * o + hi - lo), [(A("LO", 128 * o, 128 * o + 128), A("ST", S0 + lo, S0 + hi)), (A("HN"), A("SP", lo, hi))])
+            mm(ps[o], [(A("LO", 128 * o, 128 * o + 128), A("ST", S0 + lo, S0 + hi)), (A("HN"), A("SP", lo, hi))])
         for o in range(2):
-            ts(A("MM", 384 * o + lo, 384 * o + hi), A("P5", 256 * o, 256 * o + hi - lo), K(17), OP.is_equal, K(10 - o), OP.mult)
-
-    def consts_a3():
-        act(K(9), K(12), scale=2.0, bias=-1.0)
-        act(K(10), kH, scale=-1.0, bias=1.0)
-        act(K(17), K(12), scale=-8.0, bias=k7)
-        act(K(10), K(10), scale=K(9))
-        act(K(9), kH, scale=K(9))
-        act(K(17), K(17), bias=-99.0)
-        act(A("LO", 0, 128), A("B7"), scale=O(2))
-        act(A("LO", 128, 256), A("B7"), scale=O(6))
-        act(A("HN"), A("ID"), scale=-100.0)
+            act(A("MA", 384 * o + lo, 384 * o + hi), ps[o], AF.Abs, bias=K(17))
+            act(A("MM", 384 * o + lo, 384 * o + hi), A("MA", 384 * o + lo, 384 * o + hi), AF.Relu, bias=1.0, scale=-1.0)
 
     def flmat(o, d):
         asel(A("FL", 128 * (7 * o + d - 1), 128 * (7 * o + d)), A("B0", 128 * o, 128 * o + 128), [[0, 8], [1, 16]], OP.is_ge, 1 - 8 * o - d, 0)
 
     for t in range(NT):
         last = t == NT - 1
-        land = "LD%d" % t
+        land, arr = "LD%d" % t, ("arr%d" % t, 0, 1)
         gi(0)
-        gx(0, 64 if t else 128, "v")
+        gx(0, 64, "v")
+        if t == 1:
+            for d in (2, 6):
+                zero(0, d, [("arr0", 0, 1)])
+                zero(1, d)
+            zero(0, 5)
+            dma("s", A("SCM", p=(7, 128, 8)), A("ON", 0, 98))
+        if t == 2:
+            for o in range(FL1, 2):
+                flags(1, o)
+        gx(64, XA[t], "v")
         sl(0)
         gi(1)
         gv(0)
-        if t:
-            gx(XA, 128, "a")
-            if XA > 64:
-                gx(64, XA, "v")
-            if not EARLY:
-                slots(t - 1, "P5")
-                flags(t - 1, 0)
-            if t == 2:
-                fold([(0, 2), (0, 6)], False, False)
-            if EARLY < 2:
-                flags(t - 1, 1)
-            if t == 2:
-                fold([(1, 2), (1, 6)], False, False)
-            else:
-                for d in (1, 3, 5, 7):
-                    zero("AH", d)
+        gx(XA[t], 128, "a")
         sl(1)
+        mx(0)
+        if t == 2:
+            fold([(0, 4), (1, 4)], True, False, [(ID, "SCM", 0)])
+        gi(2)
+        gv(1)
+        count(0)
+        count(1)
         if t == 1:
             wrap(A("P0", 0, 56), "ZP", "ST", 0, 56)
             wrap(A("P0", 56, 112), "ZQ", "ST", 0, 56)
-        gi(2)
-        gv(1)
+        if t == 2:
+            fold([(0, 2), (0, 6)], False, False)
+        gx(128, 160, "a")
+        gx(160, 192, "a")
         sl(2)
-        if t == 1:
-            cp(A("PO", 0, 56), A("P0", 0, 56))
-            cp(A("PO", 72, 128), A("P0", 56, 112))
-        xs = XS if t else XS0
-        gx(128, xs, "a")
-        mx(0)
         mx(1)
-        if xs < 192:
-            gx(xs, 192, "v")
+        gv(2, 0, 32)
         parallel()
-        ma, mb = A("MS", 7, 1024, 8), A("MS", 1031, 2048, 8)
-        mm(A("PE", 0, 128), [(A("ID"), ma), (A("IN"), mb)])
-        act(A("MT"), A("PE", 0, 128), AF.Relu)
-        gv(2)
-        count(0)
-        mm(A("PE", 128, 256), [(A("ID"), A("MT")), (A("ID"), mb)])
-        count(1)
-        act(A("MT"), A("PE", 128, 256))
+        ma, mb, mc = A("GB", MS + 7, MS + 1024, 8), A("GB", MS + 1031, MS + 2048, 8), A("GX", GM, GM + 1017, 8)
+        r1, r2 = A("MT", 0, 128), A("MT", 128, 256)
+        mm(A("PE", 0, 128), [(ID, ma), (A("IN"), mb)])
+        act(r1, A("PE", 0, 128), AF.Relu)
+        gv(2, 32, 64)
+        mm(A("P5", 0, 8 * KW), [(ID, A("NPB"))], False, False, True)
         count(2)
         mx(2)
         if t == 0:
-            consts_a1()
-            consts_a2()
-        else:
-            act(A("EA", 0, 512), A("P6"), AF.Abs)
-            act(A("EA", 512, 1024), A("P7"), AF.Abs)
-            act(A("EQ"), A("EA"), AF.Relu, bias=2048.0, scale=-2048.0)
-        tt(A("KY"), A("P5", 0, 192), A("VL"), OP.max)
-        scan(A("SC"), A("DFL"), A("KY"), OP.max, OP.min)
-        tt(A("D1"), IND(A("SC"), A("KO", 32, 40)), A("DM"), OP.mult)
-        ts(A("NR"), A("SC", 23, 192, 24), 3072.0, OP.is_ge)
-        mm(A("P4", 0, 8), [(A("D1"), A("CM", 8, 16))])
-        mm(A("P7", 0, 8), [(A("ST", YC, VW), A("FS")), (A("ON", p=(0, 1)), A("RK", 16, 24, p=(0, 1))), (A("NI"), A("NR"))], True, t == 0)
-        if t:
-            wait("p", "sp", cnt["sp"])
-            for gg in range(8):
-                mm(A("P7", gg, gg + 1), [(A("EQ", 128 * gg, 128 * gg + 128), A("NR", gg, gg + 1))], False, gg == 7)
-        if not last:
-            act(A("SR"), IND(A("SC"), A("KO", 32, 40)), AF.Sign, bias=-3071.9)
-            mm(A("PV", 0, 1), [(A("SR"), A("ON", 0, 1))])
-            act(A("AC", 0, 1), A("PV", 0, 1), bias=64.0, scale=-0.5)
+            consts_leaders()
         if t == 1:
-            fold([(0, 4), (1, 4)], True, False)
-        if t == 2:
-            fold([], False, False, [(A("ID"), "SCM", 0)])
-        tt(A("GX", 3072, 3200), A("MT"), A("MS", 2055, 3072, 8), OP.max)
-        cp(A("SI", 0, 8), A("P4", 0, 8))
-        ts(A("SI", 8, 16), A("SI", 0, 8), 11, OP.logical_shift_right)
-        ts(A("SI", 16, 24), A("SI", 0, 8), 2047, OP.bitwise_and)
-        cp(A("SO", 8, 24), A("SI", 8, 24))
+            consts_masks()
+        if last:
+            masks(0, 256, "P6")
+        mm(A("PE", 128, 256), [(ID, r1), (ID, mb)])
+        act(r2, A("PE", 128, 256))
+        if last:
+            dma("s", A("AE", 1008, 4880, p=(0, 128, 16)), A("ZR", 0, 242), lag=3.5)
+            dma("s", A("GB", 0, 3856, p=(0, 128, 16)), A("ZR", 0, 241), lag=3.5)
+        scan(A("SC"), A("P5", 0, 8 * KW), A("VL"), OP.min, OP.max)
+        tt(A("D1"), IND(A("SC"), A("KO", 32, 40)), A("DM"), OP.mult)
+        calls[-1]["heavy"] = True
+        ts(A("NR"), A("SC", KW - 1, 8 * KW, KW), 3072.0, OP.is_ge)
+        calls[-1]["heavy"] = True
+        mm(A("P4", 0, 8), [(A("D1"), A("CM"))])
+        tt(mc, mc, r2, OP.max)
+        calls[-1]["heavy"] = True
+        mm(A("P7", 0, 8), [(A("ST", YC, VW), A("FS")), (one, A("RK", 1, 9, p=(0, 1))), (A("NI"), A("NR"))], True, t == 0)
+        if t:
+            for gg in range(8):
+                mm(A("P7", gg, gg + 1), [(A("EQ", 128 * gg, 128 * gg + 128), A("NR", gg, gg + 1))], False, gg == 7, gg == 0)
+        cp(A("SI", 8, 16), A("P4", 0, 8))
+        cp(A("SO", 8, 16), A("P4", 0, 8))
+        tt(A("SF"), A("P4", 0, 8), A("SI", 8, 16), OP.subtract)
         cp(A("G1"), IND(A("GX"), A("SO", 8, 16)))
+        lin(A("SO", 16, 24), A("SF"), 4096.0)
+        ts(A("PL", 0, 8), A("P7", 0, 8), K(32), OP.min)
         tt(A(land, 0, L), IND(A("VB"), A("SO", 16, 24)), A("G1"), OP.subtract)
-        order("g", [(land, 0, L)], [])
         trs = []
         for d in range(1, N):
             dst = peers[d - 1]
             rid, pid, _ = topo.addr(dst)
             trs.append(RemoteDMATransfer(dst_ids=[DstId(rid=rid, pnc=pid)], dma_engine_mask=1 << topo.engines(core, dst)[d - 1],
-                                         remote_sem=T.sem["arr%d" % t], src=T[land][:, 0:L], dst=T[land][:, L * d:L * d + L]))
-        g.remote_dma_fused(trs, local_sem=T.sem.sent)
-        cnt["sent"] += N - 1
-        tt(A("PL", 0, 8), A("P7", 0, 8), A("DL", 0, 8), OP.min)
-        tt(A("D2"), IND(A("PL"), A("KO", 40, 48)), A("DM"), OP.mult)
-        act(A("BS"), IND(A("ST"), A("SO", 16, 24)))
-        act(A("G2"), A(land, 0, L), AF.Abs)
-        y = A("G2")
-        mm(A("P6", 256, 264), [(A("D2"), A("CM", 0, 8))])
-        steps = [] if last else offsets(t + 1)
-
-        def step(n=1):
-            for _ in range(n):
-                if steps:
-                    steps.pop(0)()
-        ts(A("WB"), y, A("THF", t, t + 1), OP.is_ge)
-        cp(A("SO", 24, 32), A("P6", 256, 264))
-        wrap(A("P4", 64, 72), "Z8", "G2", 0, 8)
-        act(A("STP"), IND(A("ST"), A("SO", 24, 32)))
-        if t == 0:
-            consts_a6()
-        step(7)
-        if last:
-            tt(A("DF"), IND(A("VB", 0, YC), A("SO", 24, 32)), y, OP.subtract)
-            cp(A("BOH"), A("BO"))
+                                         remote_sem=T.sem[arr[0]], src=T[land][:, 0:L], dst=T[land][:, L * d:L * d + L]))
+        record("g", lambda trs=trs: g.remote_dma_fused(trs, local_sem=T.sem.sent), [(land, 0, L)], [arr], 0.3, TRAVEL[t], "send", hold=HOLD[t])
+        y, stp, cur = A("VB", YC, VW), A("STP", 0, L), A("ST", YC, VW)
         ct = A("CT", 128 * t, 128 * t + 128)
         n0 = S0 + L * t
         sp = A("SP", 128 * t, 128 * t + 128)
-        mm(A("P5", 0, 128), [(A("BO"), A("WB")), (A("LD"), A("STP"))])
-        mm(A("P6", 0, 128), [(A("DG"), A("STP")), (A("ID"), ct)])
-        mm(A("P7", 0, 128), [(A("DD"), A("STP")), (A("ID"), ct)])
-        act(A("ST", n0, n0 + L), A("P6", 0, 128))
-        cp(A("SI", 32, 40), A("P4", 64, 72))
-        ts(sp, A("P5", 0, 128), 7.5, OP.is_ge)
-        ts(A("SI", 24, 32), A("SI", 32, 40), 896, OP.bitwise_and)
-        tt(A("M1"), A("P7", 0, 128), sp, OP.mult)
-        tt(A("SI", 32, 40), A("SI", 24, 32), A("LN", 0, 8), OP.add)
-        step()
-
-        def spawn_lists():
-            if last:
-                wrap(A("PE", 0, 8), "ZE", "STP", 0, 8)
-                cp(A("SO", 48, 56), A("PE", 0, 8))
-                wrap(A("PV", 8, 16), "ZH", "STP", 0, 8)
-            else:
-                bank = "PV" if EARLY else "P5"
-                wrap(A(bank, 256, 264), "ZE", "STP", 0, 8)
-                wrap(A(bank, 264, 272), "ZH", "STP", 0, 8)
+        if t == 1:
+            cp(A("PO", 0, 56), A("P0", 0, 56))
+            cp(A("PO", 72, 128), A("P0", 56, 112))
+            for o in range(2):
+                lin(A("BOH", 128 * o, 128 * o + 128), A("BO"), K(10 - o))
+        if t == 2:
+            fold([(1, 2), (1, 6)], False, False)
+        tt(A("D2"), IND(A("PL"), A("KO", 40, 48)), A("DM"), OP.mult)
+        act(y, A(land, 0, L), AF.Abs)
+        mm(A("P6", 256, 264), [(A("D2"), A("CM"))])
+        ts(A("WB"), y, A("TH", t, t + 1), OP.is_ge)
+        cp(A("SO", 24, 32), A("P6", 256, 264))
+        act(stp, IND(A("ST"), A("SO", 24, 32)))
+        if not last:
+            act(A("SR"), IND(A("SC"), A("KO", 32, 40)), AF.Sign, bias=-3071.9)
+            mm(A("PV", 0, 1), [(A("SR"), A("ON", 0, 1))])
+            lia(A("AC", 0, 1), A("PV", 0, 1), -0.5, 64.0)
+            offsets(t + 1)
+        wrap(A("P4", 64, 72), "Z8", "VB", YC, 8)
+        act(A("BS"), IND(A("ST"), A("SO", 16, 24)))
         if last:
-            spawn_lists()
-        mm(A("P5", 0, 128), [(A("ID"), A("BS")), (A("ID"), A("M1"))])
-        act(A("ST", YC, VW), A("P5", 0, 128))
-
-        def vlist():
-            mm(A("P6", 256, 264), [(A("Z4", 15 - p, 143 - p), A("SP", 128 * t + p, 128 * t + 128, 16)) for p in range(16)]
-               + [(A("D2"), A("CM", 0, 8))])
+            tt(A("DF"), IND(A("VB", 0, YC), A("SO", 24, 32)), y, OP.subtract)
+        cp(A("SI", 32, 40), A("P4", 64, 72))
+        ts(A("SI", 24, 32), A("SI", 32, 40), 896, OP.bitwise_and)
+        tt(A("SI", 32, 40), A("SI", 24, 32), A("LN", 0, 8), OP.add)
+        cp(A("SO", 32, 40), A("SI", 32, 40))
+        mm(A("P5", 0, 128), [(A("BO"), A("WB")), (A("LD"), stp)])
+        mm(A("PV", 128, 256), [(A("ID", 4, 132), stp)])
+        mm(A("P7", 0, 128), [(A("DD"), stp), (ID, ct)])
+        mm(A("P6", 0, 128), [(A("DG"), stp), (ID, ct)])
+        ts(sp, A("P5", 0, 128), 7.5, OP.is_ge)
+        act(A("STP", 128, 256), A("PV", 128, 256))
+        tt(A("M1"), A("P7", 0, 128), sp, OP.mult)
+        mm(A("P5", 0, 128), [(ID, A("BS")), (ID, A("M1"))])
+        act(A("ST", n0, n0 + L), A("P6", 0, 128))
+        act(cur, A("P5", 0, 128))
+        if last:
+            wrap(A("PV", 256, 272), "ZF", "STP", 0, 16)
+        else:
+            lin(A("STP", 256, 384), sp, K(33))
+            wrap(A("PV", 256, 280), "ZE", "STP", 0, 24, False)
+            mm(A("PV", 272, 280), [(A("D2"), A("CM"))], False, True, True)
+        mm(A("P4", 128, 256), [(ID, y), (A("HI"), sp)])
+        cp(A("SO", 48, 64), A("PV", 256, 272))
+        act(A("VB", n0, n0 + L), A("P4", 128, 256), AF.Relu, bias=-4096.0)
+        if t:
+            cp(A("S2", 16 * t - 16, 16 * t), A("PV", 256, 272))
 
         def arrive():
-            wait("a", "arr%d" % t, N - 1)
-            act(A("ZZ"), IND(A(land), A("SO", 32, 40)), AF.Abs)
+            win = A(land)
+            act(A("ZZ"), IND((win[0], win[1] + [arr]), A("SO", 32, 40)), AF.Abs)
             wrap(A("P4", 72, 80), "ZM", "ZZ", 0, 8)
-
-        def blist():
             cp(A("SI", 40, 48), A("P4", 72, 80))
             ts(A("SI", 48, 56), A("SI", 40, 48), 31, OP.bitwise_and)
             tt(A("SI", 40, 48), A("SI", 48, 56), A("LN", 8, 16), OP.add)
             cp(A("SO", 40, 48), A("SI", 40, 48))
 
         if not last:
-            act(A("NC"), A("ST", YC, VW), scale=-1.0)
-            act(A("VB", YC, VW), y)
-            act(A("VB", n0, n0 + L), y)
-            vlist()
-            if EARLY:
-                spawn_lists()
-            cp(A("SO", 32, 40), A("SI", 32, 40))
-            step(3)
-            tt(A("SI", 56, 64), A("P6", 256, 264), A("LN", 16, 24), OP.min)
-            step()
-            cp(A("SO", 0, 8), A("SI", 56, 64))
-            act(A("CT", 128 * t + 128, 128 * t + 256), A("IO", 0, 128), scale=O(9), bias=K(62 + t))
-            cp(IND(A("VB", 0, YC), A("SO", 0, 8)), y)
-            if EARLY:
-                slots(t, "PV")
-                for o in range(EARLY):
-                    flags(t, o)
-            if t == 1:
-                consts_a3()
-                masks(0, 256)
-            else:
-                consts_a5()
-            arrive()
+            tt(A("SI", 56, 64), A("PV", 272, 280), A("LN", 16, 24), OP.min)
             if t == 0:
-                consts_a4()
-            else:
-                act(A("SCM"), A("SCM"), scale=K(12))
-            blist()
-            if not EARLY:
-                spawn_lists()
-            for hb in range(2):
-                for gq in range(4):
-                    s = A("SEL", 512 * hb + 128 * gq, 512 * hb + 128 * gq + 128)
-                    mm(A(("P6", "P7")[hb], 128 * gq, 128 * gq + 128), [(s, A("NC")), (A("ST", YC, VW), s), (A("HI"), A("TRI"))])
-            cp(IND(A("IA"), A("SO", 40, 48)), A("ST", YC, VW))
+                consts_rounds()
+            lia(A("CT", 128 * t + 128, 128 * t + 256), A("IO", 0, 128), O(9), K(62 + t))
+            cp(A("SO", 0, 8), A("SI", 56, 64))
+            cp(IND(A("VB", 0, YC), A("SO", 0, 8)), y)
+            for o in range(FL1 if t else 2):
+                flags(t, o)
+            for gg in (0, 1, 4, 5, 2, 3, 6, 7):
+                rows = (32 * (gg // 2), 32 * (gg // 2) + 32)
+                s, sn = (A("SEL", 128 * (gg % 2 + j), 128 * (gg % 2 + j) + 128, p=rows) for j in (0, 2))
+                cr = A("ST", YC, VW, p=rows)
+                mm(A(("P6", "P7")[gg // 4], 128 * (gg % 4), 128 * (gg % 4) + 128), [(sn, cr), (cr, s), (A("HI"), A("TRI"))], fence=gg in (2, 6))
+            for h in range(2):
+                act(A("EA", 512 * h, 512 * h + 512), A(("P6", "P7")[h]), AF.Abs)
+                act(A("EQ", 512 * h, 512 * h + 512), A("EA", 512 * h, 512 * h + 512), AF.Relu, bias=2048.0, scale=-2048.0)
+            arrive()
+            cp(IND(A("IA"), A("SO", 40, 48)), cur)
             cp(IND(A("XB"), A("SO", 40, 48)), A("ZZ"))
             if t == 0:
-                wait("s", "arr0", N - 1)
-                for d in (1, 3, 5, 7):
-                    zero("AE", d)
-                asel(A("B0", 0, 128), A("B0", 128, 256), [[0, 8], [-1, 16]], OP.is_ge, 7, 0)
-                flmat(0, 4)
-                flmat(1, 4)
-                asel(A("B7"), A("BO"), [[0, 16], [1, 8]], OP.not_equal, -7, 0)
-                for d in (2, 6, 1, 3, 5, 7):
+                iota(A("SCM"), [[0, 784]])
+                consts_places()
+                for d in (4, 2, 6, 1, 3, 5, 7):
                     flmat(0, d)
                     flmat(1, d)
             else:
                 iota(A("TT", 768, 784), [[0, 16]])
         else:
-            cp(A("SO", 32, 40), A("SI", 32, 40))
             flags(t, 0)
-            cp(A("SO", 56, 64), A("PV", 8, 16))
+            masks(256, 384, "P7")
             flags(t, 1)
-            act(A("VB", n0, n0 + L), y)
-            masks(256, 384)
-            fold([(0, d) for d in (1, 3, 5, 7)], False, False)
-            cp(A("S2", 0, 8), A("PE", 0, 8))
-            cp(A("S2", 8, 16), A("PV", 8, 16))
+            fold([(o, d) for o in range(2) for d in (1, 3, 5, 7)], False, True)
             tt(A("DF"), A("DF"), sp, OP.mult)
-            ts(A("S2", 16, 32), A("S2", 0, 16), PW - 1, OP.bitwise_and)
             tt(IND(A("VB", 0, YC), A("SO", 24, 32)), A("DF"), y, OP.add)
-            tt(A("VB", S0, 1152), A("VB", S0, 1152), A("SP"), OP.mult)
             dma("s", H(T.yv[:, :]), A("VB", 0, 1152))
             arrive()
-            fold([(1, d) for d in (1, 3, 5, 7)], False, True)
-            blist()
+            cp(IND(A("IA"), A("SO", 40, 48)), cur)
             cp(IND(A("XB"), A("SO", 40, 48)), A("ZZ"))
-            dma("s", H(T.yx[:, :]), A("XB"))
-            cp(IND(A("IA"), A("SO", 40, 48)), A("ST", YC, VW))
-            ts(A("PO", 48 + 8 * t, 56 + 8 * t), A("S2", 16, 24), 1.0, OP.add)
-            cp(A("PO", 120 + 8 * t, 128 + 8 * t), A("S2", 24, 32))
+            dma("s", H(T.yx[:, :]), A("XB"), lag=4.5)
             scan(A("TT", 0, 512), A("SCM", 0, 512), A("P0"), OP.mult, OP.add)
+            places()
             scan(A("TT", 512, 769), A("SCM", 512, 769), A("P1", 0, 257), OP.mult, OP.add, A("TT", 511, 512))
             tw = A("TT")
             act(A("OE", 0, S0), IND(tw, A("PO", 0, 48)), bias=-1.0)
-            mm(A("P6", 0, 256), [(A("ZS", 15 - p, 143 - p), A("IA", 256 * p, 256 * p + 256)) for p in range(16)])
+            for p in range(16):
+                mm(A("P6", 0, 256), [(A("ZS", 15 - p, 143 - p), A("IA", 256 * p, 256 * p + 256))], p == 0, p == 15)
             tt(A("TM", 0, 384), IND(tw, A("PO", 48, 72)), A("MM", 0, 384), OP.mult)
             tt(A("TM", 384, 768), IND(tw, A("PO", 120, 144)), A("MM", 384, 768), OP.mult)
-            mm(A("P4", 0, 384), [(A("BOH"), A("TM", 0, 384))])
-            mm(A("P5", 0, 384), [(A("BOH"), A("TM", 384, 768))])
-            ts(A("OH", 0, 512), IND(tw, A("PO", 72, 104)), -1.0, OP.add)
-            act(A("WN"), A("P6", 0, 256))
-            dma("s", H(T.yw[:, :]), A("WN"))
+            mm(A("P4", 0, 384), [(A("BOH", 0, 128), A("TM", 0, 384))])
+            mm(A("P5", 0, 384), [(A("BOH", 128, 256), A("TM", 384, 768))])
+            ts(A("OH", 0, 16 * OHV), IND(tw, A("PO", 72, 72 + OHV)), -1.0, OP.add)
             act(A("OE", S0, 1152), A("P4", 0, 384), bias=-1.0)
             dma("s", H(T.ye[:, :]), A("OE", p=(7, 128, 16)))
-            act(A("OH", 512, S0), IND(tw, A("PO", 104, 120)), bias=-1.0)
+            act(A("OH", 16 * OHV, S0), IND(tw, A("PO", 72 + OHV, 120)), bias=-1.0)
+            cp(A("WN"), A("P6", 0, 256))
+            dma("s", H(T.yw[:, :]), A("WN"))
             act(A("OH", S0, 1152), A("P5", 0, 384), bias=-1.0)
             dma("a", H(T.yh[:, :]), A("OH", p=(15, 128, 16)))
 
+    if not START:
+        START.update(plan())
+    issue(START)
     for sem in cnt:
         if cnt[sem]:
             wait("s" if sem[0] == "d" else "g", sem, cnt[sem])

@@ -1,22 +1,18 @@
 from concourse.bass import DstId, RemoteDMATransfer
-from concourse.mybir import AluOpType as OP, ActivationFunctionType as AF
+from concourse.mybir import AluOpType as OP, ActivationFunctionType as AF, AxisListType
 
 C, L, S0, NT = 4096, 128, 768, 3
 DUM, YC = 1152, 1280
 VW = YC + L
 PW = 1024
-XA = (104, 88, 88)
+XA = (96, 88, 88)
 KW = 25
 GM = 3079
-BUILD = "avavavav"
-FL1 = 2
-OHV = 32
 BT, MS = 3072, 6144
 TABLE = ((("AE", 2048, 5248, 256), ("AH", 2176, 4352, 256)), (("AE", 0, 3200, 256), ("AH", 0, 2176, 256)),
          (("AE", 0, 6272, 512), ("GB", 0, 4224, 512)))
-CYC, PECYC, FIX, GFIX, GATHER, SCATTER, HOP = 0.00091, 0.00046, 0.01, 0.055, 1.25, 3.0, 0.25
-XLAG, FLOOR, NEXT, POOL, FIXA = 5.0, 64, 0.2, 2.4, 0.11
-HEAVY, GUARD, HOLD, TRAVEL, SWEEPS, EARLY = 0.3, 2.5, (8.0, 2.5, 2.5), (6.5, 4.2, 4.0), 3, 66.0
+ZAT = {nm: 144 * j for j, nm in enumerate(("ZS", "ZE", "ZF", "ZP", "ZQ", "Z8", "ZM"))}
+ZW = 7 * 144 + 24
 BF, F32, I32, U16 = "bfloat16", "float32", "int32", "uint16"
 
 
@@ -29,22 +25,21 @@ SCRATCH = {
     "MT": _sb(256, BF), "TH": _sb(16, BF),
     "LD0": _sb(1024, BF), "LD1": _sb(1024, BF), "LD2": _sb(1024, BF), "AE": _sb(6272, BF), "AH": _sb(4352, BF),
     "WL": _sb(256, I32), "W1": _sb(256, F32), "W2": _sb(256, F32), "WO": _sb(256, U16), "WN": _sb(256, F32),
-    "EL": _sb(96, I32), "E1": _sb(192, I32), "NP": _sb(288, BF),
-    "IO": _sb(144, F32), "IM": _sb(128, F32), "I8": _sb(128, F32),
-    "PI": _sb(8, I32), "PJ": _sb(8, I32), "K": _sb(64, F32), "O": _sb(16, F32), "KI": _sb(48, I32), "KO": _sb(48, U16),
-    "BO": _sb(128, BF), "ID": _sb(144, BF), "LH0": _sb(128, BF), "LH1": _sb(128, BF),
-    "DM": _sb(128, F32), "CM": _sb(8, F32), "Z0": _sb(144, F32), "ZM": _sb(144, BF), "ZS": _sb(144, BF), "ZE": _sb(144, BF),
-    "ZF": _sb(144, BF), "ZP": _sb(144, BF), "ZQ": _sb(144, BF), "Z8": _sb(144, BF),
-    "FEH": _sb(16, BF), "FEN": _sb(400, BF), "I24": _sb(400, BF), "FV": _sb(8, BF), "FS": _sb(8, BF), "G8": _sb(8, BF),
-    "RK": _sb(800, BF), "OI": _sb(128, BF), "SEG": _sb(1024, BF),
-    "LD": _sb(128, BF), "DG": _sb(128, BF), "DD": _sb(128, BF), "NI": _sb(128, BF), "CT": _sb(384, BF), "SEL": _sb(512, BF),
-    "TRI": _sb(128, BF), "EA": _sb(1024, BF), "EQ": _sb(1024, BF), "ON": _sb(128, BF),
+    "EL": _sb(96, I32), "E1": _sb(192, I32), "NP": _sb(288, BF), "QF": _sb(8, F32), "TN": _sb(3, F32), "SQ": _sb(48, U16),
+    "IO": _sb(144, BF), "I8": _sb(136, BF),
+    "PI": _sb(8, I32), "PJ": _sb(8, I32), "K": _sb(80, F32), "KI": _sb(48, I32), "KO": _sb(48, U16),
+    "BO": _sb(128, BF), "ID": _sb(144, BF), "LH": _sb(136, BF),
+    "DM": _sb(128, F32), "CM": _sb(8, F32), "ZA": _sb(ZW, BF),
+    "FEN": _sb(400, BF), "I24": _sb(400, BF), "G8": _sb(8, BF),
+    "RK": _sb(528, BF), "SEG": _sb(1024, BF),
+    "LD": _sb(128, BF), "DG": _sb(128, BF), "DD": _sb(128, BF), "CT": _sb(384, BF), "SEL": _sb(512, BF),
+    "IX": _sb(128, BF), "LR": _sb(128, BF), "EA": _sb(1024, BF), "EQ": _sb(1024, BF), "ON": _sb(128, BF),
     "FL": _sb(14 * 128, BF), "B0": _sb(256, BF), "B7": _sb(128, BF), "LO": _sb(256, BF), "HI": _sb(128, BF), "HN": _sb(128, BF),
-    "SCM": _sb(784, BF), "U": _sb(64, I32), "U1": _sb(64, I32), "UU": _sb(64, I32), "UB": _sb(64, I32), "UA": _sb(192, I32),
+    "SCM": _sb(784, BF), "U": _sb(64, F32), "U1": _sb(64, I32), "UU": _sb(64, F32), "UB": _sb(64, I32), "UA": _sb(192, I32),
     "UC": _sb(192, I32), "AO": _sb(192, U16), "SL": _sb(192, U16), "AC": _sb(4, F32), "SG": _sb(400, BF), "NPB": _sb(200, BF),
     "VL": _sb(200, F32), "SC": _sb(200, F32), "SF": _sb(8, F32), "D1": _sb(128, F32), "D2": _sb(128, F32),
-    "SR": _sb(128, BF), "NR": _sb(8, BF), "PL": _sb(16, F32), "SI": _sb(64, I32), "SO": _sb(64, U16), "LN": _sb(24, F32),
-    "IN": _sb(128, BF), "ZR": _sb(800, BF), "S2": _sb(64, I32),
+    "SR": _sb(128, BF), "NR": _sb(16, BF), "PL": _sb(16, F32), "SI": _sb(64, I32), "SO": _sb(48, U16), "LN": _sb(24, F32),
+    "IN": _sb(128, BF), "ZR": _sb(864, BF), "S2": _sb(64, I32),
     "G1": _sb(128, BF), "WB": _sb(128, BF), "SP": _sb(384, BF), "STP": _sb(384, BF), "BS": _sb(128, BF),
     "M1": _sb(128, BF), "DF": _sb(128, BF), "ZZ": _sb(128, BF),
     "PO": _sb(144, U16), "TT": _sb(784, F32), "MM": _sb(768, F32), "MA": _sb(768, F32), "TM": _sb(768, "float16"),
@@ -53,8 +48,7 @@ SCRATCH = {
 PSUM = ["P0", "P1", "PE", "PV", "P4", "P5", "P6", "P7"]
 for _n in PSUM:
     SCRATCH[_n] = ("psum", [128, 512], F32)
-START = {}
-NDMA = 40
+NDMA = 48
 SEMAPHORES = ["sv", "sa", "sp", "sg", "sent", "arr0", "arr1", "arr2"] + ["d%d" % i for i in range(NDMA)]
 
 
@@ -67,8 +61,7 @@ def rank_program(g, core, T, topo):
     SEM = {"v": "sv", "a": "sa", "p": "sp", "g": "sg"}
     cnt = {"sv": 0, "sa": 0, "sp": 0, "sg": 0, "sent": 0}
     waited = {q: {} for q in Q}
-    hist = {}
-    nd = [0]
+    hist, lastp, nd = {}, {}, [0]
 
     def A(name, lo=0, hi=None, step=1, p=None):
         t = T[name]
@@ -79,6 +72,9 @@ def rank_program(g, core, T, topo):
 
     def IND(win, off):
         return (win[0].indirect(off[0]), win[1], off[1])
+
+    def H(ap):
+        return (ap, [])
 
     def wait(q, sem, val):
         if waited[q].get(sem, 0) < val:
@@ -113,29 +109,32 @@ def rank_program(g, core, T, topo):
                     h[:] = [e for e in h if not (lo <= e[3] and e[4] <= hi and nm not in PSUM)]
                 h.append((q, sem, val, lo, hi, wr))
 
-    calls, due = [], [0.0]
-
-    def record(q, fn, reads, writes, cost, lag=HOP, kind="c", **kw):
-        calls.append(dict(q=q, fn=fn, r=reads, w=writes, cost=cost, lag=lag, kind=kind, due=due[0], **kw))
-
-    def run(q, fn, out, ins, per=1.0, cost=None, **kw):
+    def run(q, fns, out, ins, fence=False):
         reads, writes = [], list(out[1])
         if len(out) == 3:
             reads += out[2]
-        aps = [x for x in ins if isinstance(x, tuple)]
-        for x in aps:
-            reads += x[1]
-            if len(x) == 3:
-                reads += x[2]
-        if cost is None:
-            ind = [x for x in [out] + aps if len(x) == 3]
-            if ind:
-                cost = GFIX + 16 * (ind[0][2][0][2] - ind[0][2][0][1]) * (SCATTER if len(out) == 3 else GATHER) * CYC
-            else:
-                if q == "v" and per == 1.0 and all(SCRATCH[x[1][0][0]][2] in (BF, U16, "float16") for x in [out] + aps if x[0].shape[1] > 1):
-                    per = 0.5
-                cost = FIX + max(FLOOR, out[0].shape[1] * per) * CYC if q == "v" else FIXA + out[0].shape[1] * CYC
-        record(q, fn, reads, writes, cost, heavy=cost > HEAVY and q in "va", **kw)
+        for x in ins:
+            if isinstance(x, tuple):
+                reads += x[1] + (x[2] if len(x) == 3 else [])
+        order(q, reads, writes)
+        if fence:
+            wait("p", "sp", lastp[writes[0][0]])
+        for fn in (fns if q == "p" else [fns]):
+            fn().then_inc(T.sem[SEM[q]], 1)
+            cnt[SEM[q]] += 1
+        if q == "p":
+            lastp[writes[0][0]] = cnt["sp"]
+        note(q, SEM[q], cnt[SEM[q]], reads, writes)
+
+    def dma(q, o, i, keep=False):
+        order(q, i[1], o[1], True, keep)
+        sem = "d%d" % nd[0]
+        nd[0] += 1
+        Q[q].dma_start(o[0], i[0]).then_inc(T.sem[sem], 16)
+        cnt[sem] = 16
+        note("dma", sem, 16, i[1], [])
+        for (nm, lo, hi) in o[1]:
+            hist.setdefault(nm, []).append(("dma", sem, 16, lo, hi, True))
 
     def val(x):
         return x[0] if isinstance(x, tuple) else x
@@ -144,7 +143,7 @@ def rank_program(g, core, T, topo):
         run("v", lambda: g.vector.tensor_copy(o[0], i[0]), o, [i])
 
     def tt(o, a, b, op):
-        run("v", lambda: g.vector.tensor_tensor(o[0], a[0], b[0], op), o, [a, b], 1.001 if a[1][0][0] in PSUM else 2.0)
+        run("v", lambda: g.vector.tensor_tensor(o[0], a[0], b[0], op), o, [a, b])
 
     def ts(o, a, s1, op0, s2=None, op1=None):
         if op1 is None:
@@ -178,475 +177,371 @@ def rank_program(g, core, T, topo):
     def mm(o, pairs, start=True, stop=True, fence=False):
         fns = [lambda l=l, r=r, n=n: g.tensor.matmul(o[0], l[0], r[0], start and n == 0, stop and n == len(pairs) - 1)
                for n, (l, r) in enumerate(pairs)]
-        cost = sum(max(64, o[0].shape[1]) * PECYC * (4 if SCRATCH[l[1][0][0]][2] == F32 else 1) for l, r in pairs)
-        run("p", fns, o, [x for pr in pairs for x in pr], cost=cost, fence=fence)
+        run("p", fns, o, [x for pr in pairs for x in pr], fence)
 
-    def iota(o, pat, base=0, cm=0, fl=True, solo=False):
-        cost = 0.13 + POOL * o[0].shape[1] * CYC
-        if fl:
-            run("g", lambda: g.iota(o[0], pat, base, cm, allow_small_or_imprecise_dtypes=True), o, [], cost=cost, solo=solo)
+    def iota(o, pat, base=0, cm=0):
+        if SCRATCH[o[1][0][0]][2] == I32:
+            run("g", lambda: g.iota(o[0], pat, base, cm), o, [])
         else:
-            run("g", lambda: g.iota(o[0], pat, base, cm), o, [], cost=cost)
+            run("g", lambda: g.iota(o[0], pat, base, cm, allow_small_or_imprecise_dtypes=True), o, [])
 
-    def asel(o, i, pat, op, base, cm, fill=0.0, solo=False):
-        run("g", lambda: g.affine_select(o[0], i[0], pat, op, fill, base, cm), o, [i], cost=0.17 + POOL * o[0].shape[1] * CYC, solo=solo)
-
-    def dma(q, o, i, keep=False, lag=2.5, after=()):
-        record(q, lambda: Q[q].dma_start(o[0], i[0]), list(i[1]) + list(after), list(o[1]), 0.1, lag, "dma", keep=keep, heavy=True)
-
-    def plan():
-        seen, preds, lastq = {}, [], {}
-        for n, c in enumerate(calls):
-            ps = {}
-            for rs, wr in ((c["r"], False), (c["w"], True)):
-                for (nm, lo, hi) in rs:
-                    h = seen.setdefault(nm, [])
-                    for (m, l2, h2, w2) in h:
-                        if m != n and (nm in PSUM or ((wr or w2) and l2 < hi and lo < h2 and not (c.get("keep") and calls[m].get("keep")))):
-                            same = calls[m]["q"] == c["q"] and calls[m]["kind"] == "c"
-                            ps[m] = calls[m]["lag"] if not same else NEXT if c["q"] != "p" or c.get("fence") else 0.0
-                    if nm in PSUM or wr and not c.get("keep"):
-                        h[:] = [e for e in h if not (nm in PSUM or lo <= e[1] and e[2] <= hi)]
-                    h.append((n, lo, hi, wr))
-            if c.get("heavy"):
-                if c["q"] in lastq:
-                    ps.setdefault(lastq[c["q"]], 0.0)
-                lastq[c["q"]] = n
-            preds.append(ps)
-        succs = [{} for c in calls]
-        for n in range(len(calls)):
-            for m in preds[n]:
-                succs[m][n] = preds[n][m]
-        tail = [c["lag"] if c["kind"] == "dma" else 0.0 for c in calls]
-
-        def place(turn, before, head, forward):
-            busy, first, end = {q: [] for q in Q}, {}, {}
-            for n in turn:
-                c = calls[n]
-                at = max([end[m] + before[n][m] for m in before[n]] + [head[n]])
-                for (a, b) in busy[c["q"]]:
-                    if at + c["cost"] <= a:
-                        break
-                    at = max(at, b)
-                first[n], end[n] = at, at + c["cost"]
-                ahead, behind = (GUARD, c["hold"]) if c["kind"] == "send" else (0.0, 0.0)
-                busy[c["q"]].append((at - ahead, end[n] + behind) if forward else (at - behind, end[n] + ahead))
-                busy[c["q"]].sort()
-            return first, end
-
-        late = [max(tail[n], c["due"]) for n, c in enumerate(calls)]
-        way = list(late)
-        for n in reversed(range(len(calls))):
-            way[n] += calls[n]["cost"]
-            for m in preds[n]:
-                way[m] = max(way[m], way[n] + preds[n][m])
-        best = None
-        for sweep in range(SWEEPS):
-            first, end = place(sorted(range(len(calls)), key=lambda n: (-way[n], n)), preds, [0.0] * len(calls), True)
-            span = max(end[n] + tail[n] for n in end)
-            if best is None or span < best:
-                best, start = span, first
-            way = place(sorted(range(len(calls)), key=lambda n: (-end[n], -n)), succs, late, False)[1]
-        return start
-
-    def issue(start):
-        solo, lastp = False, {}
-        for n in sorted(range(len(calls)), key=lambda n: (start[n], n)):
-            c = calls[n]
-            q = c["q"]
-            reads, writes = ([x for x in rs if x[0] in SCRATCH] for rs in (c["r"], c["w"]))
-            for (nm, lo, hi) in c["r"]:
-                if nm not in SCRATCH:
-                    wait(q, nm, N - 1)
-            if c["kind"] == "dma":
-                order(q, reads, writes, True, c["keep"])
-                sem = "d%d" % nd[0]
-                nd[0] += 1
-                c["fn"]().then_inc(T.sem[sem], 16)
-                cnt[sem] = 16
-                note("dma", sem, 16, reads, [])
-                for (nm, lo, hi) in writes:
-                    hist.setdefault(nm, []).append(("dma", sem, 16, lo, hi, True))
-                continue
-            if q == "g":
-                if solo or c.get("solo"):
-                    wait("g", "sg", cnt["sg"])
-                solo = c.get("solo")
-            order(q, reads, writes)
-            if c["kind"] == "send":
-                c["fn"]()
-                cnt["sent"] += N - 1
-                continue
-            if c.get("fence"):
-                wait("p", "sp", lastp[writes[0][0]])
-            for fn in (c["fn"] if q == "p" else [c["fn"]]):
-                fn().then_inc(T.sem[SEM[q]], 1)
-                cnt[SEM[q]] += 1
-            if q == "p":
-                lastp[writes[0][0]] = cnt["sp"]
-            note(q, SEM[q], cnt[SEM[q]], reads, writes)
-
-    def H(ap):
-        return (ap, [])
+    def asel(o, i, pat, op, base, cm, fill=0.0):
+        run("g", lambda: g.affine_select(o[0], i[0], pat, op, fill, base, cm), o, [i])
 
     def wrap(o, Z, name, lo, n, stop=True):
-        mm(o, [(A(Z, 15 - p, 143 - p), A(name, lo + p, lo + 16 * n, 16)) for p in range(16)], True, stop)
+        mm(o, [(A("ZA", ZAT[Z] + 15 - p, ZAT[Z] + 143 - p), A(name, lo + p, lo + 16 * n, 16)) for p in range(16)], True, stop)
 
     def K(j):
         return A("K", j, j + 1)
 
     def O(r):
-        return A("O", r, r + 1)
+        return A("DM", r, r + 1)
 
     def plane(o, d):
         t = 0 if d == 4 else 1 + d % 2
         nm, lo, hi, unit = TABLE[t][o]
         return nm, lo + unit * (d + (4 >> t) * (1 - 2 * o))
 
-    def zero(o, d, after=()):
+    def zero(o, d):
         nm, c = plane(o, d)
-        dma("s", A(nm, c - 16 + 16 * o, c + 784), A("ZR", 0, 800 - 16 * o), lag=6.0, after=after)
+        dma("s", A(nm, c - 16 + 16 * o, c + 784), A("ZR", 0, 800 - 16 * o))
 
-    dma("a", A("EL", 0, 48), H(T.e0[:, :]))
-    dma("s", A("EL", 48, 96), H(T.h0[:, :]))
-    for h in range(2):
-        dma("as"[h], A("WL", 128 * h, 128 * h + 128), H(T.w0[h::2, :]))
-    dma("a", A("VB", 0, L), H(T.v0[:, 0:L]))
-    for j in range(2):
-        dma("sa"[j], A("XB", 2048 * j, 2048 * j + 2048), H(T.x0[:, 2048 * j:2048 * j + 2048]), lag=XLAG + j)
-    dma("a", A("VB", L, S0), H(T.v0[:, L:S0]), lag=XLAG + 2)
-
-    iota(A("PI", 0, 1), [[0, 1]], 0, 1, False)
-    iota(A("IO"), [[1, 144]])
-    iota(A("KI", 0, 16), [[16, 8], [128, 2]], 0, 0, False)
-    iota(A("KI", 16, 32), [[2, 16]], 0, 0, False)
-    iota(A("KI", 32, 40), [[KW, 8]], KW - 1, 0, False)
-    iota(A("KI", 40, 48), [[1, 8]], 0, 0, False)
-    iota(A("I8"), [[1, 16], [0, 8]])
-    iota(A("IM"), [[0, 8], [1, 16]])
-    ms(A("ST", 0, YC), 0.0)
-    ms(A("ON"), 1.0)
-    ms(A("AC"), 0.0)
-    p_ = A("PI", 0, 1)
-    ts(A("PJ", 0, 1), p_, 15, OP.bitwise_and)
-    ts(A("PJ", 1, 2), p_, 4, OP.logical_shift_right)
-    ts(A("PJ", 2, 3), p_, 3, OP.bitwise_and)
-    ts(A("PJ", 3, 4), p_, 2, OP.logical_shift_right, 3, OP.bitwise_and)
-    ts(A("PJ", 4, 5), p_, 7, OP.bitwise_and)
-    ts(A("PJ", 5, 6), p_, 3, OP.logical_shift_right, 1, OP.bitwise_and)
-    ts(A("PJ", 6, 7), p_, 127, OP.bitwise_and)
-    ts(A("PJ", 7, 8), p_, 4, OP.logical_shift_right, 1, OP.bitwise_and)
-    cp(A("K", 0, 7), A("PJ", 0, 7))
-    kR, kG, kS, kQ, k7, kH, kP = [K(j) for j in range(7)]
-    ts(K(30), kR, 2.0, OP.is_equal, 8.0, OP.mult)
-    ts(A("NP", 192, 240), A("ON", 0, 48), kR, OP.mult, 1.5, OP.mult)
-    act(A("ST", 0, S0), A("ST", 0, S0), bias=K(30))
-    cp(A("NP", 240, 288), A("IO", 0, 48))
-    lin(K(7), k7, 32.0, kH)
-    ts(A("O"), A("IO", 0, 16), kR, OP.is_equal)
-    ts(A("K", 18, 22), A("IO", 0, 4), kS, OP.is_equal)
-    ts(A("K", 22, 26), A("IO", 0, 4), kQ, OP.is_equal)
-    ts(A("CM"), A("IO", 0, 8), kG, OP.is_equal)
-    lin(K(35), kG, 16.0, 15.0)
-    lin(K(26), K(18), 32.0, K(19))
-    ts(A("Z0"), A("IO"), K(35), OP.is_equal)
-    due[0] = EARLY + 1.0
-    lia(K(8), kR, 2.0, 1.0)
-    lia(K(9), kG, 2.0)
-    lia(K(10), kG, 2.0, 1.0)
-    act(A("K", 11, 14), A("IO", 0, 24, 8), bias=k7)
-    lia(K(31), kP, 8.0)
-    act(A("K", 14, 17), A("K", 11, 14), AF.Square, bias=0.5)
-    lia(K(52), kQ, 8.0, kG)
-    act(A("K", 14, 17), A("K", 14, 17), bias=0.75)
-    due[0] = 0.0
-    ts(A("E1", 0, 96), A("EL"), 5, OP.logical_shift_right)
-    ts(A("E1", 96, 192), A("EL"), 31, OP.bitwise_and)
-    cp(A("NP", 0, 192), A("E1"))
-    ts(A("KI", 0, 16), A("KI", 0, 16), kR, OP.add)
-    ts(A("KI", 16, 32), A("KI", 16, 32), K(7), OP.add)
-    cp(A("KO"), A("KI"))
-    cp(A("W1"), IND(A("WL"), A("KO", 0, 16)))
-    for j, row, q in ((4, 8, "s"), (5, 9, "s"), (0, 0, "a"), (1, 4, "s"), (2, 1, "a"), (3, 5, "s")):
-        dma(q, A("ST", 0, S0, p=(row, 128, 16)), A("NP", 48 * j, 48 * j + 48), True)
-    dma("s", A("TH", 0, 3), H(T.th[:, :]))
-    run("v", lambda: g.vector.transpose(T.W2[:, :], T.W1[:, :]), A("W2"), [A("W1")])
-    ts(A("LH0"), A("I8"), K(9), OP.is_equal, K(8), OP.mult)
-    ts(A("LH1"), A("I8"), K(10), OP.is_equal, K(8), OP.mult)
-    cp(A("WO"), IND(A("W2"), A("KO", 16, 32)))
-
-    def offsets(t):
-        y0 = YC if t else 0
-        mm(A("PE", 0, 64), [(A("LH0"), A("VB", y0, y0 + L, 2)), (A("LH1"), A("VB", y0 + 1, y0 + L, 2))])
-        cp(A("U1"), A("PE", 0, 64))
-        ts(A("U"), A("U1"), 4095, OP.bitwise_and)
-        tt(A("UU"), A("U"), A("U"), OP.mult)
-        for m in range(3):
-            lin(A("UA", 64 * m, 64 * m + 64), A("U"), K(14 + m), A("AC", 0, 1))
-        ts(A("UB"), A("UU"), 5, OP.logical_shift_right)
-        for m in range(3):
-            tt(A("UC", 64 * m, 64 * m + 64), A("UA", 64 * m, 64 * m + 64), A("UB"), OP.add)
-        ts(A("UA"), A("UC"), 4095, OP.bitwise_and)
-        cp(A("AO"), A("UA"))
-        calls[-1]["heavy"] = True
-
-    due[0] = EARLY
-    lia(K(29), K(20), -0.125, K(26))
-    lia(A("K", 36, 40), A("K", 22, 26), K(26))
-    lia(A("K", 44, 48), A("K", 22, 26), K(29))
-    lia(K(54), K(29), -1.0)
-    lia(K(48), K(38), 1.0 / 4096)
-    lia(A("ZS"), A("Z0"), K(38))
-    lia(A("FEH", 0, 8), A("CM"), K(44))
-    lia(A("FEH", 8, 16), A("CM"), K(45))
-    lia(A("FV"), A("CM"), K(48))
-    due[0] = 0.0
-    rk = [A("RK", 200 * j, 200 * j + 200, p=(0, 1)) for j in range(4)]
-    iota(A("RK", 0, 600, p=(0, 1)), [[0, 600]])
-    iota(rk[3], [[0, 8], [-1, KW]], KW - 1)
-    asel(rk[0], rk[0], [[0, 8], [1, KW]], OP.is_ge, -17, 0, 1016.0)
-    iota(A("OI", p=(0, 1)), [[1, 128]])
-    asel(rk[0], rk[0], [[0, 8], [1, KW]], OP.is_ge, -9, 0, 2032.0)
-    for j, c in ((1, 1 / 4096), (2, -2.0 ** 19), (3, GM - 3072 + YC / 4096), (0, 3072.0)):
-        o = A("RK", 200 * j, 200 * j + 200, KW, p=(0, 1))
-        asel(o, o, [[0, 8]], OP.is_gt, 0, 0, c)
-    iota(A("I24"), [[1, 16], [0, KW]])
-    lia(A("VB", S0, YC), A("ST", S0, YC), 0.0)
+    def weigh(name, n, r, w):
+        o = A("ZA", ZAT[name] + 15, ZAT[name] + 144 * n, 16)
+        asel(o, o, [[0, n], [-16, 9]], OP.not_equal, -r, 1, w)
 
     def diag(name, c):
         n = T[name].shape[1]
-        asel(A(name), A("ST", S0, S0 + n), [[-1, n]], OP.not_equal, 0, 1, c)
+        asel(A(name), A("ZR", 0, n), [[-1, n]], OP.not_equal, 0, 1, c)
 
-    ID = A("ID", 0, 128)
-    diag("ID", 1.0)
-    iota(A("SEG"), [[0, 128], [256, 8]])
-    diag("IN", -1.0)
-    iota(A("ZR"), [[0, 800]])
-    diag("NI", -2032.0)
-    iota(A("PL", 8, 16), [[0, 8]])
-    asel(A("BO"), A("ON"), [[-16, 8], [0, 16]], OP.is_ge, 0, 1)
-    asel(A("LD"), A("ST", S0, S0 + 128), [[-16, 8], [0, 16]], OP.not_equal, -11, 1, -100.0)
-    asel(A("BO"), A("BO"), [[16, 8], [0, 16]], OP.is_ge, 15, -1)
-    asel(A("DD"), A("IN"), [[0, 8], [1, 16]], OP.is_ge, -8, 0)
-    asel(A("DG"), ID, [[0, 8], [-1, 16]], OP.is_ge, 6, 0)
-    asel(A("DG"), A("DG"), [[0, 8], [1, 16]], OP.not_equal, -3, 0)
-    diag("HI", 4096.0)
-    asel(A("TRI"), A("ON"), [[-1, 128]], OP.is_ge, 0, 1)
+    def flmat(o, d):
+        asel(A("FL", 128 * (7 * o + d - 1), 128 * (7 * o + d)), A("B0", 128 * o, 128 * o + 128), [[0, 8], [1, 16]], OP.is_ge, 1 - 8 * o - d, 0)
+
+    def build(j, f):
+        f(A("IA", 512 * j, 512 * j + 512), IND(A("ST", 0, S0), A("WO", 32 * j, 32 * j + 32)))
+
+    def mark_whole(y0):
+        mm(A("PE", 0, 64), [(A("LH", 8, 136), A("VB", y0, y0 + L, 2)), (A("LH", 0, 128), A("VB", y0 + 1, y0 + L, 2))])
+        ts(A("U1"), A("PE", 0, 64), 0.5 - 1.0 / 8192, OP.subtract)
+
+    def mark_part():
+        tt(A("U"), A("PE", 0, 64), A("U1"), OP.subtract)
+
+    def terms(a):
+        act(A("UU"), A("U"), AF.Square, -512.0, 1024.0)
+        for m in range(3):
+            lia(A("PE", 64 * m + 64, 64 * m + 128), A("U"), K(14 + m), a)
+
+    def square():
+        ts(A("UB"), A("UU"), 0.5, OP.mult, 31.0 / 64, OP.subtract)
+
+    def sums():
+        for m in range(3):
+            tt(A("UC", 64 * m, 64 * m + 64), A("PE", 64 * m + 64, 64 * m + 128), A("UB"), OP.add)
+
+    def modulo():
+        ts(A("UA"), A("UC"), 4095, OP.bitwise_and)
+
+    FEH, FV, FS = A("ZA", ZW - 24, ZW - 8), A("ZA", ZW - 8, ZW), A("ZA", 15, 143, 16)
+    ID, one, z8 = A("ID", 0, 128), A("ON", p=(0, 1)), A("ZA", ZAT["Z8"] + 15, ZAT["Z8"] + 144, 16)
+    rk, rkl, rk2 = A("RK", 0, 200, p=(0, 3)), A("RK", 400, 528, p=(0, 3)), A("RK", 200, 400, p=(0, 1))
+    kR, kG, kQ, kO, k7, kH, kP = [K(j) for j in range(7)]
+    y, stp, cur, cells = A("VB", YC, VW), A("STP", 0, L), A("ST", YC, VW), A("SO", 40, 48)
+
+    def banks():
+        mm(A("PE", 0, 16 * KW), [(cur, A("FEN"))], True, False)
+        mm(A("PV", 0, 8 * KW), [(rkl, rk)], True, False)
+
+    dma("a", A("EL", 0, 48), H(T.e0[:, :]))
+    dma("s", A("EL", 48, 96), H(T.h0[:, :]))
+    dma("a", A("VB", 0, L), H(T.v0[:, 0:L]))
+    for h in range(2):
+        dma("sa"[h], A("WL", 128 * h, 128 * h + 128), H(T.w0[h::2, :]))
+    dma("s", A("XB", 0, 2048), H(T.x0[:, 0:2048]))
+    iota(A("PI", 0, 1), [[0, 1]], 0, 1)
+    iota(A("IO"), [[1, 144]])
+    iota(A("KI", 0, 16), [[16, 8], [128, 2]])
+    iota(A("I8"), [[1, 17], [0, 8]])
+    iota(A("NP", 240, 288), [[0, 48]], 8)
+    iota(A("KI", 16, 32), [[2, 16]])
+    iota(kP, [[0, 1]], 0, 1)
+    iota(A("SEG", 0, 256), [[0, 32], [256, 8]])
+    ms(A("ZR"), 0.0)
+    act(A("ST", 0, S0), A("ZR", 0, S0))
+    p_ = A("PI", 0, 1)
+    ts(A("PJ", 0, 1), p_, 15, OP.bitwise_and)
+    ts(A("PJ", 1, 2), p_, 4, OP.logical_shift_right)
+    ts(A("PJ", 2, 3), p_, 124, OP.bitwise_and)
+    ts(A("PJ", 3, 4), p_, 4, OP.logical_shift_right, 1, OP.bitwise_and)
+    ts(A("PJ", 4, 5), p_, 7, OP.bitwise_and)
+    ts(A("PJ", 5, 6), p_, 3, OP.logical_shift_right, 1, OP.bitwise_and)
+    ms(A("ON"), 1.0)
+    cp(A("K", 0, 6), A("PJ", 0, 6))
+    lia(K(10), kR, 1.5)
+    lia(K(8), kR, 2.0 / 4096, 1.0 / 4096)
+    lia(K(9), kG, 2.0, 1.0)
+    act(A("NP", 192, 240), A("ZR", 0, 48), bias=K(10))
+    act(A("K", 11, 14), A("IO", 0, 24, 8), bias=k7)
+    lia(K(7), k7, 32.0, kH)
+    act(A("K", 14, 17), A("K", 11, 14), AF.Square, bias=0.5)
+    ts(A("KO", 0, 16), A("KI", 0, 16), kR, OP.add)
+    ts(A("DM", 0, 16), A("IO", 0, 16), kR, OP.is_equal)
+    ts(A("CM"), A("IO", 0, 8), kG, OP.is_equal)
+    ts(A("E1", 0, 96), A("EL"), 5, OP.logical_shift_right)
+    ts(A("E1", 96, 192), A("EL"), 31, OP.bitwise_and)
+    ts(A("LH"), A("I8"), K(9), OP.is_equal, K(8), OP.mult)
+    cp(A("NP", 0, 192), A("E1"))
+    dma("s", A("ST", 0, S0, p=(9, 128, 16)), A("IO", 0, 48), True)
+    for j, row, q in ((5, 2, "s"), (4, 8, "s"), (0, 0, "a"), (1, 4, "s"), (2, 1, "a"), (3, 5, "s")):
+        dma(q, A("ST", 0, S0, p=(row, 128, 16)), A("NP", 48 * j, 48 * j + 48), True)
+    dma("a", A("XB", 2048, C), H(T.x0[:, 2048:C]))
+    lia(A("K", 14, 17), A("K", 14, 17), 4096.0, 4096 * 128.75)
+    lia(A("G8"), A("CM"), -8192.0)
+    dma("s", A("VB", L, S0), H(T.v0[:, L:S0]))
+    for j in range(1, 4):
+        dma("s", A("SEG", 256 * j, 256 * j + 256), A("SEG", 0, 256))
+    dma("s", cur, A("ST", 0, L))
+    dma("s", A("ZA", 144, ZW - 24), A("ZR"))
+    dma("s", y, H(T.v0[:, 0:L]))
+    dma("s", A("TH", 0, 3), H(T.th[:, :]))
+    for j in range(1, 8):
+        dma("s", A("DM", 16 * j, 16 * j + 16), A("DM", 0, 16))
+    dma("s", A("VB", S0, YC), A("ZR", 0, YC - S0))
+    dma("s", A("ST", S0, DUM), A("ZR", 0, DUM - S0))
     for o in range(2):
         zero(o, 4)
+    dma("s", A("SCM"), A("ZR", 0, 784))
+    dma("s", A("SCM", p=(7, 128, 8)), A("ON", 0, 98))
+    cp(A("W1"), IND(A("WL"), A("KO", 0, 16)))
+    mark_whole(0)
+    ts(A("KO", 16, 32), A("KI", 16, 32), K(7), OP.add)
+    run("v", lambda: g.vector.transpose(T.W2[:, :], T.W1[:, :]), A("W2"), [A("W1")])
+    mark_part()
+    lia(K(31), kP, 8.0)
+    act(K(32), kP, bias=float(DUM))
+    terms(None)
+    cp(A("WO"), IND(A("W2"), A("KO", 16, 32)))
+    square()
+    act(K(53), O(1), bias=O(5))
+    lia(K(56), O(2), 12.0, O(11))
+    lia(K(58), O(2), -1.0, O(6))
+    lia(K(59), O(8), 24.0, O(3))
+    lia(K(56), O(6), 8.0, K(56))
+    lia(K(33), O(0), 128.0)
+    lia(K(61), K(58), 4.0, K(59))
+    sums()
+    asel(A("ZA", 0, 144), A("ZR", 0, 144), [[-16, 9], [200, 16]], OP.not_equal, -3008, 1, 32.0)
+    asel(FEH, A("ZR", 0, 16), [[-4, 2], [-16, 8]], OP.not_equal, 0, 1, 32.0)
+    asel(FV, A("ZR", 0, 8), [[-16, 8]], OP.not_equal, -8, 1, 32.0 / 4096)
+    weigh("ZS", 1, 9, 1.0)
+    asel(FEH, FEH, [[-4, 2], [-16, 8]], OP.not_equal, -1, 1, 1.0)
+    asel(FV, FV, [[-16, 8]], OP.not_equal, -9, 1, 1.0 / 4096)
+    iota(rk, [[0, 8], [-1, KW]], KW - 1)
+    asel(FEH, FEH, [[-4, 2], [-16, 8]], OP.not_equal, -2, 1, -0.125)
+    asel(rk, rk, [[0, 200]], OP.is_equal, -1, 1)
+    iota(A("I24"), [[4, 2], [16, 8], [0, KW]])
+    asel(rk, rk, [[0, 8], [1, KW]], OP.is_ge, -17, 100, 1016.0)
+    asel(rkl, A("IO", 0, L, p=(0, 3)), [[0, L]], OP.is_equal, -2, 1, 1.0)
+    asel(rk, rk, [[0, 8], [1, KW]], OP.is_ge, -9, 100, 2032.0)
+    iota(A("KI", 32, 40), [[KW, 8]], KW - 1)
+    for j, c in enumerate((3072.0, GM - 3072 + YC / 4096, 1 / 4096)):
+        o = A("RK", 0, 200, KW, p=(0, 3))
+        asel(o, o, [[0, 8]], OP.not_equal, -j, 1, c)
+        if j < 2:
+            iota((A("KI", 40, 48), A("PL", 8, 16))[j], [[1 - j, 8]])
+    asel(rk2, A("ZR", 0, 200, p=(0, 1)), [[0, 8], [1, KW]], OP.is_gt, 0, 0, -2.0 ** 19)
+    diag("ID", 1.0)
+    diag("IN", -1.0)
+    diag("HI", 4096.0)
+    asel(A("BO"), A("ON"), [[-16, 8], [0, 16]], OP.is_ge, 0, 1)
+    iota(z8, [[-256, 9]], 8, 16)
+    asel(A("BO"), A("BO"), [[16, 8], [0, 16]], OP.is_ge, 15, -1)
+    asel(z8, z8, [[-16, 9]], OP.is_ge, 0, 1)
+    asel(A("LD"), A("ZR", 0, 128), [[-16, 8], [0, 16]], OP.not_equal, -11, 1, -100.0)
+    asel(z8, z8, [[16, 9]], OP.is_ge, 15, -1)
+    asel(A("DG"), ID, [[0, 8], [-1, 16]], OP.is_ge, 6, 0)
+    weigh("ZE", 3, 0, 32.0)
+    asel(A("DG"), A("DG"), [[0, 8], [1, 16]], OP.not_equal, -3, 0)
+    weigh("ZE", 3, 1, 1.0)
+    asel(A("DD"), A("IN"), [[0, 8], [1, 16]], OP.is_ge, -8, 0)
+    weigh("ZE", 1, 2, 256.0)
+    asel(A("IX"), ID, [[0, 8], [1, 16]], OP.not_equal, -10, 0)
+    run("v", lambda: g.vector.tensor_reduce(K(54)[0], FEH[0], AxisListType.X, OP.add, negate=True), K(54), [FEH])
+    modulo()
+    build(0, act)
+    build(2, cp)
+    cp(A("AO"), A("UA"))
+    build(1, act)
+    build(4, cp)
+    build(3, act)
+    build(6, cp)
+    build(5, act)
+    build(7, cp)
+    ts(A("FEN"), A("I24"), kQ, OP.is_equal, K(54), OP.mult)
+    banks()
 
-    def consts_first():
-        lin(A("G8"), A("CM"), -8192.0)
-        lin(A("FS"), A("CM"), K(38))
-        ts(K(32), kP, float(DUM), OP.add)
-        cp(A("VB", YC, VW), A("VB", 0, L))
-
-    def consts_leaders():
-        ts(K(53), O(1), O(5), OP.add)
-        lin(K(56), O(2), 12.0, O(11))
-        lin(K(58), O(2), -1.0, O(6))
-        lin(K(59), O(8), 24.0, O(3))
-        lin(K(56), O(6), 8.0, K(56))
-        lin(K(28), K(20), 256.0, K(26))
-        lin(K(61), K(58), 4.0, K(59))
-        lin(K(40), K(22), K(28))
-        lin(K(33), O(0), 128.0)
-        ts(A("LN", 0, 8), A("IO", 0, 128, 16), kR, OP.add)
-        lia(A("ST", DUM, YC), A("IO", 0, 128), K(53), K(56))
-        lin(A("LN", 8, 16), A("LN", 0, 8), 32.0)
-        ts(A("LN", 16, 24), A("LN", 0, 8), float(DUM), OP.add)
-        lia(A("ZM"), A("Z0"), K(8))
-        lin(A("CT", 0, 128), A("IO", 0, 128), O(9), K(61))
-        lia(A("Z8"), A("ZM"), 8.0)
-        lin(A("ZE"), A("Z0"), K(40))
-
-    def consts_rounds():
-        lin(K(34), K(38), K(60))
-        for t in range(1, NT):
-            lin(K(61 + t), K(58), float(4 >> t), K(59))
-        lin(K(55), K(34), -1.0, K(38))
-        for t in range(1, NT):
-            lin(K(61 + t), O(8), 4.0 * t, K(61 + t))
-        for j, (k, w) in enumerate(((55, 1.0), (34, 1.0), (55, -1.0), (34, -1.0))):
-            ts(A("SEL", 128 * j, 128 * j + 128), A("ON"), K(k), OP.mult, w, OP.mult)
-
-    def consts_masks():
-        ts(K(12), O(7), O(15), OP.add)
-        lin(K(10), kH, -1.0, 1.0)
-        lin(K(9), K(12), 2.0, -1.0)
-        lin(K(17), K(12), 8.0, 99.0)
-        lin(K(10), K(10), K(9))
-        lin(K(17), k7, -1.0, K(17))
-        lin(K(9), kH, K(9))
-
-    def consts_places():
-        for nm, ws in (("ZP", ((0, 32.0), (1, 1.0), (3, 1.0))), ("ZQ", ((4, 32.0), (5, 1.0)))):
-            iota(A(nm), [[0, 144]])
-            for r, w in ws:
-                asel(A(nm, 15, 144, 16), A(nm, 15, 144, 16), [[-16, 9]], OP.not_equal, -r, 1, w)
-        asel(A("ZF"), A("ZE"), [[0, 144]], OP.is_equal, 0, 0)
-        asel(A("ZF", 15, 144, 16), A("ZF", 15, 144, 16), [[-16, 9]], OP.not_equal, -2, 1, 512.0)
-        asel(A("HN"), A("ZR", 0, 128), [[-1, 128]], OP.not_equal, 0, 1, -100.0)
+    def later_constants():
+        weigh("ZP", 1, 3, 1.0)
+        asel(A("B0", 128, 256), A("ON"), [[-16, 8], [0, 16]], OP.is_equal, 0, 1)
+        weigh("ZQ", 1, 4, 32.0)
+        asel(A("B0", 0, 128), A("B0", 128, 256), [[0, 8], [-1, 16]], OP.is_ge, 7, 0)
+        weigh("ZQ", 1, 5, 1.0)
         asel(A("B7"), A("ON"), [[0, 16], [1, 8]], OP.not_equal, -7, 0)
+        weigh("ZF", 1, 2, 512.0)
+        for d in (4, 2, 6):
+            flmat(0, d)
+            flmat(1, d)
+        diag("HN", -100.0)
         for o in range(2):
             asel(A("LO", 128 * o, 128 * o + 128), A("B7"), [[-16, 8], [0, 16]], OP.is_equal, -2 - 4 * o, 1)
-        asel(A("B0", 128, 256), A("ON"), [[-16, 8], [0, 16]], OP.is_equal, 0, 1)
-        asel(A("B0", 0, 128), A("B0", 128, 256), [[0, 8], [-1, 16]], OP.is_ge, 7, 0)
 
-    def build(j, q):
-        o, i = A("IA", 512 * j, 512 * j + 512), IND(A("ST", 0, S0), A("WO", 32 * j, 32 * j + 32))
-        (act if q == "a" else cp)(o, i)
+    small = [lambda: lin(K(77), O(9), 256.0, O(10)), lambda: lin(K(62), K(58), 2.0, K(59)), lambda: lin(K(77), O(8), 8192.0, K(77)),
+             lambda: lin(K(62), O(8), 4.0, K(62)), lambda: lin(K(34), K(77), kO), lambda: lin(K(63), K(58), 1.0, K(59)),
+             lambda: lin(K(55), K(34), -1.0, K(77)), lambda: lin(K(63), O(8), 8.0, K(63))]
+    for j, k, w in ((1, 34, 1.0), (3, 34, -1.0), (0, 55, 1.0), (2, 55, -1.0)):
+        small.append(lambda j=j, k=k, w=w: ts(A("SEL", 128 * j, 128 * j + 128), A("ON"), K(k), OP.mult, w, OP.mult))
+    small += [lambda: ts(K(12), O(7), O(15), OP.add), lambda: lin(K(10), kH, -1.0, 1.0), lambda: lin(K(9), K(12), 2.0, -1.0),
+              lambda: lin(K(17), K(12), 8.0, 99.0), lambda: lin(K(10), K(10), K(9)), lambda: lin(K(17), k7, -1.0, K(17)),
+              lambda: lin(K(9), kH, K(9)), lambda: lin(A("BOH", 0, 128), A("BO"), K(10)), lambda: lin(A("BOH", 128, 256), A("BO"), K(9))]
 
-    consts_first()
-    offsets(0)
-    ts(A("DM"), A("IM"), kR, OP.is_equal)
-    cp(K(60), A("PJ", 7, 8))
-    ts(A("FEN"), A("I24"), K(52), OP.is_equal, K(54), OP.mult)
-    for j in range(8):
-        build(j, BUILD[j])
-    cp(A("ST", YC, VW), A("ST", 0, L))
+    def fill(n):
+        for f in small[:n]:
+            f()
+        del small[:n]
 
     peers = [T.cores[(rank - d) % N] for d in range(1, N)]
     SB = ("P4", "P5", "P4")
-    one = A("ON", p=(0, 1))
 
-    def gx(lo, hi, q):
-        (act if q == "a" else cp)(A("GX", 16 * lo, 16 * hi), IND(A("XB"), A("AO", lo, hi)))
+    def gx(lo, hi, f):
+        f(A("GX", 16 * lo, 16 * hi), IND(A("XB"), A("AO", lo, hi)))
 
     def gi(m):
         act(A("GB", 1024 * m, 1024 * m + 1024), IND(A("IA"), A("AO", 64 * m, 64 * m + 64)))
-        if m == 0:
-            mm(A("PE", 0, 16 * KW), [(A("ST", YC, VW), A("FEN"))], True, False)
-            mm(A("PV", 0, 8 * KW), [(one, rk[0]), (one, rk[3]), (A("OI", p=(0, 1)), rk[1])], True, False)
         wrap(A(SB[m], 0, 64), "ZS", "GB", 1024 * m, 64)
+
+    def labels(m, bank, w, width):
         for kk in range(8):
             k = 8 * m + kk
-            l = A("GB", 1024 * m + kk, 1024 * m + 1024, 8)
-            mm(A("PE", KW - 1 - k, 16 * KW, KW), [(l, A("FEH"))], False, k == 23, k == 0)
-            mm(A("PV", KW - 1 - k, 8 * KW, KW), [(l, A("FV"))], False, k == 23, k == 0)
+            mm(A(bank, KW - 1 - k, width * KW, KW), [(A("GB", 1024 * m + kk, 1024 * m + 1024, 8), w)], False, k == 23, k == 0)
 
     def sl(m):
         cp(A("SL", 64 * m, 64 * m + 64), A(SB[m], 0, 64))
-        calls[-1]["heavy"] = True
 
-    def gv(m, c0=0, c1=64):
+    def gv(t, m, c0=0, c1=64):
         lo, hi = 64 * m + c0, 64 * m + c1
-        tt(A("GB", BT + 16 * lo, BT + 16 * hi), IND(A("VB", 0, 1152), A("SL", lo, hi)), A("GX", 16 * lo, 16 * hi), OP.is_gt)
+        tt(A("GB", BT + 16 * lo, BT + 16 * hi), IND(A("VB", 0, S0 + L * t), A("SL", lo, hi)), A("GX", 16 * lo, 16 * hi), OP.is_gt)
 
     def mx(m):
         o = A("GB", MS + 1024 * m, MS + 1024 * m + 1024) if m < 2 else A("GX", GM - 7, GM + 1017)
         scan(o, A("SEG"), A("GX", 1024 * m, 1024 * m + 1024), OP.min, OP.max)
 
     def count(m):
-        if m == 0:
-            mm(A("P5", 0, 8 * KW), [(one, rk[2])], True, False)
         for kk in range(8):
             k = 8 * m + kk
             mm(A("P5", KW - 1 - k, 8 * KW, KW), [(A("GB", BT + 1024 * m + kk, BT + 1024 * m + 1024, 8), A("G8"))], False, k == 23, k in (0, 16))
 
-    def parallel():
-        act(A("SG"), A("PE", 0, 16 * KW), AF.Sign, bias=0.0625)
-        mm(A("P4", 256, 256 + 8 * KW), [(ID, A("SG", 0, 8 * KW)), (ID, A("SG", 8 * KW, 16 * KW))])
-        act(A("VL"), A("PV", 0, 8 * KW), bias=K(31))
-        act(A("NPB"), A("P4", 256, 256 + 8 * KW), AF.Abs, scale=29.0 * 4096, bias=93.0 * 1024)
-        calls[-1]["heavy"] = True
-
-    def fold(ds, start, stop, first=()):
+    def fold(ds, halves=(0, 1), start=False, stop=False, first=()):
         prs = list(first) + [(A("FL", 128 * (7 * o + d - 1), 128 * (7 * o + d)), plane(o, d)[0], plane(o, d)[1] - 1 + o) for (o, d) in ds]
-        for n, (l, nm, c0) in enumerate(prs):
-            mm(A("P0"), [(l, A(nm, c0, c0 + 512))], start and n == 0, stop and n == len(prs) - 1)
-            mm(A("P1", 0, 257), [(l, A(nm, c0 + 512, c0 + 769))], start and n == 0, stop and n == len(prs) - 1)
-
-    def places():
-        ts(A("S2", 32, 64), A("S2", 0, 32), PW - 1, OP.bitwise_and)
-        for t in range(1, NT):
-            ts(A("PO", 48 + 8 * t, 56 + 8 * t), A("S2", 16 + 16 * t, 24 + 16 * t), 1.0, OP.add)
-            cp(A("PO", 120 + 8 * t, 128 + 8 * t), A("S2", 24 + 16 * t, 32 + 16 * t))
+        for h in halves:
+            for n, (l, nm, c0) in enumerate(prs):
+                mm(A(("P0", "P1")[h], 0, (512, 257)[h]), [(l, A(nm, c0 + 512 * h, c0 + (512, 769)[h]))], start and n == 0, stop and n == len(prs) - 1)
 
     def flags(t, o):
         nm, lo, hi, unit = TABLE[t][o]
-        cp(IND(A(nm, lo, hi), A("SO", 48 + 8 * o, 56 + 8 * o)), A("SP", 128 * t, 128 * t + 128))
+        cp(IND(A(nm, lo, hi), A("SQ", 16 * t + 8 * o, 16 * t + 8 * o + 8)), A("SP", 128 * t, 128 * t + 128))
 
-    def masks(lo, hi, bank):
-        ps = [A(bank, 256 * o, 256 * o + hi - lo) for o in range(2)]
+    def masks_p(lo, hi, bank):
         for o in range(2):
-            mm(ps[o], [(A("LO", 128 * o, 128 * o + 128), A("ST", S0 + lo, S0 + hi)), (A("HN"), A("SP", lo, hi))])
+            mm(A(bank, 256 * o, 256 * o + hi - lo), [(A("LO", 128 * o, 128 * o + 128), A("ST", S0 + lo, S0 + hi)), (A("HN"), A("SP", lo, hi))])
+
+    def masks_a(lo, hi, bank):
         for o in range(2):
-            act(A("MA", 384 * o + lo, 384 * o + hi), ps[o], AF.Abs, bias=K(17))
+            act(A("MA", 384 * o + lo, 384 * o + hi), A(bank, 256 * o, 256 * o + hi - lo), AF.Abs, bias=K(17))
+
+    def masks_m(lo, hi):
+        for o in range(2):
             act(A("MM", 384 * o + lo, 384 * o + hi), A("MA", 384 * o + lo, 384 * o + hi), AF.Relu, bias=1.0, scale=-1.0)
 
-    def flmat(o, d):
-        asel(A("FL", 128 * (7 * o + d - 1), 128 * (7 * o + d)), A("B0", 128 * o, 128 * o + 128), [[0, 8], [1, 16]], OP.is_ge, 1 - 8 * o - d, 0)
-
     for t in range(NT):
-        last = t == NT - 1
-        land, arr = "LD%d" % t, ("arr%d" % t, 0, 1)
+        first, last = t == 0, t == NT - 1
+        land, arr = "LD%d" % t, "arr%d" % t
+        ct, sp, n0 = A("CT", 128 * t, 128 * t + 128), A("SP", 128 * t, 128 * t + 128), S0 + L * t
         gi(0)
-        gx(0, 64, "v")
-        if t == 1:
-            for d in (2, 6):
-                zero(0, d, [("arr0", 0, 1)])
-                zero(1, d)
-            zero(0, 5)
-            dma("s", A("SCM", p=(7, 128, 8)), A("ON", 0, 98))
-        if t == 2:
-            for o in range(FL1, 2):
-                flags(1, o)
-        gx(64, XA[t], "v")
+        gx(0, 64, cp)
+        gx(64, XA[t], cp)
+        labels(0, "PE", FEH, 16)
+        labels(0, "PV", FV, 8)
         sl(0)
+        if first:
+            cp(A("KO", 32, 48), A("KI", 32, 48))
         gi(1)
-        gv(0)
-        gx(XA[t], 128, "a")
+        gv(t, 0)
+        labels(1, "PE", FEH, 16)
+        labels(1, "PV", FV, 8)
+        gx(XA[t], 128, act)
         sl(1)
         mx(0)
-        if t == 2:
-            fold([(0, 4), (1, 4)], True, False, [(ID, "SCM", 0)])
+        mm(A("P5", 0, 8 * KW), [(one, rk2)], True, False)
         gi(2)
-        gv(1)
+        gv(t, 1)
+        labels(2, "PE", FEH, 16)
         count(0)
-        count(1)
-        if t == 1:
-            wrap(A("P0", 0, 56), "ZP", "ST", 0, 56)
-            wrap(A("P0", 56, 112), "ZQ", "ST", 0, 56)
-        if t == 2:
-            fold([(0, 2), (0, 6)], False, False)
-        gx(128, 160, "a")
-        gx(160, 192, "a")
+        labels(2, "PV", FV, 8)
+        gx(128, 160, act)
+        gx(160, 192, act)
         sl(2)
         mx(1)
-        gv(2, 0, 32)
-        parallel()
+        count(1)
+        if last:
+            dma("s", A("AE", 1008, 4880, p=(0, 128, 16)), A("ZR", 0, 242))
+        gv(t, 2, 0, 32)
+        act(A("SG"), A("PE", 0, 16 * KW), AF.Sign, bias=0.0625)
+        mm(A("P4", 256, 256 + 8 * KW), [(ID, A("SG", 0, 8 * KW)), (ID, A("SG", 8 * KW, 16 * KW))])
+        act(A("VL"), A("PV", 0, 8 * KW), bias=K(31))
         ma, mb, mc = A("GB", MS + 7, MS + 1024, 8), A("GB", MS + 1031, MS + 2048, 8), A("GX", GM, GM + 1017, 8)
         r1, r2 = A("MT", 0, 128), A("MT", 128, 256)
         mm(A("PE", 0, 128), [(ID, ma), (A("IN"), mb)])
+        act(A("NPB"), A("P4", 256, 256 + 8 * KW), AF.Abs, scale=29.0 * 4096, bias=93.0 * 1024)
         act(r1, A("PE", 0, 128), AF.Relu)
-        gv(2, 32, 64)
+        gv(t, 2, 32, 64)
         mm(A("P5", 0, 8 * KW), [(ID, A("NPB"))], False, False, True)
+        mm(A("PE", 128, 256), [(ID, r1), (ID, mb)])
         count(2)
         mx(2)
-        if t == 0:
-            consts_leaders()
-        if t == 1:
-            consts_masks()
         if last:
-            masks(0, 256, "P6")
-        mm(A("PE", 128, 256), [(ID, r1), (ID, mb)])
+            dma("s", A("GB", 0, 3856, p=(0, 128, 16)), A("ZR", 0, 241))
+            masks_p(0, 256, "P6")
         act(r2, A("PE", 128, 256))
-        if last:
-            dma("s", A("AE", 1008, 4880, p=(0, 128, 16)), A("ZR", 0, 242), lag=3.5)
-            dma("s", A("GB", 0, 3856, p=(0, 128, 16)), A("ZR", 0, 241), lag=3.5)
+        if first:
+            lia(A("TN"), A("TH", 0, 3), -1.0, 0.5)
+            lia(A("ST", DUM, YC), A("IO", 0, 128), K(53), K(56))
         scan(A("SC"), A("P5", 0, 8 * KW), A("VL"), OP.min, OP.max)
         tt(A("D1"), IND(A("SC"), A("KO", 32, 40)), A("DM"), OP.mult)
-        calls[-1]["heavy"] = True
-        ts(A("NR"), A("SC", KW - 1, 8 * KW, KW), 3072.0, OP.is_ge)
-        calls[-1]["heavy"] = True
+        act(A("NR", 8, 16), A("SC", KW - 1, 8 * KW, KW), AF.Relu, 3072.0, -1.0)
+        if t:
+            act(A("NR", 0, 8), A("SC", KW - 1, 8 * KW, KW), AF.Relu, -3072.0)
         mm(A("P4", 0, 8), [(A("D1"), A("CM"))])
         tt(mc, mc, r2, OP.max)
-        calls[-1]["heavy"] = True
-        mm(A("P7", 0, 8), [(A("ST", YC, VW), A("FS")), (one, A("RK", 1, 9, p=(0, 1))), (A("NI"), A("NR"))], True, t == 0)
+        mm(A("P7", 0, 8), [(cur, FS), (A("HI"), A("NR", 8, 16))], True, first)
+        if not last:
+            act(A("SR"), IND(A("SC"), A("KO", 32, 40)), AF.Sign, bias=-3071.9)
+            mm(A("PV", 0, 1), [(A("SR"), A("ON", 0, 1))])
         if t:
             for gg in range(8):
                 mm(A("P7", gg, gg + 1), [(A("EQ", 128 * gg, 128 * gg + 128), A("NR", gg, gg + 1))], False, gg == 7, gg == 0)
+        if first:
+            lia(ct, A("IO", 0, 128), O(9), K(61))
+            act(A("LN", 0, 8), A("IO", 0, 128, 16), bias=kR)
+            lia(A("LR"), A("IO", 0, L), O(10))
+        if last:
+            masks_a(0, 256, "P6")
+            masks_m(0, 256)
+            fold([(1, 2), (1, 6)])
+        else:
+            lia(A("AC", 0, 1), A("PV", 0, 1), -0.5, 64.0)
+        if t == 1:
+            wrap(A("P0", 0, 56), "ZP", "ST", 0, 56)
+            wrap(A("P0", 56, 112), "ZQ", "ST", 0, 56)
         cp(A("SI", 8, 16), A("P4", 0, 8))
         cp(A("SO", 8, 16), A("P4", 0, 8))
         tt(A("SF"), A("P4", 0, 8), A("SI", 8, 16), OP.subtract)
@@ -654,137 +549,162 @@ def rank_program(g, core, T, topo):
         lin(A("SO", 16, 24), A("SF"), 4096.0)
         ts(A("PL", 0, 8), A("P7", 0, 8), K(32), OP.min)
         tt(A(land, 0, L), IND(A("VB"), A("SO", 16, 24)), A("G1"), OP.subtract)
+        act(A("BS"), IND(A("ST"), A("SO", 16, 24)))
         trs = []
         for d in range(1, N):
             dst = peers[d - 1]
             rid, pid, _ = topo.addr(dst)
             trs.append(RemoteDMATransfer(dst_ids=[DstId(rid=rid, pnc=pid)], dma_engine_mask=1 << topo.engines(core, dst)[d - 1],
-                                         remote_sem=T.sem[arr[0]], src=T[land][:, 0:L], dst=T[land][:, L * d:L * d + L]))
-        record("g", lambda trs=trs: g.remote_dma_fused(trs, local_sem=T.sem.sent), [(land, 0, L)], [arr], 0.3, TRAVEL[t], "send", hold=HOLD[t])
-        y, stp, cur = A("VB", YC, VW), A("STP", 0, L), A("ST", YC, VW)
-        ct = A("CT", 128 * t, 128 * t + 128)
-        n0 = S0 + L * t
-        sp = A("SP", 128 * t, 128 * t + 128)
+                                         remote_sem=T.sem[arr], src=T[land][:, 0:L], dst=T[land][:, L * d:L * d + L]))
+        order("g", [(land, 0, L)], [])
+        g.remote_dma_fused(trs, local_sem=T.sem.sent)
+        cnt["sent"] += N - 1
+        if first:
+            later_constants()
         if t == 1:
-            cp(A("PO", 0, 56), A("P0", 0, 56))
-            cp(A("PO", 72, 128), A("P0", 56, 112))
-            for o in range(2):
-                lin(A("BOH", 128 * o, 128 * o + 128), A("BO"), K(10 - o))
-        if t == 2:
-            fold([(1, 2), (1, 6)], False, False)
+            for d in (1, 3, 5, 7):
+                flmat(0, d)
+                flmat(1, d)
+            iota(A("TT", 768, 784), [[0, 16]])
         tt(A("D2"), IND(A("PL"), A("KO", 40, 48)), A("DM"), OP.mult)
         act(y, A(land, 0, L), AF.Abs)
         mm(A("P6", 256, 264), [(A("D2"), A("CM"))])
-        ts(A("WB"), y, A("TH", t, t + 1), OP.is_ge)
+        fill(4)
+        if t == 1:
+            cp(A("PO", 0, 56), A("P0", 0, 56))
+            cp(A("PO", 72, 128), A("P0", 56, 112))
         cp(A("SO", 24, 32), A("P6", 256, 264))
-        act(stp, IND(A("ST"), A("SO", 24, 32)))
+        act(A("WB"), y, AF.Sign, A("TN", t, t + 1))
+        fill(2)
         if not last:
-            act(A("SR"), IND(A("SC"), A("KO", 32, 40)), AF.Sign, bias=-3071.9)
-            mm(A("PV", 0, 1), [(A("SR"), A("ON", 0, 1))])
-            lia(A("AC", 0, 1), A("PV", 0, 1), -0.5, 64.0)
-            offsets(t + 1)
+            mark_whole(YC)
+        act(stp, IND(A("ST"), A("SO", 24, 32)))
         wrap(A("P4", 64, 72), "Z8", "VB", YC, 8)
-        act(A("BS"), IND(A("ST"), A("SO", 16, 24)))
+        fill(2)
         if last:
             tt(A("DF"), IND(A("VB", 0, YC), A("SO", 24, 32)), y, OP.subtract)
-        cp(A("SI", 32, 40), A("P4", 64, 72))
-        ts(A("SI", 24, 32), A("SI", 32, 40), 896, OP.bitwise_and)
-        tt(A("SI", 32, 40), A("SI", 24, 32), A("LN", 0, 8), OP.add)
-        cp(A("SO", 32, 40), A("SI", 32, 40))
+        else:
+            mark_part()
+            terms(A("AC", 0, 1))
         mm(A("P5", 0, 128), [(A("BO"), A("WB")), (A("LD"), stp)])
         mm(A("PV", 128, 256), [(A("ID", 4, 132), stp)])
         mm(A("P7", 0, 128), [(A("DD"), stp), (ID, ct)])
         mm(A("P6", 0, 128), [(A("DG"), stp), (ID, ct)])
-        ts(sp, A("P5", 0, 128), 7.5, OP.is_ge)
+        fill(2)
+        cp(A("SI", 32, 40), A("P4", 64, 72))
+        ts(sp, A("P5", 0, 128), -0.5, OP.is_ge)
         act(A("STP", 128, 256), A("PV", 128, 256))
+        ts(A("SI", 24, 32), A("SI", 32, 40), 896, OP.bitwise_and)
         tt(A("M1"), A("P7", 0, 128), sp, OP.mult)
-        mm(A("P5", 0, 128), [(ID, A("BS")), (ID, A("M1"))])
-        act(A("ST", n0, n0 + L), A("P6", 0, 128))
-        act(cur, A("P5", 0, 128))
         if last:
             wrap(A("PV", 256, 272), "ZF", "STP", 0, 16)
+            act(A("ST", n0, n0 + L), A("P6", 0, 128))
+            tt(A("SI", 32, 40), A("SI", 24, 32), A("LN", 0, 8), OP.add)
+            tt(A("DF"), A("DF"), sp, OP.mult)
+            cp(A("SQ", 16 * t, 16 * t + 16), A("PV", 256, 272))
+            cp(A("SO", 32, 40), A("SI", 32, 40))
+            mm(A("P5", 0, 128), [(A("IX"), A("BS")), (ID, A("M1"))])
+            mm(A("P4", 128, 256), [(ID, y), (A("HI"), sp)])
+            masks_p(256, 384, "P7")
+            flags(t, 0)
+            flags(t, 1)
+            act(A("VB", n0, n0 + L), A("P4", 128, 256), AF.Relu, bias=-4096.0)
+            act(cur, A("P5", 0, 128))
+            fold([(0, d) for d in (1, 3, 5, 7)], (0,))
+            masks_a(256, 384, "P7")
+            tt(IND(A("VB", 0, YC), A("SO", 24, 32)), A("DF"), y, OP.add)
+            dma("s", H(T.yv[:, :]), A("VB", 0, 1152))
+            cp(A("S2", 0, 32), A("SQ", 16, 48))
+            masks_m(256, 384)
+            ts(A("S2", 32, 64), A("S2", 0, 32), PW - 1, OP.bitwise_and)
         else:
-            lin(A("STP", 256, 384), sp, K(33))
+            lia(A("STP", 256, 384), sp, K(33))
+            mm(A("P5", 0, 128), [(A("IX"), A("BS")), (ID, A("M1")), (ID, A("LR"))])
+            mm(A("P4", 128, 256), [(ID, y), (A("HI"), sp)])
             wrap(A("PV", 256, 280), "ZE", "STP", 0, 24, False)
             mm(A("PV", 272, 280), [(A("D2"), A("CM"))], False, True, True)
-        mm(A("P4", 128, 256), [(ID, y), (A("HI"), sp)])
-        cp(A("SO", 48, 64), A("PV", 256, 272))
-        act(A("VB", n0, n0 + L), A("P4", 128, 256), AF.Relu, bias=-4096.0)
-        if t:
-            cp(A("S2", 16 * t - 16, 16 * t), A("PV", 256, 272))
-
-        def arrive():
-            win = A(land)
-            act(A("ZZ"), IND((win[0], win[1] + [arr]), A("SO", 32, 40)), AF.Abs)
-            wrap(A("P4", 72, 80), "ZM", "ZZ", 0, 8)
-            cp(A("SI", 40, 48), A("P4", 72, 80))
-            ts(A("SI", 48, 56), A("SI", 40, 48), 31, OP.bitwise_and)
-            tt(A("SI", 40, 48), A("SI", 48, 56), A("LN", 8, 16), OP.add)
-            cp(A("SO", 40, 48), A("SI", 40, 48))
-
-        if not last:
+            tt(A("SI", 32, 40), A("SI", 24, 32), A("LN", 0, 8), OP.add)
+            square()
+            cp(A("SO", 32, 40), A("SI", 32, 40))
+            sums()
+            fill(2)
+            modulo()
+            fill(4)
+            act(cur, A("P5", 0, 128))
+            if first:
+                act(A("LN", 16, 24), A("LN", 0, 8), bias=float(DUM))
+                act(A("LN", 8, 16), A("LN", 0, 8), bias=31.0 / 64)
+                lia(A("ZA", ZAT["ZM"] + 15, ZAT["ZM"] + 144, 16), z8, 1.0 / 256)
+            act(A("ST", n0, n0 + L), A("P6", 0, 128))
+            act(A("VB", n0, n0 + L), A("P4", 128, 256), AF.Relu, bias=-4096.0)
+            cp(A("AO"), A("UA"))
             tt(A("SI", 56, 64), A("PV", 272, 280), A("LN", 16, 24), OP.min)
-            if t == 0:
-                consts_rounds()
-            lia(A("CT", 128 * t + 128, 128 * t + 256), A("IO", 0, 128), O(9), K(62 + t))
+            cp(A("SQ", 16 * t, 16 * t + 16), A("PV", 256, 272))
             cp(A("SO", 0, 8), A("SI", 56, 64))
-            cp(IND(A("VB", 0, YC), A("SO", 0, 8)), y)
-            for o in range(FL1 if t else 2):
-                flags(t, o)
+            lia(A("CT", 128 * t + 128, 128 * t + 256), A("IO", 0, 128), O(9), K(62 + t))
             for gg in (0, 1, 4, 5, 2, 3, 6, 7):
                 rows = (32 * (gg // 2), 32 * (gg // 2) + 32)
                 s, sn = (A("SEL", 128 * (gg % 2 + j), 128 * (gg % 2 + j) + 128, p=rows) for j in (0, 2))
                 cr = A("ST", YC, VW, p=rows)
-                mm(A(("P6", "P7")[gg // 4], 128 * (gg % 4), 128 * (gg % 4) + 128), [(sn, cr), (cr, s), (A("HI"), A("TRI"))], fence=gg in (2, 6))
-            for h in range(2):
-                act(A("EA", 512 * h, 512 * h + 512), A(("P6", "P7")[h]), AF.Abs)
-                act(A("EQ", 512 * h, 512 * h + 512), A("EA", 512 * h, 512 * h + 512), AF.Relu, bias=2048.0, scale=-2048.0)
-            arrive()
-            cp(IND(A("IA"), A("SO", 40, 48)), cur)
-            cp(IND(A("XB"), A("SO", 40, 48)), A("ZZ"))
-            if t == 0:
-                iota(A("SCM"), [[0, 784]])
-                consts_places()
-                for d in (4, 2, 6, 1, 3, 5, 7):
-                    flmat(0, d)
-                    flmat(1, d)
-            else:
-                iota(A("TT", 768, 784), [[0, 16]])
-        else:
+                mm(A(("P6", "P7")[gg // 4], 128 * (gg % 4), 128 * (gg % 4) + 128), [(sn, cr), (cr, s)], fence=gg in (2, 6))
             flags(t, 0)
-            masks(256, 384, "P7")
+            cp(IND(A("VB", 0, YC), A("SO", 0, 8)), y)
+            fill(3)
             flags(t, 1)
-            fold([(o, d) for o in range(2) for d in (1, 3, 5, 7)], False, True)
-            tt(A("DF"), A("DF"), sp, OP.mult)
-            tt(IND(A("VB", 0, YC), A("SO", 24, 32)), A("DF"), y, OP.add)
-            dma("s", H(T.yv[:, :]), A("VB", 0, 1152))
-            arrive()
-            cp(IND(A("IA"), A("SO", 40, 48)), cur)
-            cp(IND(A("XB"), A("SO", 40, 48)), A("ZZ"))
-            dma("s", H(T.yx[:, :]), A("XB"), lag=4.5)
-            scan(A("TT", 0, 512), A("SCM", 0, 512), A("P0"), OP.mult, OP.add)
-            places()
-            scan(A("TT", 512, 769), A("SCM", 512, 769), A("P1", 0, 257), OP.mult, OP.add, A("TT", 511, 512))
-            tw = A("TT")
-            act(A("OE", 0, S0), IND(tw, A("PO", 0, 48)), bias=-1.0)
-            for p in range(16):
-                mm(A("P6", 0, 256), [(A("ZS", 15 - p, 143 - p), A("IA", 256 * p, 256 * p + 256))], p == 0, p == 15)
-            tt(A("TM", 0, 384), IND(tw, A("PO", 48, 72)), A("MM", 0, 384), OP.mult)
-            tt(A("TM", 384, 768), IND(tw, A("PO", 120, 144)), A("MM", 384, 768), OP.mult)
-            mm(A("P4", 0, 384), [(A("BOH", 0, 128), A("TM", 0, 384))])
-            mm(A("P5", 0, 384), [(A("BOH", 128, 256), A("TM", 384, 768))])
-            ts(A("OH", 0, 16 * OHV), IND(tw, A("PO", 72, 72 + OHV)), -1.0, OP.add)
-            act(A("OE", S0, 1152), A("P4", 0, 384), bias=-1.0)
-            dma("s", H(T.ye[:, :]), A("OE", p=(7, 128, 16)))
-            act(A("OH", 16 * OHV, S0), IND(tw, A("PO", 72 + OHV, 120)), bias=-1.0)
-            cp(A("WN"), A("P6", 0, 256))
-            dma("s", H(T.yw[:, :]), A("WN"))
-            act(A("OH", S0, 1152), A("P5", 0, 384), bias=-1.0)
-            dma("a", H(T.yh[:, :]), A("OH", p=(15, 128, 16)))
+            fill(9)
+        wait("a", arr, N - 1)
+        act(A("ZZ"), IND(A(land), A("SO", 32, 40)), AF.Abs)
+        wrap(A("P4", 72, 80), "ZM", "ZZ", 0, 8)
+        if last:
+            fold([(1, d) for d in (1, 3, 5, 7)], (0,), stop=True)
+            fold([(o, d) for o in range(2) for d in (1, 3, 5, 7)], (1,), stop=True)
+            for r in range(1, NT):
+                ts(A("PO", 48 + 8 * r, 56 + 8 * r), A("S2", 16 + 16 * r, 24 + 16 * r), 1.0, OP.add)
+                cp(A("PO", 120 + 8 * r, 128 + 8 * r), A("S2", 24 + 16 * r, 32 + 16 * r))
+        else:
+            banks()
+            for h in range(2):
+                act(A("EA", 512 * h, 512 * h + 512), A(("P6", "P7")[h]), AF.Abs, bias=64.0)
+            for h in range(2):
+                act(A("EQ", 512 * h, 512 * h + 512), A("EA", 512 * h, 512 * h + 512), AF.Relu, bias=64.0 * 2048, scale=-2048.0)
+        if first:
+            wait("s", arr, N - 1)
+            for d in (2, 6):
+                zero(0, d)
+                zero(1, d)
+            zero(0, 5)
+        if t == 1:
+            fold([(0, 4), (1, 4), (0, 2), (0, 6)], start=True, first=[(ID, "SCM", 0)])
+        tt(A("SI", 40, 48), A("P4", 72, 80), A("LN", 8, 16), OP.subtract)
+        tt(A("QF"), A("P4", 72, 80), A("SI", 40, 48), OP.subtract)
+        lin(cells, A("QF"), 32.0)
+        if not last:
+            cp(IND(A("IA"), cells), cur)
+            cp(IND(A("XB"), cells), A("ZZ"))
 
-    if not START:
-        START.update(plan())
-    issue(START)
+    cp(IND(A("XB"), cells), A("ZZ"))
+    dma("s", H(T.yx[:, :]), A("XB"))
+    cp(IND(A("IA"), cells), cur)
+    scan(A("TT", 0, 512), A("SCM", 0, 512), A("P0"), OP.mult, OP.add)
+    for p in range(12):
+        mm(A("P6", 0, 256), [(A("ZA", 15 - p, 143 - p), A("IA", 256 * p, 256 * p + 256))], p == 0, False)
+    scan(A("TT", 512, 769), A("SCM", 512, 769), A("P1", 0, 257), OP.mult, OP.add, A("TT", 511, 512))
+    tw = A("TT")
+    tt(A("TM", 0, 384), IND(tw, A("PO", 48, 72)), A("MM", 0, 384), OP.mult)
+    act(A("OE", 0, S0), IND(tw, A("PO", 0, 48)), bias=-1.0)
+    tt(A("TM", 384, 768), IND(tw, A("PO", 120, 144)), A("MM", 384, 768), OP.mult)
+    mm(A("P4", 0, 384), [(A("BOH", 0, 128), A("TM", 0, 384))])
+    for p in range(12, 16):
+        mm(A("P6", 0, 256), [(A("ZA", 15 - p, 143 - p), A("IA", 256 * p, 256 * p + 256))], False, p == 15)
+    mm(A("P5", 0, 384), [(A("BOH", 128, 256), A("TM", 384, 768))])
+    act(A("OH", 0, S0), IND(tw, A("PO", 72, 120)), bias=-1.0)
+    ts(A("OE", S0, 1152), A("P4", 0, 384), -1.0, OP.add)
+    dma("s", H(T.ye[:, :]), A("OE", p=(7, 128, 16)))
+    cp(A("WN"), A("P6", 0, 256))
+    dma("s", H(T.yw[:, :]), A("WN"))
+    ts(A("OH", S0, 1152), A("P5", 0, 384), -1.0, OP.add)
+    dma("a", H(T.yh[:, :]), A("OH", p=(15, 128, 16)))
+
     for sem in cnt:
         if cnt[sem]:
             wait("s" if sem[0] == "d" else "g", sem, cnt[sem])

from concourse.bass import DstId, RemoteDMATransfer
from concourse.mybir import AluOpType as OP, ActivationFunctionType as AF, AxisListType

C, L, S0, NT = 4096, 128, 768, 3
DUM, YC = 1152, 1280
VW = YC + L
PW = 1024
XA = (96, 88, 88)
KW = 25
GM = 3079
BT, MS = 3072, 6144
TABLE = ((("AE", 2048, 5248, 256), ("AH", 2176, 4352, 256)), (("AE", 0, 3200, 256), ("AH", 0, 2176, 256)),
         (("AE", 0, 6272, 512), ("GB", 0, 4224, 512)))
ZAT = {nm: 144 * j for j, nm in enumerate(("ZS", "ZE", "ZF", "ZP", "ZQ", "Z8", "ZM"))}
ZW = 7 * 144 + 24
BF, F32, I32, U16 = "bfloat16", "float32", "int32", "uint16"


def _sb(n, d):
    return ("sbuf", [128, n], d)


SCRATCH = {
    "XB": _sb(C, BF), "VB": _sb(VW, BF), "ST": _sb(VW, BF), "IA": _sb(C, BF), "GX": _sb(4096, BF), "GB": _sb(8192, BF),
    "MT": _sb(256, BF), "TH": _sb(16, BF),
    "LD0": _sb(1024, BF), "LD1": _sb(1024, BF), "LD2": _sb(1024, BF), "AE": _sb(6272, BF), "AH": _sb(4352, BF),
    "WL": _sb(256, I32), "W1": _sb(256, F32), "W2": _sb(256, F32), "WO": _sb(256, U16), "WN": _sb(256, F32),
    "EL": _sb(96, I32), "E1": _sb(192, I32), "NP": _sb(288, BF), "QF": _sb(8, F32), "TN": _sb(3, F32), "SQ": _sb(48, U16),
    "IO": _sb(144, BF), "I8": _sb(136, BF),
    "PI": _sb(8, I32), "PJ": _sb(8, I32), "K": _sb(80, F32), "KI": _sb(48, I32), "KO": _sb(48, U16),
    "BO": _sb(128, BF), "ID": _sb(144, BF), "LH": _sb(136, BF),
    "DM": _sb(128, F32), "CM": _sb(8, F32), "ZA": _sb(ZW, BF),
    "FEN": _sb(400, BF), "I24": _sb(400, BF), "G8": _sb(8, BF),
    "RK": _sb(528, BF), "SEG": _sb(1024, BF),
    "LD": _sb(128, BF), "DG": _sb(128, BF), "DD": _sb(128, BF), "CT": _sb(384, BF), "SEL": _sb(512, BF),
    "IX": _sb(128, BF), "LR": _sb(128, BF), "EA": _sb(1024, BF), "EQ": _sb(1024, BF), "ON": _sb(128, BF),
    "FL": _sb(14 * 128, BF), "B0": _sb(256, BF), "B7": _sb(128, BF), "LO": _sb(256, BF), "HI": _sb(128, BF), "HN": _sb(128, BF),
    "SCM": _sb(784, BF), "U": _sb(64, F32), "U1": _sb(64, I32), "UU": _sb(64, F32), "UB": _sb(64, I32), "UA": _sb(192, I32),
    "UC": _sb(192, I32), "AO": _sb(192, U16), "SL": _sb(192, U16), "AC": _sb(4, F32), "SG": _sb(400, BF), "NPB": _sb(200, BF),
    "VL": _sb(200, F32), "SC": _sb(200, F32), "SF": _sb(8, F32), "D1": _sb(128, F32), "D2": _sb(128, F32),
    "SR": _sb(128, BF), "NR": _sb(16, BF), "PL": _sb(16, F32), "SI": _sb(64, I32), "SO": _sb(48, U16), "LN": _sb(24, F32),
    "IN": _sb(128, BF), "ZR": _sb(864, BF), "S2": _sb(64, I32),
    "G1": _sb(128, BF), "WB": _sb(128, BF), "SP": _sb(384, BF), "STP": _sb(384, BF), "BS": _sb(128, BF),
    "M1": _sb(128, BF), "DF": _sb(128, BF), "ZZ": _sb(128, BF),
    "PO": _sb(144, U16), "TT": _sb(784, F32), "MM": _sb(768, F32), "MA": _sb(768, F32), "TM": _sb(768, "float16"),
    "BOH": _sb(256, "float16"), "OE": _sb(1152, F32), "OH": _sb(1152, F32),
}
PSUM = ["P0", "P1", "PE", "PV", "P4", "P5", "P6", "P7"]
for _n in PSUM:
    SCRATCH[_n] = ("psum", [128, 512], F32)
NDMA = 48
SEMAPHORES = ["sv", "sa", "sp", "sg", "sent", "arr0", "arr1", "arr2"] + ["d%d" % i for i in range(NDMA)]


def rank_program(g, core, T, topo):
    rank = T.rank_of(core)
    if rank is None:
        return
    N = len(T.cores)
    Q = {"v": g.vector, "a": g.scalar, "p": g.tensor, "g": g, "s": g.sync}
    SEM = {"v": "sv", "a": "sa", "p": "sp", "g": "sg"}
    cnt = {"sv": 0, "sa": 0, "sp": 0, "sg": 0, "sent": 0}
    waited = {q: {} for q in Q}
    hist, lastp, nd = {}, {}, [0]

    def A(name, lo=0, hi=None, step=1, p=None):
        t = T[name]
        if hi is None:
            hi = t.shape[1]
        ps = slice(0, 128) if p is None else slice(*p)
        return (t[ps, lo:hi:step] if step != 1 else t[ps, lo:hi], [(name, lo, hi)])

    def IND(win, off):
        return (win[0].indirect(off[0]), win[1], off[1])

    def H(ap):
        return (ap, [])

    def wait(q, sem, val):
        if waited[q].get(sem, 0) < val:
            Q[q].wait_ge(T.sem[sem], val)
            waited[q][sem] = val

    def order(q, reads, writes, dma=False, keep=False):
        need = {}
        for rs, wr in ((reads, False), (writes, True)):
            for (nm, lo, hi) in rs:
                bank = nm in PSUM
                for (q2, sem, val, l2, h2, w2) in hist.get(nm, ()):
                    if keep and wr and q2 == "dma":
                        continue
                    same = q2 == q and not dma
                    if bank and not same:
                        hit = True
                    elif same and q == "p":
                        hit = False
                    else:
                        hit = (wr or w2) and l2 < hi and lo < h2
                    if hit and need.get(sem, 0) < val:
                        need[sem] = val
        for sem in need:
            wait(q, sem, need[sem])

    def note(q, sem, val, reads, writes):
        for rs, wr in ((reads, False), (writes, True)):
            for (nm, lo, hi) in rs:
                h = hist.setdefault(nm, [])
                if wr:
                    h[:] = [e for e in h if not (lo <= e[3] and e[4] <= hi and nm not in PSUM)]
                h.append((q, sem, val, lo, hi, wr))

    def run(q, fns, out, ins, fence=False):
        reads, writes = [], list(out[1])
        if len(out) == 3:
            reads += out[2]
        for x in ins:
            if isinstance(x, tuple):
                reads += x[1] + (x[2] if len(x) == 3 else [])
        order(q, reads, writes)
        if fence:
            wait("p", "sp", lastp[writes[0][0]])
        for fn in (fns if q == "p" else [fns]):
            fn().then_inc(T.sem[SEM[q]], 1)
            cnt[SEM[q]] += 1
        if q == "p":
            lastp[writes[0][0]] = cnt["sp"]
        note(q, SEM[q], cnt[SEM[q]], reads, writes)

    def dma(q, o, i, keep=False):
        order(q, i[1], o[1], True, keep)
        sem = "d%d" % nd[0]
        nd[0] += 1
        Q[q].dma_start(o[0], i[0]).then_inc(T.sem[sem], 16)
        cnt[sem] = 16
        note("dma", sem, 16, i[1], [])
        for (nm, lo, hi) in o[1]:
            hist.setdefault(nm, []).append(("dma", sem, 16, lo, hi, True))

    def val(x):
        return x[0] if isinstance(x, tuple) else x

    def cp(o, i):
        run("v", lambda: g.vector.tensor_copy(o[0], i[0]), o, [i])

    def tt(o, a, b, op):
        run("v", lambda: g.vector.tensor_tensor(o[0], a[0], b[0], op), o, [a, b])

    def ts(o, a, s1, op0, s2=None, op1=None):
        if op1 is None:
            run("v", lambda: g.vector.tensor_scalar(o[0], a[0], val(s1), None, op0), o, [a, s1])
        else:
            run("v", lambda: g.vector.tensor_scalar(o[0], a[0], val(s1), val(s2), op0, op1), o, [a, s1, s2])

    def lin(o, i, a, b=None):
        if b is None:
            ts(o, i, a, OP.mult)
        else:
            ts(o, i, a, OP.mult, b, OP.add)

    def ms(o, c):
        run("v", lambda: g.vector.memset(o[0], c), o, [])

    def scan(o, a, b, op0, op1, ini=0.0):
        run("v", lambda: g.vector.tensor_tensor_scan(o[0], a[0], b[0], val(ini), op0, op1), o, [a, b, ini])

    def act(o, i, f=AF.Identity, bias=None, scale=None):
        kw = {}
        if bias is not None:
            kw["bias"] = val(bias)
        if scale is not None:
            kw["scale"] = val(scale)
        run("a", lambda: g.scalar.activation(o[0], i[0], f, **kw), o, [i, bias, scale])

    def lia(o, i, a, b=None):
        act(o, i, scale=a, bias=b)

    def mm(o, pairs, start=True, stop=True, fence=False):
        fns = [lambda l=l, r=r, n=n: g.tensor.matmul(o[0], l[0], r[0], start and n == 0, stop and n == len(pairs) - 1)
               for n, (l, r) in enumerate(pairs)]
        run("p", fns, o, [x for pr in pairs for x in pr], fence)

    def iota(o, pat, base=0, cm=0):
        if SCRATCH[o[1][0][0]][2] == I32:
            run("g", lambda: g.iota(o[0], pat, base, cm), o, [])
        else:
            run("g", lambda: g.iota(o[0], pat, base, cm, allow_small_or_imprecise_dtypes=True), o, [])

    def asel(o, i, pat, op, base, cm, fill=0.0):
        run("g", lambda: g.affine_select(o[0], i[0], pat, op, fill, base, cm), o, [i])

    def wrap(o, Z, name, lo, n, stop=True):
        mm(o, [(A("ZA", ZAT[Z] + 15 - p, ZAT[Z] + 143 - p), A(name, lo + p, lo + 16 * n, 16)) for p in range(16)], True, stop)

    def K(j):
        return A("K", j, j + 1)

    def O(r):
        return A("DM", r, r + 1)

    def plane(o, d):
        t = 0 if d == 4 else 1 + d % 2
        nm, lo, hi, unit = TABLE[t][o]
        return nm, lo + unit * (d + (4 >> t) * (1 - 2 * o))

    def zero(o, d):
        nm, c = plane(o, d)
        dma("s", A(nm, c - 16 + 16 * o, c + 784), A("ZR", 0, 800 - 16 * o))

    def weigh(name, n, r, w):
        o = A("ZA", ZAT[name] + 15, ZAT[name] + 144 * n, 16)
        asel(o, o, [[0, n], [-16, 9]], OP.not_equal, -r, 1, w)

    def diag(name, c):
        n = T[name].shape[1]
        asel(A(name), A("ZR", 0, n), [[-1, n]], OP.not_equal, 0, 1, c)

    def flmat(o, d):
        asel(A("FL", 128 * (7 * o + d - 1), 128 * (7 * o + d)), A("B0", 128 * o, 128 * o + 128), [[0, 8], [1, 16]], OP.is_ge, 1 - 8 * o - d, 0)

    def build(j, f):
        f(A("IA", 512 * j, 512 * j + 512), IND(A("ST", 0, S0), A("WO", 32 * j, 32 * j + 32)))

    def mark_whole(y0):
        mm(A("PE", 0, 64), [(A("LH", 8, 136), A("VB", y0, y0 + L, 2)), (A("LH", 0, 128), A("VB", y0 + 1, y0 + L, 2))])
        ts(A("U1"), A("PE", 0, 64), 0.5 - 1.0 / 8192, OP.subtract)

    def mark_part():
        tt(A("U"), A("PE", 0, 64), A("U1"), OP.subtract)

    def terms(a):
        act(A("UU"), A("U"), AF.Square, -512.0, 1024.0)
        for m in range(3):
            lia(A("PE", 64 * m + 64, 64 * m + 128), A("U"), K(14 + m), a)

    def square():
        ts(A("UB"), A("UU"), 0.5, OP.mult, 31.0 / 64, OP.subtract)

    def sums():
        for m in range(3):
            tt(A("UC", 64 * m, 64 * m + 64), A("PE", 64 * m + 64, 64 * m + 128), A("UB"), OP.add)

    def modulo():
        ts(A("UA"), A("UC"), 4095, OP.bitwise_and)

    FEH, FV, FS = A("ZA", ZW - 24, ZW - 8), A("ZA", ZW - 8, ZW), A("ZA", 15, 143, 16)
    ID, one, z8 = A("ID", 0, 128), A("ON", p=(0, 1)), A("ZA", ZAT["Z8"] + 15, ZAT["Z8"] + 144, 16)
    rk, rkl, rk2 = A("RK", 0, 200, p=(0, 3)), A("RK", 400, 528, p=(0, 3)), A("RK", 200, 400, p=(0, 1))
    kR, kG, kQ, kO, k7, kH, kP = [K(j) for j in range(7)]
    y, stp, cur, cells = A("VB", YC, VW), A("STP", 0, L), A("ST", YC, VW), A("SO", 40, 48)

    def banks():
        mm(A("PE", 0, 16 * KW), [(cur, A("FEN"))], True, False)
        mm(A("PV", 0, 8 * KW), [(rkl, rk)], True, False)

    dma("a", A("EL", 0, 48), H(T.e0[:, :]))
    dma("s", A("EL", 48, 96), H(T.h0[:, :]))
    dma("a", A("VB", 0, L), H(T.v0[:, 0:L]))
    for h in range(2):
        dma("sa"[h], A("WL", 128 * h, 128 * h + 128), H(T.w0[h::2, :]))
    dma("s", A("XB", 0, 2048), H(T.x0[:, 0:2048]))
    iota(A("PI", 0, 1), [[0, 1]], 0, 1)
    iota(A("IO"), [[1, 144]])
    iota(A("KI", 0, 16), [[16, 8], [128, 2]])
    iota(A("I8"), [[1, 17], [0, 8]])
    iota(A("NP", 240, 288), [[0, 48]], 8)
    iota(A("KI", 16, 32), [[2, 16]])
    iota(kP, [[0, 1]], 0, 1)
    iota(A("SEG", 0, 256), [[0, 32], [256, 8]])
    ms(A("ZR"), 0.0)
    act(A("ST", 0, S0), A("ZR", 0, S0))
    p_ = A("PI", 0, 1)
    ts(A("PJ", 0, 1), p_, 15, OP.bitwise_and)
    ts(A("PJ", 1, 2), p_, 4, OP.logical_shift_right)
    ts(A("PJ", 2, 3), p_, 124, OP.bitwise_and)
    ts(A("PJ", 3, 4), p_, 4, OP.logical_shift_right, 1, OP.bitwise_and)
    ts(A("PJ", 4, 5), p_, 7, OP.bitwise_and)
    ts(A("PJ", 5, 6), p_, 3, OP.logical_shift_right, 1, OP.bitwise_and)
    ms(A("ON"), 1.0)
    cp(A("K", 0, 6), A("PJ", 0, 6))
    lia(K(10), kR, 1.5)
    lia(K(8), kR, 2.0 / 4096, 1.0 / 4096)
    lia(K(9), kG, 2.0, 1.0)
    act(A("NP", 192, 240), A("ZR", 0, 48), bias=K(10))
    act(A("K", 11, 14), A("IO", 0, 24, 8), bias=k7)
    lia(K(7), k7, 32.0, kH)
    act(A("K", 14, 17), A("K", 11, 14), AF.Square, bias=0.5)
    ts(A("KO", 0, 16), A("KI", 0, 16), kR, OP.add)
    ts(A("DM", 0, 16), A("IO", 0, 16), kR, OP.is_equal)
    ts(A("CM"), A("IO", 0, 8), kG, OP.is_equal)
    ts(A("E1", 0, 96), A("EL"), 5, OP.logical_shift_right)
    ts(A("E1", 96, 192), A("EL"), 31, OP.bitwise_and)
    ts(A("LH"), A("I8"), K(9), OP.is_equal, K(8), OP.mult)
    cp(A("NP", 0, 192), A("E1"))
    dma("s", A("ST", 0, S0, p=(9, 128, 16)), A("IO", 0, 48), True)
    for j, row, q in ((5, 2, "s"), (4, 8, "s"), (0, 0, "a"), (1, 4, "s"), (2, 1, "a"), (3, 5, "s")):
        dma(q, A("ST", 0, S0, p=(row, 128, 16)), A("NP", 48 * j, 48 * j + 48), True)
    dma("a", A("XB", 2048, C), H(T.x0[:, 2048:C]))
    lia(A("K", 14, 17), A("K", 14, 17), 4096.0, 4096 * 128.75)
    lia(A("G8"), A("CM"), -8192.0)
    dma("s", A("VB", L, S0), H(T.v0[:, L:S0]))
    for j in range(1, 4):
        dma("s", A("SEG", 256 * j, 256 * j + 256), A("SEG", 0, 256))
    dma("s", cur, A("ST", 0, L))
    dma("s", A("ZA", 144, ZW - 24), A("ZR"))
    dma("s", y, H(T.v0[:, 0:L]))
    dma("s", A("TH", 0, 3), H(T.th[:, :]))
    for j in range(1, 8):
        dma("s", A("DM", 16 * j, 16 * j + 16), A("DM", 0, 16))
    dma("s", A("VB", S0, YC), A("ZR", 0, YC - S0))
    dma("s", A("ST", S0, DUM), A("ZR", 0, DUM - S0))
    for o in range(2):
        zero(o, 4)
    dma("s", A("SCM"), A("ZR", 0, 784))
    dma("s", A("SCM", p=(7, 128, 8)), A("ON", 0, 98))
    cp(A("W1"), IND(A("WL"), A("KO", 0, 16)))
    mark_whole(0)
    ts(A("KO", 16, 32), A("KI", 16, 32), K(7), OP.add)
    run("v", lambda: g.vector.transpose(T.W2[:, :], T.W1[:, :]), A("W2"), [A("W1")])
    mark_part()
    lia(K(31), kP, 8.0)
    act(K(32), kP, bias=float(DUM))
    terms(None)
    cp(A("WO"), IND(A("W2"), A("KO", 16, 32)))
    square()
    act(K(53), O(1), bias=O(5))
    lia(K(56), O(2), 12.0, O(11))
    lia(K(58), O(2), -1.0, O(6))
    lia(K(59), O(8), 24.0, O(3))
    lia(K(56), O(6), 8.0, K(56))
    lia(K(33), O(0), 128.0)
    lia(K(61), K(58), 4.0, K(59))
    sums()
    asel(A("ZA", 0, 144), A("ZR", 0, 144), [[-16, 9], [200, 16]], OP.not_equal, -3008, 1, 32.0)
    asel(FEH, A("ZR", 0, 16), [[-4, 2], [-16, 8]], OP.not_equal, 0, 1, 32.0)
    asel(FV, A("ZR", 0, 8), [[-16, 8]], OP.not_equal, -8, 1, 32.0 / 4096)
    weigh("ZS", 1, 9, 1.0)
    asel(FEH, FEH, [[-4, 2], [-16, 8]], OP.not_equal, -1, 1, 1.0)
    asel(FV, FV, [[-16, 8]], OP.not_equal, -9, 1, 1.0 / 4096)
    iota(rk, [[0, 8], [-1, KW]], KW - 1)
    asel(FEH, FEH, [[-4, 2], [-16, 8]], OP.not_equal, -2, 1, -0.125)
    asel(rk, rk, [[0, 200]], OP.is_equal, -1, 1)
    iota(A("I24"), [[4, 2], [16, 8], [0, KW]])
    asel(rk, rk, [[0, 8], [1, KW]], OP.is_ge, -17, 100, 1016.0)
    asel(rkl, A("IO", 0, L, p=(0, 3)), [[0, L]], OP.is_equal, -2, 1, 1.0)
    asel(rk, rk, [[0, 8], [1, KW]], OP.is_ge, -9, 100, 2032.0)
    iota(A("KI", 32, 40), [[KW, 8]], KW - 1)
    for j, c in enumerate((3072.0, GM - 3072 + YC / 4096, 1 / 4096)):
        o = A("RK", 0, 200, KW, p=(0, 3))
        asel(o, o, [[0, 8]], OP.not_equal, -j, 1, c)
        if j < 2:
            iota((A("KI", 40, 48), A("PL", 8, 16))[j], [[1 - j, 8]])
    asel(rk2, A("ZR", 0, 200, p=(0, 1)), [[0, 8], [1, KW]], OP.is_gt, 0, 0, -2.0 ** 19)
    diag("ID", 1.0)
    diag("IN", -1.0)
    diag("HI", 4096.0)
    asel(A("BO"), A("ON"), [[-16, 8], [0, 16]], OP.is_ge, 0, 1)
    iota(z8, [[-256, 9]], 8, 16)
    asel(A("BO"), A("BO"), [[16, 8], [0, 16]], OP.is_ge, 15, -1)
    asel(z8, z8, [[-16, 9]], OP.is_ge, 0, 1)
    asel(A("LD"), A("ZR", 0, 128), [[-16, 8], [0, 16]], OP.not_equal, -11, 1, -100.0)
    asel(z8, z8, [[16, 9]], OP.is_ge, 15, -1)
    asel(A("DG"), ID, [[0, 8], [-1, 16]], OP.is_ge, 6, 0)
    weigh("ZE", 3, 0, 32.0)
    asel(A("DG"), A("DG"), [[0, 8], [1, 16]], OP.not_equal, -3, 0)
    weigh("ZE", 3, 1, 1.0)
    asel(A("DD"), A("IN"), [[0, 8], [1, 16]], OP.is_ge, -8, 0)
    weigh("ZE", 1, 2, 256.0)
    asel(A("IX"), ID, [[0, 8], [1, 16]], OP.not_equal, -10, 0)
    run("v", lambda: g.vector.tensor_reduce(K(54)[0], FEH[0], AxisListType.X, OP.add, negate=True), K(54), [FEH])
    modulo()
    build(0, act)
    build(2, cp)
    cp(A("AO"), A("UA"))
    build(1, act)
    build(4, cp)
    build(3, act)
    build(6, cp)
    build(5, act)
    build(7, cp)
    ts(A("FEN"), A("I24"), kQ, OP.is_equal, K(54), OP.mult)
    banks()

    def later_constants():
        weigh("ZP", 1, 3, 1.0)
        asel(A("B0", 128, 256), A("ON"), [[-16, 8], [0, 16]], OP.is_equal, 0, 1)
        weigh("ZQ", 1, 4, 32.0)
        asel(A("B0", 0, 128), A("B0", 128, 256), [[0, 8], [-1, 16]], OP.is_ge, 7, 0)
        weigh("ZQ", 1, 5, 1.0)
        asel(A("B7"), A("ON"), [[0, 16], [1, 8]], OP.not_equal, -7, 0)
        weigh("ZF", 1, 2, 512.0)
        for d in (4, 2, 6):
            flmat(0, d)
            flmat(1, d)
        diag("HN", -100.0)
        for o in range(2):
            asel(A("LO", 128 * o, 128 * o + 128), A("B7"), [[-16, 8], [0, 16]], OP.is_equal, -2 - 4 * o, 1)

    small = [lambda: lin(K(77), O(9), 256.0, O(10)), lambda: lin(K(62), K(58), 2.0, K(59)), lambda: lin(K(77), O(8), 8192.0, K(77)),
             lambda: lin(K(62), O(8), 4.0, K(62)), lambda: lin(K(34), K(77), kO), lambda: lin(K(63), K(58), 1.0, K(59)),
             lambda: lin(K(55), K(34), -1.0, K(77)), lambda: lin(K(63), O(8), 8.0, K(63))]
    for j, k, w in ((1, 34, 1.0), (3, 34, -1.0), (0, 55, 1.0), (2, 55, -1.0)):
        small.append(lambda j=j, k=k, w=w: ts(A("SEL", 128 * j, 128 * j + 128), A("ON"), K(k), OP.mult, w, OP.mult))
    small += [lambda: ts(K(12), O(7), O(15), OP.add), lambda: lin(K(10), kH, -1.0, 1.0), lambda: lin(K(9), K(12), 2.0, -1.0),
              lambda: lin(K(17), K(12), 8.0, 99.0), lambda: lin(K(10), K(10), K(9)), lambda: lin(K(17), k7, -1.0, K(17)),
              lambda: lin(K(9), kH, K(9)), lambda: lin(A("BOH", 0, 128), A("BO"), K(10)), lambda: lin(A("BOH", 128, 256), A("BO"), K(9))]

    def fill(n):
        for f in small[:n]:
            f()
        del small[:n]

    peers = [T.cores[(rank - d) % N] for d in range(1, N)]
    SB = ("P4", "P5", "P4")

    def gx(lo, hi, f):
        f(A("GX", 16 * lo, 16 * hi), IND(A("XB"), A("AO", lo, hi)))

    def gi(m):
        act(A("GB", 1024 * m, 1024 * m + 1024), IND(A("IA"), A("AO", 64 * m, 64 * m + 64)))
        wrap(A(SB[m], 0, 64), "ZS", "GB", 1024 * m, 64)

    def labels(m, bank, w, width):
        for kk in range(8):
            k = 8 * m + kk
            mm(A(bank, KW - 1 - k, width * KW, KW), [(A("GB", 1024 * m + kk, 1024 * m + 1024, 8), w)], False, k == 23, k == 0)

    def sl(m):
        cp(A("SL", 64 * m, 64 * m + 64), A(SB[m], 0, 64))

    def gv(t, m, c0=0, c1=64):
        lo, hi = 64 * m + c0, 64 * m + c1
        tt(A("GB", BT + 16 * lo, BT + 16 * hi), IND(A("VB", 0, S0 + L * t), A("SL", lo, hi)), A("GX", 16 * lo, 16 * hi), OP.is_gt)

    def mx(m):
        o = A("GB", MS + 1024 * m, MS + 1024 * m + 1024) if m < 2 else A("GX", GM - 7, GM + 1017)
        scan(o, A("SEG"), A("GX", 1024 * m, 1024 * m + 1024), OP.min, OP.max)

    def count(m):
        for kk in range(8):
            k = 8 * m + kk
            mm(A("P5", KW - 1 - k, 8 * KW, KW), [(A("GB", BT + 1024 * m + kk, BT + 1024 * m + 1024, 8), A("G8"))], False, k == 23, k in (0, 16))

    def fold(ds, halves=(0, 1), start=False, stop=False, first=()):
        prs = list(first) + [(A("FL", 128 * (7 * o + d - 1), 128 * (7 * o + d)), plane(o, d)[0], plane(o, d)[1] - 1 + o) for (o, d) in ds]
        for h in halves:
            for n, (l, nm, c0) in enumerate(prs):
                mm(A(("P0", "P1")[h], 0, (512, 257)[h]), [(l, A(nm, c0 + 512 * h, c0 + (512, 769)[h]))], start and n == 0, stop and n == len(prs) - 1)

    def flags(t, o):
        nm, lo, hi, unit = TABLE[t][o]
        cp(IND(A(nm, lo, hi), A("SQ", 16 * t + 8 * o, 16 * t + 8 * o + 8)), A("SP", 128 * t, 128 * t + 128))

    def masks_p(lo, hi, bank):
        for o in range(2):
            mm(A(bank, 256 * o, 256 * o + hi - lo), [(A("LO", 128 * o, 128 * o + 128), A("ST", S0 + lo, S0 + hi)), (A("HN"), A("SP", lo, hi))])

    def masks_a(lo, hi, bank):
        for o in range(2):
            act(A("MA", 384 * o + lo, 384 * o + hi), A(bank, 256 * o, 256 * o + hi - lo), AF.Abs, bias=K(17))

    def masks_m(lo, hi):
        for o in range(2):
            act(A("MM", 384 * o + lo, 384 * o + hi), A("MA", 384 * o + lo, 384 * o + hi), AF.Relu, bias=1.0, scale=-1.0)

    for t in range(NT):
        first, last = t == 0, t == NT - 1
        land, arr = "LD%d" % t, "arr%d" % t
        ct, sp, n0 = A("CT", 128 * t, 128 * t + 128), A("SP", 128 * t, 128 * t + 128), S0 + L * t
        gi(0)
        gx(0, 64, cp)
        gx(64, XA[t], cp)
        labels(0, "PE", FEH, 16)
        labels(0, "PV", FV, 8)
        sl(0)
        if first:
            cp(A("KO", 32, 48), A("KI", 32, 48))
        gi(1)
        gv(t, 0)
        labels(1, "PE", FEH, 16)
        labels(1, "PV", FV, 8)
        gx(XA[t], 128, act)
        sl(1)
        mx(0)
        mm(A("P5", 0, 8 * KW), [(one, rk2)], True, False)
        gi(2)
        gv(t, 1)
        labels(2, "PE", FEH, 16)
        count(0)
        labels(2, "PV", FV, 8)
        gx(128, 160, act)
        gx(160, 192, act)
        sl(2)
        mx(1)
        count(1)
        if last:
            dma("s", A("AE", 1008, 4880, p=(0, 128, 16)), A("ZR", 0, 242))
        gv(t, 2, 0, 32)
        act(A("SG"), A("PE", 0, 16 * KW), AF.Sign, bias=0.0625)
        mm(A("P4", 256, 256 + 8 * KW), [(ID, A("SG", 0, 8 * KW)), (ID, A("SG", 8 * KW, 16 * KW))])
        act(A("VL"), A("PV", 0, 8 * KW), bias=K(31))
        ma, mb, mc = A("GB", MS + 7, MS + 1024, 8), A("GB", MS + 1031, MS + 2048, 8), A("GX", GM, GM + 1017, 8)
        r1, r2 = A("MT", 0, 128), A("MT", 128, 256)
        mm(A("PE", 0, 128), [(ID, ma), (A("IN"), mb)])
        act(A("NPB"), A("P4", 256, 256 + 8 * KW), AF.Abs, scale=29.0 * 4096, bias=93.0 * 1024)
        act(r1, A("PE", 0, 128), AF.Relu)
        gv(t, 2, 32, 64)
        mm(A("P5", 0, 8 * KW), [(ID, A("NPB"))], False, False, True)
        mm(A("PE", 128, 256), [(ID, r1), (ID, mb)])
        count(2)
        mx(2)
        if last:
            dma("s", A("GB", 0, 3856, p=(0, 128, 16)), A("ZR", 0, 241))
            masks_p(0, 256, "P6")
        act(r2, A("PE", 128, 256))
        if first:
            lia(A("TN"), A("TH", 0, 3), -1.0, 0.5)
            lia(A("ST", DUM, YC), A("IO", 0, 128), K(53), K(56))
        scan(A("SC"), A("P5", 0, 8 * KW), A("VL"), OP.min, OP.max)
        tt(A("D1"), IND(A("SC"), A("KO", 32, 40)), A("DM"), OP.mult)
        act(A("NR", 8, 16), A("SC", KW - 1, 8 * KW, KW), AF.Relu, 3072.0, -1.0)
        if t:
            act(A("NR", 0, 8), A("SC", KW - 1, 8 * KW, KW), AF.Relu, -3072.0)
        mm(A("P4", 0, 8), [(A("D1"), A("CM"))])
        tt(mc, mc, r2, OP.max)
        mm(A("P7", 0, 8), [(cur, FS), (A("HI"), A("NR", 8, 16))], True, first)
        if not last:
            act(A("SR"), IND(A("SC"), A("KO", 32, 40)), AF.Sign, bias=-3071.9)
            mm(A("PV", 0, 1), [(A("SR"), A("ON", 0, 1))])
        if t:
            for gg in range(8):
                mm(A("P7", gg, gg + 1), [(A("EQ", 128 * gg, 128 * gg + 128), A("NR", gg, gg + 1))], False, gg == 7, gg == 0)
        if first:
            lia(ct, A("IO", 0, 128), O(9), K(61))
            act(A("LN", 0, 8), A("IO", 0, 128, 16), bias=kR)
            lia(A("LR"), A("IO", 0, L), O(10))
        if last:
            masks_a(0, 256, "P6")
            masks_m(0, 256)
            fold([(1, 2), (1, 6)])
        else:
            lia(A("AC", 0, 1), A("PV", 0, 1), -0.5, 64.0)
        if t == 1:
            wrap(A("P0", 0, 56), "ZP", "ST", 0, 56)
            wrap(A("P0", 56, 112), "ZQ", "ST", 0, 56)
        cp(A("SI", 8, 16), A("P4", 0, 8))
        cp(A("SO", 8, 16), A("P4", 0, 8))
        tt(A("SF"), A("P4", 0, 8), A("SI", 8, 16), OP.subtract)
        cp(A("G1"), IND(A("GX"), A("SO", 8, 16)))
        lin(A("SO", 16, 24), A("SF"), 4096.0)
        ts(A("PL", 0, 8), A("P7", 0, 8), K(32), OP.min)
        tt(A(land, 0, L), IND(A("VB"), A("SO", 16, 24)), A("G1"), OP.subtract)
        act(A("BS"), IND(A("ST"), A("SO", 16, 24)))
        trs = []
        for d in range(1, N):
            dst = peers[d - 1]
            rid, pid, _ = topo.addr(dst)
            trs.append(RemoteDMATransfer(dst_ids=[DstId(rid=rid, pnc=pid)], dma_engine_mask=1 << topo.engines(core, dst)[d - 1],
                                         remote_sem=T.sem[arr], src=T[land][:, 0:L], dst=T[land][:, L * d:L * d + L]))
        order("g", [(land, 0, L)], [])
        g.remote_dma_fused(trs, local_sem=T.sem.sent)
        cnt["sent"] += N - 1
        if first:
            later_constants()
        if t == 1:
            for d in (1, 3, 5, 7):
                flmat(0, d)
                flmat(1, d)
            iota(A("TT", 768, 784), [[0, 16]])
        tt(A("D2"), IND(A("PL"), A("KO", 40, 48)), A("DM"), OP.mult)
        act(y, A(land, 0, L), AF.Abs)
        mm(A("P6", 256, 264), [(A("D2"), A("CM"))])
        fill(4)
        if t == 1:
            cp(A("PO", 0, 56), A("P0", 0, 56))
            cp(A("PO", 72, 128), A("P0", 56, 112))
        cp(A("SO", 24, 32), A("P6", 256, 264))
        act(A("WB"), y, AF.Sign, A("TN", t, t + 1))
        fill(2)
        if not last:
            mark_whole(YC)
        act(stp, IND(A("ST"), A("SO", 24, 32)))
        wrap(A("P4", 64, 72), "Z8", "VB", YC, 8)
        fill(2)
        if last:
            tt(A("DF"), IND(A("VB", 0, YC), A("SO", 24, 32)), y, OP.subtract)
        else:
            mark_part()
            terms(A("AC", 0, 1))
        mm(A("P5", 0, 128), [(A("BO"), A("WB")), (A("LD"), stp)])
        mm(A("PV", 128, 256), [(A("ID", 4, 132), stp)])
        mm(A("P7", 0, 128), [(A("DD"), stp), (ID, ct)])
        mm(A("P6", 0, 128), [(A("DG"), stp), (ID, ct)])
        fill(2)
        cp(A("SI", 32, 40), A("P4", 64, 72))
        ts(sp, A("P5", 0, 128), -0.5, OP.is_ge)
        act(A("STP", 128, 256), A("PV", 128, 256))
        ts(A("SI", 24, 32), A("SI", 32, 40), 896, OP.bitwise_and)
        tt(A("M1"), A("P7", 0, 128), sp, OP.mult)
        if last:
            wrap(A("PV", 256, 272), "ZF", "STP", 0, 16)
            act(A("ST", n0, n0 + L), A("P6", 0, 128))
            tt(A("SI", 32, 40), A("SI", 24, 32), A("LN", 0, 8), OP.add)
            tt(A("DF"), A("DF"), sp, OP.mult)
            cp(A("SQ", 16 * t, 16 * t + 16), A("PV", 256, 272))
            cp(A("SO", 32, 40), A("SI", 32, 40))
            mm(A("P5", 0, 128), [(A("IX"), A("BS")), (ID, A("M1"))])
            mm(A("P4", 128, 256), [(ID, y), (A("HI"), sp)])
            masks_p(256, 384, "P7")
            flags(t, 0)
            flags(t, 1)
            act(A("VB", n0, n0 + L), A("P4", 128, 256), AF.Relu, bias=-4096.0)
            act(cur, A("P5", 0, 128))
            fold([(0, d) for d in (1, 3, 5, 7)], (0,))
            masks_a(256, 384, "P7")
            tt(IND(A("VB", 0, YC), A("SO", 24, 32)), A("DF"), y, OP.add)
            dma("s", H(T.yv[:, :]), A("VB", 0, 1152))
            cp(A("S2", 0, 32), A("SQ", 16, 48))
            masks_m(256, 384)
            ts(A("S2", 32, 64), A("S2", 0, 32), PW - 1, OP.bitwise_and)
        else:
            lia(A("STP", 256, 384), sp, K(33))
            mm(A("P5", 0, 128), [(A("IX"), A("BS")), (ID, A("M1")), (ID, A("LR"))])
            mm(A("P4", 128, 256), [(ID, y), (A("HI"), sp)])
            wrap(A("PV", 256, 280), "ZE", "STP", 0, 24, False)
            mm(A("PV", 272, 280), [(A("D2"), A("CM"))], False, True, True)
            tt(A("SI", 32, 40), A("SI", 24, 32), A("LN", 0, 8), OP.add)
            square()
            cp(A("SO", 32, 40), A("SI", 32, 40))
            sums()
            fill(2)
            modulo()
            fill(4)
            act(cur, A("P5", 0, 128))
            if first:
                act(A("LN", 16, 24), A("LN", 0, 8), bias=float(DUM))
                act(A("LN", 8, 16), A("LN", 0, 8), bias=31.0 / 64)
                lia(A("ZA", ZAT["ZM"] + 15, ZAT["ZM"] + 144, 16), z8, 1.0 / 256)
            act(A("ST", n0, n0 + L), A("P6", 0, 128))
            act(A("VB", n0, n0 + L), A("P4", 128, 256), AF.Relu, bias=-4096.0)
            cp(A("AO"), A("UA"))
            tt(A("SI", 56, 64), A("PV", 272, 280), A("LN", 16, 24), OP.min)
            cp(A("SQ", 16 * t, 16 * t + 16), A("PV", 256, 272))
            cp(A("SO", 0, 8), A("SI", 56, 64))
            lia(A("CT", 128 * t + 128, 128 * t + 256), A("IO", 0, 128), O(9), K(62 + t))
            for gg in (0, 1, 4, 5, 2, 3, 6, 7):
                rows = (32 * (gg // 2), 32 * (gg // 2) + 32)
                s, sn = (A("SEL", 128 * (gg % 2 + j), 128 * (gg % 2 + j) + 128, p=rows) for j in (0, 2))
                cr = A("ST", YC, VW, p=rows)
                mm(A(("P6", "P7")[gg // 4], 128 * (gg % 4), 128 * (gg % 4) + 128), [(sn, cr), (cr, s)], fence=gg in (2, 6))
            flags(t, 0)
            cp(IND(A("VB", 0, YC), A("SO", 0, 8)), y)
            fill(3)
            flags(t, 1)
            fill(9)
        wait("a", arr, N - 1)
        act(A("ZZ"), IND(A(land), A("SO", 32, 40)), AF.Abs)
        wrap(A("P4", 72, 80), "ZM", "ZZ", 0, 8)
        if last:
            fold([(1, d) for d in (1, 3, 5, 7)], (0,), stop=True)
            fold([(o, d) for o in range(2) for d in (1, 3, 5, 7)], (1,), stop=True)
            for r in range(1, NT):
                ts(A("PO", 48 + 8 * r, 56 + 8 * r), A("S2", 16 + 16 * r, 24 + 16 * r), 1.0, OP.add)
                cp(A("PO", 120 + 8 * r, 128 + 8 * r), A("S2", 24 + 16 * r, 32 + 16 * r))
        else:
            banks()
            for h in range(2):
                act(A("EA", 512 * h, 512 * h + 512), A(("P6", "P7")[h]), AF.Abs, bias=64.0)
            for h in range(2):
                act(A("EQ", 512 * h, 512 * h + 512), A("EA", 512 * h, 512 * h + 512), AF.Relu, bias=64.0 * 2048, scale=-2048.0)
        if first:
            wait("s", arr, N - 1)
            for d in (2, 6):
                zero(0, d)
                zero(1, d)
            zero(0, 5)
        if t == 1:
            fold([(0, 4), (1, 4), (0, 2), (0, 6)], start=True, first=[(ID, "SCM", 0)])
        tt(A("SI", 40, 48), A("P4", 72, 80), A("LN", 8, 16), OP.subtract)
        tt(A("QF"), A("P4", 72, 80), A("SI", 40, 48), OP.subtract)
        lin(cells, A("QF"), 32.0)
        if not last:
            cp(IND(A("IA"), cells), cur)
            cp(IND(A("XB"), cells), A("ZZ"))

    cp(IND(A("XB"), cells), A("ZZ"))
    dma("s", H(T.yx[:, :]), A("XB"))
    cp(IND(A("IA"), cells), cur)
    scan(A("TT", 0, 512), A("SCM", 0, 512), A("P0"), OP.mult, OP.add)
    for p in range(12):
        mm(A("P6", 0, 256), [(A("ZA", 15 - p, 143 - p), A("IA", 256 * p, 256 * p + 256))], p == 0, False)
    scan(A("TT", 512, 769), A("SCM", 512, 769), A("P1", 0, 257), OP.mult, OP.add, A("TT", 511, 512))
    tw = A("TT")
    tt(A("TM", 0, 384), IND(tw, A("PO", 48, 72)), A("MM", 0, 384), OP.mult)
    act(A("OE", 0, S0), IND(tw, A("PO", 0, 48)), bias=-1.0)
    tt(A("TM", 384, 768), IND(tw, A("PO", 120, 144)), A("MM", 384, 768), OP.mult)
    mm(A("P4", 0, 384), [(A("BOH", 0, 128), A("TM", 0, 384))])
    for p in range(12, 16):
        mm(A("P6", 0, 256), [(A("ZA", 15 - p, 143 - p), A("IA", 256 * p, 256 * p + 256))], False, p == 15)
    mm(A("P5", 0, 384), [(A("BOH", 128, 256), A("TM", 384, 768))])
    act(A("OH", 0, S0), IND(tw, A("PO", 72, 120)), bias=-1.0)
    ts(A("OE", S0, 1152), A("P4", 0, 384), -1.0, OP.add)
    dma("s", H(T.ye[:, :]), A("OE", p=(7, 128, 16)))
    cp(A("WN"), A("P6", 0, 256))
    dma("s", H(T.yw[:, :]), A("WN"))
    ts(A("OH", S0, 1152), A("P5", 0, 384), -1.0, OP.add)
    dma("a", H(T.yh[:, :]), A("OH", p=(15, 128, 16)))

    for sem in cnt:
        if cnt[sem]:
            wait("s" if sem[0] == "d" else "g", sem, cnt[sem])
